import numpy as np
import ml_dtypes


def mxq(x, axis, fmt="e4m3"):
    dtype, down = {"e4m3": (ml_dtypes.float8_e4m3fn, 7), "e5m2": (ml_dtypes.float8_e5m2, 14)}[fmt]
    v = np.moveaxis(np.asarray(x, np.float32).astype(ml_dtypes.bfloat16).astype(np.float64), axis, -1)
    blocks = v.reshape(v.shape[:-1] + (-1, 32))
    amax = np.abs(blocks).max(-1, keepdims=True)
    byte = np.maximum(np.where(amax > 0, np.frexp(amax)[1] - 1 + 127, 0) - down, 1)
    scale = np.exp2(byte - 127.0)
    codes = (blocks / scale).astype(np.float32).astype(dtype).astype(np.float64)
    return np.moveaxis((codes * scale).reshape(v.shape), -1, axis)


WIDE = False


def mx_kscale(k):
    if not WIDE:
        return np.ones(k)
    levels = np.array([18, -18])
    if k % 512:
        return np.exp2(np.random.permutation(np.resize(levels, k // 32))).repeat(32)
    a = np.empty((k // 512, 16))
    for p in range(k // 512):
        a[p, :8] = np.random.permutation(np.resize(levels, 8))
        for g in range(8):
            far = levels[np.abs(levels - a[p, g]) >= 10]
            a[p, g + 8] = far[np.random.randint(len(far))]
    return np.exp2(a.ravel()).repeat(32)


def f64(x):
    return np.asarray(x).astype(np.float64)


def striped(idx):
    return np.tile(np.asarray(idx).reshape(-1, 16).T, (8, 1)).astype(np.uint16)


def unstriped(offs):
    return offs[:16].T.reshape(-1).astype(np.int64)


B, N, T, D, DV = 2, 512, 2048, 512, 512


def setup_inputs():
    n = np.random.standard_normal
    idx = np.random.permutation(T)[:B * N]
    u = np.ones(T)
    u[idx] = mx_kscale(B * N)
    v = mx_kscale(DV)[:, None]
    coarse = lambda x: x.astype(np.float32).astype(ml_dtypes.bfloat16).astype(np.float64)
    r = np.random.randint(8, 33, T) / 16.0 * u
    return {
        "xT": (n((D, T)) / np.sqrt(N) / u).astype(np.float32),
        "dyT": (coarse(n((DV, T))) * v).astype(np.float32),
        "ts": np.tile(r, (128, 1)).astype(np.float32),
        "wm": (n((B, DV, D)) / np.sqrt(DV) / v).astype(np.float32),
        "offs": striped(idx),
    }


def reference(xT, dyT, ts, wm, offs):
    idx = unstriped(offs)
    pick = lambda x: x[:, idx].reshape(x.shape[0], B, N).transpose(1, 0, 2)
    dz = pick(f64(ts))[:, :1, :] * pick(f64(dyT))
    gw = mxq(pick(f64(xT)), 2, "e4m3") @ mxq(dz, 2, "e5m2").transpose(0, 2, 1)
    dx = mxq(f64(wm), 1, "e4m3").transpose(0, 2, 1) @ mxq(dz, 1, "e5m2")
    gx = np.zeros((D, T))
    gx[:, idx] = dx.transpose(1, 0, 2).reshape(D, B * N)
    return gw, gx

@@ -1,0 +1,265 @@
+from contextlib import ExitStack
+
+import concourse.mybir as mybir
+from concourse.masks import make_identity
+
+B, N, T, D, DV = 2, 512, 2048, 512, 512
+FLOPS = 2 * 2 * B * N * D * DV
+
+F32 = mybir.dt.float32
+BF16 = mybir.dt.bfloat16
+U32 = mybir.dt.uint32
+U16 = mybir.dt.uint16
+U8 = mybir.dt.uint8
+E4M3 = mybir.dt.float8_e4m3fn_x4
+E5M2 = mybir.dt.float8_e5m2_x4
+COPY = mybir.ActivationFunctionType.Copy
+MULT = mybir.AluOpType.mult
+
+P = 128
+PACK = 4
+BLOCKS = D // P
+HALF = D // 2
+LIST_COLS = N // 16
+SLOT_OF_PLACE = (0, 2, 1, 3)
+
+
+def tile_attend_gex_wx_kernel(tc, xT, dyT, ts, wm, offs, out_0, out_1):
+    nc = tc.nc
+
+    with ExitStack() as ctx:
+        keep = ctx.enter_context(tc.tile_pool(name="keep", bufs=1))
+        ring2 = ctx.enter_context(tc.tile_pool(name="ring2", bufs=2))
+        ring4 = ctx.enter_context(tc.tile_pool(name="ring4", bufs=4))
+        turn_banks = ctx.enter_context(tc.psum_pool(name="turn_banks", bufs=2))
+        dx_banks = ctx.enter_context(tc.psum_pool(name="dx_banks", bufs=2))
+        gw_banks = ctx.enter_context(tc.psum_pool(name="gw_banks", bufs=4))
+
+        offsets = keep.tile([P, B * LIST_COLS], U16, name="offsets")
+        ts_sb = keep.tile([P, T], F32, name="ts_sb", tag="reused_a")
+        dy_sb = [keep.tile([P, T], F32, name=f"dy{t}", tag=f"dy{t}", align_bytes=64) for t in range(PACK)]
+        x_sb = [keep.tile([P, T], F32, name=f"x{j}") for j in range(BLOCKS)]
+        wm_sb = {(b, h): keep.tile([P, PACK, HALF], F32, name=f"wm{b}{h}") for b in range(B) for h in range(2)}
+
+        dy_planes = dyT.rearrange("(p t) c -> t p c", t=PACK)
+
+        def load_wm(b, h):
+            nc.sync.dma_start(
+                out=wm_sb[b, h][:], in_=wm[b].rearrange("(p t) d -> p t d", t=PACK)[:, :, h * HALF : (h + 1) * HALF]
+            )
+
+        nc.sync.dma_start(out=ts_sb[:], in_=ts)
+        nc.sync.dma_start(offsets[:], offs)
+        for t in range(PACK):
+            nc.sync.dma_start(out=dy_sb[t][:], in_=dy_planes[t])
+            if t == 1:
+                load_wm(0, 0)
+        nc.sync.dma_start(out=x_sb[0][:], in_=xT[0:P, :])
+        load_wm(1, 0)
+        load_wm(0, 1)
+        load_wm(1, 1)
+        for j in range(1, BLOCKS):
+            nc.sync.dma_start(out=x_sb[j][:], in_=xT[j * P : (j + 1) * P, :])
+
+        def expert_offsets(b):
+            return offsets[:, b * LIST_COLS : (b + 1) * LIST_COLS]
+
+        ident = keep.tile([P, P], F32, name="ident")
+        make_identity(nc, ident[:])
+
+        windows = {}
+        for j in range(2):
+            windows[j] = keep.tile([P, T], F32, name=f"window{j}")
+            nc.vector.memset(windows[j][:], 0.0)
+
+        ts_g = keep.tile([P, B * N], F32, name="ts_g")
+        dz = keep.tile([P, PACK, B * N], F32, name="dz")
+        dzt_bf = [keep.tile([P, PACK, P, PACK], BF16, name=f"dzt_bf{b}", align_bytes=64) for b in range(B)]
+        dzn_bf = [keep.tile([P, N, PACK], BF16, name=f"dzn_bf{b}", tag=f"dzn_bf{b}", align_bytes=64) for b in range(B)]
+        wm_bf = {k: keep.tile([P, HALF, PACK], BF16, name=f"wm_bf{k[0]}{k[1]}", align_bytes=64) for k in wm_sb}
+
+        def quantize(name, src, width, fmt, tag=None):
+            codes = keep.tile([P, width], U32, name=name + "_codes", tag=tag or name, align_bytes=64)
+            scales = keep.tile([P, width], U8, name=name + "_scales", align_bytes=64)
+            nc.vector.quantize_mx(out=codes[:].bitcast(fmt), scales=scales[:], in_=src)
+            return codes, scales
+
+        def interleave(dst, src):
+            nc.scalar.copy(
+                out=dst.rearrange("p (c i) t -> p c t i", i=4), in_=src.rearrange("p t (c i) -> p c t i", i=4)
+            )
+
+        def turn_dz(t, b):
+            bank = turn_banks.tile([P, PACK, P], F32, name="turn_bank")
+            for place, r in enumerate(SLOT_OF_PLACE):
+                nc.tensor.transpose(bank[:, place, :], dz[:, t, b * N + r : (b + 1) * N : PACK], ident[:])
+            nc.scalar.activation(dzt_bf[b][:, t], bank[:].rearrange("s k p -> s p k"), COPY)
+
+        def interleave_dz(b, h):
+            lo, hi = h * (N // 2), (h + 1) * (N // 2)
+            interleave(dzn_bf[b][:, lo:hi, :], dz[:, :, b * N + lo : b * N + hi])
+
+        def interleave_wm(b, h):
+            interleave(wm_bf[b, h][:], wm_sb[b, h][:])
+
+        wm_q, dzn_q, dzt_q, x_q, dx_sb, x_g, xt_bf, x_bf = {}, {}, {}, {}, {}, {}, {}, {}
+
+        def quantize_wm(b, h):
+            wm_q[b, h] = quantize(f"wm_q{b}{h}", wm_bf[b, h][:].rearrange("p d t -> p (d t)"), HALF, E4M3, "dy3" if (b, h) == (0, 0) else None)
+
+        def quantize_dzn(b):
+            dzn_q[b] = quantize(f"dzn_q{b}", dzn_bf[b][:].rearrange("p i t -> p (i t)"), N, E5M2)
+
+        def quantize_dzt(b):
+            dzt_q[b] = quantize(f"dzt_q{b}", dzt_bf[b][:].rearrange("s t p k -> s (t p k)"), DV, E5M2)
+
+        def multiply_dx(j, b):
+            codes, scales = wm_q[b, j // 2]
+            cols = slice((j % 2) * P, (j % 2 + 1) * P)
+            bank = dx_banks.tile([P, N], F32, name="dx_bank")
+            nc.tensor.matmul_mx(
+                out=bank[:],
+                lhsT=codes[:, cols].bitcast(E4M3),
+                lhsT_scale=scales[:, cols],
+                rhs=dzn_q[b][0][:].bitcast(E5M2),
+                rhs_scale=dzn_q[b][1][:],
+                start=True,
+                stop=True,
+            )
+            dx_sb[j, b] = keep.tile([P, N], F32, name=f"dx_sb{j}{b}")
+            nc.scalar.copy(out=dx_sb[j, b][:], in_=bank[:])
+
+        def scatter(j, b):
+            nc.vector.tensor_copy(windows[j][:].indirect(expert_offsets(b)), dx_sb[j, b][:])
+            if b == B - 1:
+                nc.sync.dma_start(out=out_1[j * P : (j + 1) * P, :], in_=windows[j][:])
+
+        def cast_x(j):
+            x_bf[j] = ring2.tile([P, T], BF16, name="x_bf")
+            nc.scalar.activation(x_bf[j][:], x_sb[j][:], COPY)
+
+        def gather_x(j, b):
+            if j == 0:
+                tag = "dzn_bf0" if b == 1 else "x_g00"
+                x_g[j, b] = keep.tile([P, 2, N // 2], BF16, name=f"x_g{j}{b}", tag=tag, align_bytes=64)
+                nc.vector.tensor_copy(x_g[j, b][:].rearrange("p u c -> p c u"), x_sb[j][:].indirect(expert_offsets(b)))
+            else:
+                x_g[j, b] = ring4.tile([P, 2, N // 2], BF16, name="x_g")
+                nc.scalar.activation(
+                    x_g[j, b][:].rearrange("p u c -> p c u"), x_bf[j][:].indirect(expert_offsets(b)), COPY
+                )
+
+        def turn_x(j):
+            bank = turn_banks.tile([P, B, 2, P], F32, name="turn_bank")
+            for b in range(B):
+                for u in range(2):
+                    nc.tensor.transpose(bank[:, b, u, :], x_g[j, b][:, u, :].bitcast(F32), ident[:])
+            xt_bf[j] = ring2.tile([P, B * P * PACK], BF16, name="xt_bf", align_bytes=64)
+            nc.scalar.copy(
+                out=xt_bf[j][:].bitcast(F32).rearrange("s (b d u) -> s b d u", b=B, u=2),
+                in_=bank[:].rearrange("s b u d -> s b d u"),
+            )
+
+        def quantize_x(j):
+            x_q[j] = quantize(f"x_q{j}", xt_bf[j][:], B * P, E4M3)
+
+        def multiply_gw(j, b, on_vector=0):
+            codes, scales = x_q[j]
+            cols = slice(b * P, (b + 1) * P)
+            bank = gw_banks.tile([P, DV], F32, name="gw_bank")
+            nc.tensor.matmul_mx(
+                out=bank[:],
+                lhsT=codes[:, cols].bitcast(E4M3),
+                lhsT_scale=scales[:, cols],
+                rhs=dzt_q[b][0][:].bitcast(E5M2),
+                rhs_scale=dzt_q[b][1][:],
+                start=True,
+                stop=True,
+            )
+            gw_sb = keep.tile([P, P, PACK], F32, name=f"gw_sb{j}{b}")
+            copy = nc.vector.tensor_copy if on_vector else nc.scalar.copy
+            copy(out=gw_sb[:], in_=bank[:].rearrange("d (t p) -> d p t", t=PACK))
+            nc.scalar.dma_start(out=out_0[b, j * P : (j + 1) * P, :], in_=gw_sb[:].rearrange("d p t -> d (p t)"))
+
+        nc.vector.tensor_copy(ts_g[:], ts_sb[:].indirect(offsets[:]))
+        windows[2] = keep.tile([P, T], F32, name="window2", tag="reused_a")
+        nc.gpsimd.memset(windows[2][:], 0.0)
+
+        def gather_dz(t, b):
+            cols = slice(b * N, (b + 1) * N)
+            nc.vector.tensor_tensor(dz[:, t, cols], dy_sb[t][:].indirect(expert_offsets(b)), ts_g[:, cols], MULT)
+
+        for t in range(2):
+            nc.vector.tensor_tensor(dz[:, t, :], dy_sb[t][:].indirect(offsets[:]), ts_g[:], MULT)
+            if t == 0:
+                windows[3] = keep.tile([P, T], F32, name="window3", tag="dy0", align_bytes=64)
+                nc.gpsimd.memset(windows[3][:], 0.0)
+            if t == 1:
+                interleave_wm(0, 0)
+            for b in range(B):
+                turn_dz(t, b)
+        for b in range(B):
+            gather_dz(2, b)
+            turn_dz(2, b)
+        for b in range(B):
+            gather_dz(3, b)
+        quantize_wm(0, 0)
+        interleave_dz(0, 0)
+        interleave_dz(0, 1)
+        interleave_wm(0, 1)
+        quantize_dzn(0)
+        cast_x(1)
+        quantize_wm(0, 1)
+        turn_dz(3, 0)
+        turn_dz(3, 1)
+        multiply_dx(1, 0)
+        interleave_wm(1, 1)
+        gather_x(0, 1)
+        quantize_dzt(0)
+        gather_x(1, 0)
+        multiply_dx(0, 0)
+        interleave_wm(1, 0)
+        multiply_dx(2, 0)
+        gather_x(0, 0)
+        quantize_wm(1, 1)
+        quantize_wm(1, 0)
+        gather_x(1, 1)
+        interleave_dz(1, 1)
+        quantize_dzt(1)
+        interleave_dz(1, 0)
+        quantize_dzn(1)
+        multiply_dx(3, 0)
+        scatter(0, 0)
+        multiply_dx(0, 1)
+        turn_x(0)
+        multiply_dx(1, 1)
+        cast_x(3)
+        gather_x(3, 1)
+        turn_x(1)
+        scatter(2, 0)
+        cast_x(2)
+        quantize_x(1)
+        quantize_x(0)
+        gather_x(2, 1)
+        multiply_gw(0, 1)
+        scatter(3, 0)
+        multiply_dx(2, 1)
+        scatter(0, 1)
+        multiply_gw(0, 0)
+        scatter(1, 0)
+        gather_x(2, 0)
+        turn_x(2)
+        gather_x(3, 0)
+        multiply_gw(1, 0)
+        quantize_x(2)
+        multiply_gw(2, 1)
+        turn_x(3)
+        scatter(2, 1)
+        multiply_dx(3, 1)
+        quantize_x(3)
+        scatter(3, 1)
+        multiply_gw(2, 0)
+        scatter(1, 1)
+        multiply_gw(3, 1)
+        multiply_gw(1, 1, on_vector=1)
+        multiply_gw(3, 0)

@@ -9,6 +9,7 @@ FLOPS = 2 * 2 * B * N * D * DV
 F32 = mybir.dt.float32
 BF16 = mybir.dt.bfloat16
 U32 = mybir.dt.uint32
+I32 = mybir.dt.int32
 U16 = mybir.dt.uint16
 U8 = mybir.dt.uint8
 E4M3 = mybir.dt.float8_e4m3fn_x4
@@ -22,6 +23,7 @@ BLOCKS = D // P
 HALF = D // 2
 LIST_COLS = N // 16
 SLOT_OF_PLACE = (0, 2, 1, 3)
+DX_BANK = {(0, 0): "p", (0, 1): "p", (1, 0): "q", (1, 1): "r", (2, 0): "p", (2, 1): "r", (3, 0): "p", (3, 1): "r"}
 
 
 def tile_attend_gex_wx_kernel(tc, xT, dyT, ts, wm, offs, out_0, out_1):
@@ -29,17 +31,20 @@ def tile_attend_gex_wx_kernel(tc, xT, dyT, ts, wm, offs, out_0, out_1):
 
     with ExitStack() as ctx:
         keep = ctx.enter_context(tc.tile_pool(name="keep", bufs=1))
-        ring2 = ctx.enter_context(tc.tile_pool(name="ring2", bufs=2))
-        ring4 = ctx.enter_context(tc.tile_pool(name="ring4", bufs=4))
-        turn_banks = ctx.enter_context(tc.psum_pool(name="turn_banks", bufs=2))
-        dx_banks = ctx.enter_context(tc.psum_pool(name="dx_banks", bufs=2))
-        gw_banks = ctx.enter_context(tc.psum_pool(name="gw_banks", bufs=4))
+        turn_banks = ctx.enter_context(tc.psum_pool(name="turn_banks", bufs=3))
+        dx_banks = ctx.enter_context(tc.psum_pool(name="dx_banks", bufs=1))
+
+        slot_of = {}
+
+        def held(name, shape, dtype, after=None):
+            slot_of[name] = slot_of[after] if after else name
+            return keep.tile(shape, dtype, name=name, tag=slot_of[name], align_bytes=64)
 
         offsets = keep.tile([P, B * LIST_COLS], U16, name="offsets")
-        ts_sb = keep.tile([P, T], F32, name="ts_sb", tag="reused_a")
-        dy_sb = [keep.tile([P, T], F32, name=f"dy{t}", tag=f"dy{t}", align_bytes=64) for t in range(PACK)]
-        x_sb = [keep.tile([P, T], F32, name=f"x{j}") for j in range(BLOCKS)]
-        wm_sb = {(b, h): keep.tile([P, PACK, HALF], F32, name=f"wm{b}{h}") for b in range(B) for h in range(2)}
+        ts_sb = held("ts_sb", [P, T], F32)
+        dy_sb = [held(f"dy{t}", [P, T], F32) for t in range(PACK)]
+        x_sb = {}
+        wm_sb = {(b, h): held(f"wm{b}{h}", [P, PACK, HALF], F32) for b in range(B) for h in range(2)}
 
         dy_planes = dyT.rearrange("(p t) c -> t p c", t=PACK)
 
@@ -52,13 +57,9 @@ def tile_attend_gex_wx_kernel(tc, xT, dyT, ts, wm, offs, out_0, out_1):
         nc.sync.dma_start(offsets[:], offs)
         for t in range(PACK):
             nc.sync.dma_start(out=dy_sb[t][:], in_=dy_planes[t])
-            if t == 1:
-                load_wm(0, 0)
-        nc.sync.dma_start(out=x_sb[0][:], in_=xT[0:P, :])
-        load_wm(1, 0)
-        load_wm(0, 1)
-        load_wm(1, 1)
-        for j in range(1, BLOCKS):
+
+        def load_x(j):
+            x_sb[j] = held(f"x{j}", [P, T], F32, {2: "dy1", 3: "ts_sb"}.get(j))
             nc.sync.dma_start(out=x_sb[j][:], in_=xT[j * P : (j + 1) * P, :])
 
         def expert_offsets(b):
@@ -70,24 +71,22 @@ def tile_attend_gex_wx_kernel(tc, xT, dyT, ts, wm, offs, out_0, out_1):
         windows = {}
         for j in range(2):
             windows[j] = keep.tile([P, T], F32, name=f"window{j}")
-            nc.vector.memset(windows[j][:], 0.0)
+            nc.vector.memset(windows[j][:].bitcast(I32), 0)
 
-        ts_g = keep.tile([P, B * N], F32, name="ts_g")
-        dz = keep.tile([P, PACK, B * N], F32, name="dz")
-        dzt_bf = [keep.tile([P, PACK, P, PACK], BF16, name=f"dzt_bf{b}", align_bytes=64) for b in range(B)]
-        dzn_bf = [keep.tile([P, N, PACK], BF16, name=f"dzn_bf{b}", tag=f"dzn_bf{b}", align_bytes=64) for b in range(B)]
-        wm_bf = {k: keep.tile([P, HALF, PACK], BF16, name=f"wm_bf{k[0]}{k[1]}", align_bytes=64) for k in wm_sb}
+        ts_g = held("ts_g", [P, B * N], F32)
+        dz = held("dz", [P, PACK, B * N], F32)
+        dzt_bf = [held(f"dzt_bf{b}", [P, PACK, P, PACK], BF16) for b in range(B)]
+        dzn_bf, wm_bf = {}, {}
 
-        def quantize(name, src, width, fmt, tag=None):
-            codes = keep.tile([P, width], U32, name=name + "_codes", tag=tag or name, align_bytes=64)
+        def quantize(name, src, width, fmt, after=None):
+            codes = held(name + "_codes", [P, width], U32, after)
             scales = keep.tile([P, width], U8, name=name + "_scales", align_bytes=64)
             nc.vector.quantize_mx(out=codes[:].bitcast(fmt), scales=scales[:], in_=src)
             return codes, scales
 
-        def interleave(dst, src):
-            nc.scalar.copy(
-                out=dst.rearrange("p (c i) t -> p c t i", i=4), in_=src.rearrange("p t (c i) -> p c t i", i=4)
-            )
+        def interleave(dst, src, on_vector):
+            copy = nc.vector.tensor_copy if on_vector else nc.scalar.copy
+            copy(out=dst.rearrange("p (c i) t -> p c t i", i=4), in_=src.rearrange("p t (c i) -> p c t i", i=4))
 
         def turn_dz(t, b):
             bank = turn_banks.tile([P, PACK, P], F32, name="turn_bank")
@@ -95,28 +94,32 @@ def tile_attend_gex_wx_kernel(tc, xT, dyT, ts, wm, offs, out_0, out_1):
                 nc.tensor.transpose(bank[:, place, :], dz[:, t, b * N + r : (b + 1) * N : PACK], ident[:])
             nc.scalar.activation(dzt_bf[b][:, t], bank[:].rearrange("s k p -> s p k"), COPY)
 
-        def interleave_dz(b, h):
+        def interleave_dz(b, h, after=None, on_vector=0):
             lo, hi = h * (N // 2), (h + 1) * (N // 2)
-            interleave(dzn_bf[b][:, lo:hi, :], dz[:, :, b * N + lo : b * N + hi])
+            if h == 0:
+                dzn_bf[b] = held(f"dzn_bf{b}", [P, N, PACK], BF16, after)
+            interleave(dzn_bf[b][:, lo:hi, :], dz[:, :, b * N + lo : b * N + hi], on_vector)
 
-        def interleave_wm(b, h):
-            interleave(wm_bf[b, h][:], wm_sb[b, h][:])
+        def interleave_wm(b, h, after=None, on_vector=0):
+            wm_bf[b, h] = held(f"wm_bf{b}{h}", [P, HALF, PACK], BF16, after)
+            interleave(wm_bf[b, h][:], wm_sb[b, h][:], on_vector)
 
-        wm_q, dzn_q, dzt_q, x_q, dx_sb, x_g, xt_bf, x_bf = {}, {}, {}, {}, {}, {}, {}, {}
 
-        def quantize_wm(b, h):
-            wm_q[b, h] = quantize(f"wm_q{b}{h}", wm_bf[b, h][:].rearrange("p d t -> p (d t)"), HALF, E4M3, "dy3" if (b, h) == (0, 0) else None)
+        wm_q, dzn_q, dzt_q, x_q, dx_sb, x_g, xt_bf, x_bf, x_bank = {}, {}, {}, {}, {}, {}, {}, {}, {}
 
-        def quantize_dzn(b):
-            dzn_q[b] = quantize(f"dzn_q{b}", dzn_bf[b][:].rearrange("p i t -> p (i t)"), N, E5M2)
+        def quantize_wm(b, h, after=None):
+            wm_q[b, h] = quantize(f"wm_q{b}{h}", wm_bf[b, h][:].rearrange("p d t -> p (d t)"), HALF, E4M3, after)
 
-        def quantize_dzt(b):
-            dzt_q[b] = quantize(f"dzt_q{b}", dzt_bf[b][:].rearrange("s t p k -> s (t p k)"), DV, E5M2)
+        def quantize_dzn(b, after=None):
+            dzn_q[b] = quantize(f"dzn_q{b}", dzn_bf[b][:].rearrange("p i t -> p (i t)"), N, E5M2, after)
 
-        def multiply_dx(j, b):
+        def quantize_dzt(b, after=None):
+            dzt_q[b] = quantize(f"dzt_q{b}", dzt_bf[b][:].rearrange("s t p k -> s (t p k)"), DV, E5M2, after)
+
+        def multiply_dx(j, b, on_vector=0, after=None):
             codes, scales = wm_q[b, j // 2]
             cols = slice((j % 2) * P, (j % 2 + 1) * P)
-            bank = dx_banks.tile([P, N], F32, name="dx_bank")
+            bank = dx_banks.tile([P, N], F32, name=f"dx_bank{j}{b}", tag=DX_BANK[j, b])
             nc.tensor.matmul_mx(
                 out=bank[:],
                 lhsT=codes[:, cols].bitcast(E4M3),
@@ -126,47 +129,48 @@ def tile_attend_gex_wx_kernel(tc, xT, dyT, ts, wm, offs, out_0, out_1):
                 start=True,
                 stop=True,
             )
-            dx_sb[j, b] = keep.tile([P, N], F32, name=f"dx_sb{j}{b}")
-            nc.scalar.copy(out=dx_sb[j, b][:], in_=bank[:])
+            dx_sb[j, b] = held(f"dx_sb{j}{b}", [P, N], F32, after)
+            copy = nc.vector.tensor_copy if on_vector else nc.scalar.copy
+            copy(out=dx_sb[j, b][:], in_=bank[:])
 
         def scatter(j, b):
-            nc.vector.tensor_copy(windows[j][:].indirect(expert_offsets(b)), dx_sb[j, b][:])
+            nc.vector.tensor_copy(windows[j % 2][:].indirect(expert_offsets(b)), dx_sb[j, b][:])
             if b == B - 1:
-                nc.sync.dma_start(out=out_1[j * P : (j + 1) * P, :], in_=windows[j][:])
+                nc.sync.dma_start(out=out_1[j * P : (j + 1) * P, :], in_=windows[j % 2][:])
 
-        def cast_x(j):
-            x_bf[j] = ring2.tile([P, T], BF16, name="x_bf")
-            nc.scalar.activation(x_bf[j][:], x_sb[j][:], COPY)
-
-        def gather_x(j, b):
-            if j == 0:
-                tag = "dzn_bf0" if b == 1 else "x_g00"
-                x_g[j, b] = keep.tile([P, 2, N // 2], BF16, name=f"x_g{j}{b}", tag=tag, align_bytes=64)
-                nc.vector.tensor_copy(x_g[j, b][:].rearrange("p u c -> p c u"), x_sb[j][:].indirect(expert_offsets(b)))
+        def cast_x(j, after=None, on_vector=0):
+            x_bf[j] = held(f"x_bf{j}", [P, T], BF16, after)
+            if on_vector:
+                nc.vector.tensor_copy(x_bf[j][:], x_sb[j][:])
             else:
-                x_g[j, b] = ring4.tile([P, 2, N // 2], BF16, name="x_g")
-                nc.scalar.activation(
-                    x_g[j, b][:].rearrange("p u c -> p c u"), x_bf[j][:].indirect(expert_offsets(b)), COPY
-                )
+                nc.scalar.activation(x_bf[j][:], x_sb[j][:], COPY)
 
-        def turn_x(j):
-            bank = turn_banks.tile([P, B, 2, P], F32, name="turn_bank")
-            for b in range(B):
-                for u in range(2):
-                    nc.tensor.transpose(bank[:, b, u, :], x_g[j, b][:, u, :].bitcast(F32), ident[:])
-            xt_bf[j] = ring2.tile([P, B * P * PACK], BF16, name="xt_bf", align_bytes=64)
+        def gather_x(j, b, after=None):
+            x_g[j, b] = held(f"x_g{j}{b}", [P, 2, N // 2], BF16, after)
+            parted = x_g[j, b][:].rearrange("p u c -> p c u")
+            if j in x_bf:
+                nc.scalar.activation(parted, x_bf[j][:].indirect(expert_offsets(b)), COPY)
+            else:
+                nc.vector.tensor_copy(parted, x_sb[j][:].indirect(expert_offsets(b)))
+            if j not in x_bank:
+                x_bank[j] = turn_banks.tile([P, B, 2, P], F32, name="turn_bank")
+            for u in range(2):
+                nc.tensor.transpose(x_bank[j][:, b, u, :], x_g[j, b][:, u, :].bitcast(F32), ident[:])
+
+        def turn_x(j, after=None):
+            xt_bf[j] = held(f"xt_bf{j}", [P, B * P * PACK], BF16, after)
             nc.scalar.copy(
                 out=xt_bf[j][:].bitcast(F32).rearrange("s (b d u) -> s b d u", b=B, u=2),
-                in_=bank[:].rearrange("s b u d -> s b d u"),
+                in_=x_bank[j][:].rearrange("s b u d -> s b d u"),
             )
 
-        def quantize_x(j):
-            x_q[j] = quantize(f"x_q{j}", xt_bf[j][:], B * P, E4M3)
+        def quantize_x(j, after=None):
+            x_q[j] = quantize(f"x_q{j}", xt_bf[j][:], B * P, E4M3, after)
 
-        def multiply_gw(j, b, on_vector=0):
+        def multiply_gw(j, b, on_vector=0, after=None, own_queue=0):
             codes, scales = x_q[j]
             cols = slice(b * P, (b + 1) * P)
-            bank = gw_banks.tile([P, DV], F32, name="gw_bank")
+            bank = dx_banks.tile([P, DV], F32, name=f"gw_bank{j}{b}", tag="pq"[b])
             nc.tensor.matmul_mx(
                 out=bank[:],
                 lhsT=codes[:, cols].bitcast(E4M3),
@@ -176,14 +180,13 @@ def tile_attend_gex_wx_kernel(tc, xT, dyT, ts, wm, offs, out_0, out_1):
                 start=True,
                 stop=True,
             )
-            gw_sb = keep.tile([P, P, PACK], F32, name=f"gw_sb{j}{b}")
+            gw_sb = held(f"gw_sb{j}{b}", [P, P, PACK], F32, after)
             copy = nc.vector.tensor_copy if on_vector else nc.scalar.copy
             copy(out=gw_sb[:], in_=bank[:].rearrange("d (t p) -> d p t", t=PACK))
-            nc.scalar.dma_start(out=out_0[b, j * P : (j + 1) * P, :], in_=gw_sb[:].rearrange("d p t -> d (p t)"))
+            queue = nc.scalar if own_queue else nc.sync
+            queue.dma_start(out=out_0[b, j * P : (j + 1) * P, :], in_=gw_sb[:].rearrange("d p t -> d (p t)"))
 
         nc.vector.tensor_copy(ts_g[:], ts_sb[:].indirect(offsets[:]))
-        windows[2] = keep.tile([P, T], F32, name="window2", tag="reused_a")
-        nc.gpsimd.memset(windows[2][:], 0.0)
 
         def gather_dz(t, b):
             cols = slice(b * N, (b + 1) * N)
@@ -191,75 +194,80 @@ def tile_attend_gex_wx_kernel(tc, xT, dyT, ts, wm, offs, out_0, out_1):
 
         for t in range(2):
             nc.vector.tensor_tensor(dz[:, t, :], dy_sb[t][:].indirect(offsets[:]), ts_g[:], MULT)
-            if t == 0:
-                windows[3] = keep.tile([P, T], F32, name="window3", tag="dy0", align_bytes=64)
-                nc.gpsimd.memset(windows[3][:], 0.0)
-            if t == 1:
-                interleave_wm(0, 0)
             for b in range(B):
                 turn_dz(t, b)
         for b in range(B):
             gather_dz(2, b)
-            turn_dz(2, b)
+        turn_dz(2, 0)
         for b in range(B):
             gather_dz(3, b)
-        quantize_wm(0, 0)
-        interleave_dz(0, 0)
+        load_wm(0, 0)
+        load_wm(1, 0)
+        load_x(0)
+        load_wm(0, 1)
+        load_wm(1, 1)
+        load_x(1)
+        load_x(2)
+        load_x(3)
+        interleave_dz(0, 0, on_vector=1)
         interleave_dz(0, 1)
-        interleave_wm(0, 1)
+        interleave_wm(0, 0)
+        interleave_dz(1, 0, on_vector=1)
         quantize_dzn(0)
-        cast_x(1)
-        quantize_wm(0, 1)
+        interleave_dz(1, 1, on_vector=1)
+        quantize_wm(0, 0)
         turn_dz(3, 0)
-        turn_dz(3, 1)
-        multiply_dx(1, 0)
-        interleave_wm(1, 1)
-        gather_x(0, 1)
-        quantize_dzt(0)
-        gather_x(1, 0)
-        multiply_dx(0, 0)
-        interleave_wm(1, 0)
-        multiply_dx(2, 0)
-        gather_x(0, 0)
-        quantize_wm(1, 1)
-        quantize_wm(1, 0)
-        gather_x(1, 1)
-        interleave_dz(1, 1)
-        quantize_dzt(1)
-        interleave_dz(1, 0)
+        gather_x(0, 0, after="dzn_bf0")
         quantize_dzn(1)
-        multiply_dx(3, 0)
+        gather_x(0, 1, after="wm_bf00")
+        turn_dz(3, 1)
+        interleave_wm(1, 0)
+        multiply_dx(0, 0)
+        turn_dz(2, 1)
+        quantize_dzt(0)
+        quantize_wm(1, 0)
         scatter(0, 0)
-        multiply_dx(0, 1)
+        interleave_wm(0, 1, after="wm10")
+        quantize_dzt(1)
+        interleave_wm(1, 1, after="wm01")
         turn_x(0)
-        multiply_dx(1, 1)
-        cast_x(3)
-        gather_x(3, 1)
-        turn_x(1)
-        scatter(2, 0)
-        cast_x(2)
-        quantize_x(1)
         quantize_x(0)
-        gather_x(2, 1)
-        multiply_gw(0, 1)
-        scatter(3, 0)
-        multiply_dx(2, 1)
-        scatter(0, 1)
-        multiply_gw(0, 0)
+        multiply_dx(1, 0, after="x_g01")
         scatter(1, 0)
-        gather_x(2, 0)
-        turn_x(2)
-        gather_x(3, 0)
-        multiply_gw(1, 0)
-        quantize_x(2)
-        multiply_gw(2, 1)
-        turn_x(3)
-        scatter(2, 1)
-        multiply_dx(3, 1)
-        quantize_x(3)
-        scatter(3, 1)
-        multiply_gw(2, 0)
+        multiply_dx(0, 1, after="wm11")
+        scatter(0, 1)
+        cast_x(1, after="x_g00")
+        gather_x(1, 0)
+        gather_x(1, 1)
+        multiply_gw(0, 0, after="x1")
+        multiply_gw(0, 1, after="x_g10")
+        turn_x(1)
+        quantize_wm(0, 1, after="dx_sb01")
+        quantize_wm(1, 1, after="dx_sb10")
+        quantize_x(1)
+        multiply_dx(1, 1, after="x_g11")
         scatter(1, 1)
-        multiply_gw(3, 1)
-        multiply_gw(1, 1, on_vector=1)
-        multiply_gw(3, 0)
+        cast_x(2, after="x_bf1")
+        multiply_dx(2, 0)
+        scatter(2, 0)
+        gather_x(2, 0)
+        gather_x(2, 1)
+        multiply_gw(1, 0, after="x2")
+        multiply_gw(1, 1, after="x_g20")
+        turn_x(2)
+        quantize_x(2)
+        multiply_dx(2, 1, after="x_g21")
+        scatter(2, 1)
+        cast_x(3, after="x_bf2")
+        multiply_dx(3, 0)
+        scatter(3, 0)
+        gather_x(3, 0)
+        gather_x(3, 1)
+        multiply_gw(2, 0, after="x3")
+        multiply_gw(2, 1, after="x_g30")
+        turn_x(3)
+        quantize_x(3)
+        multiply_dx(3, 1, after="x_g31")
+        scatter(3, 1)
+        multiply_gw(3, 0, own_queue=1)
+        multiply_gw(3, 1, own_queue=1)

@@ -16,14 +16,20 @@ E4M3 = mybir.dt.float8_e4m3fn_x4
 E5M2 = mybir.dt.float8_e5m2_x4
 COPY = mybir.ActivationFunctionType.Copy
 MULT = mybir.AluOpType.mult
+ADD = mybir.AluOpType.add
 
 P = 128
 PACK = 4
 BLOCKS = D // P
-HALF = D // 2
+HALF_D = D // 2
+HALF_N = N // 2
 LIST_COLS = N // 16
+LINE = 4
+WINDOWS = 2
+TURN_BANKS = 3
 SLOT_OF_PLACE = (0, 2, 1, 3)
 DX_BANK = {(0, 0): "p", (0, 1): "p", (1, 0): "q", (1, 1): "r", (2, 0): "p", (2, 1): "r", (3, 0): "p", (3, 1): "r"}
+GW_BANK = ("p", "q")
 
 
 def tile_attend_gex_wx_kernel(tc, xT, dyT, ts, wm, offs, out_0, out_1):
@@ -31,62 +37,63 @@ def tile_attend_gex_wx_kernel(tc, xT, dyT, ts, wm, offs, out_0, out_1):
 
     with ExitStack() as ctx:
         keep = ctx.enter_context(tc.tile_pool(name="keep", bufs=1))
-        turn_banks = ctx.enter_context(tc.psum_pool(name="turn_banks", bufs=3))
-        dx_banks = ctx.enter_context(tc.psum_pool(name="dx_banks", bufs=1))
+        turn_banks = ctx.enter_context(tc.psum_pool(name="turn_banks", bufs=TURN_BANKS))
+        product_banks = ctx.enter_context(tc.psum_pool(name="product_banks", bufs=1))
 
-        slot_of = {}
+        tag_of = {}
 
-        def held(name, shape, dtype, after=None):
-            slot_of[name] = slot_of[after] if after else name
-            return keep.tile(shape, dtype, name=name, tag=slot_of[name], align_bytes=64)
+        def held(name, shape, dtype, reuses=None):
+            tag_of[name] = tag_of[reuses] if reuses else name
+            return keep.tile(shape, dtype, name=name, tag=tag_of[name], align_bytes=64)
 
         offsets = keep.tile([P, B * LIST_COLS], U16, name="offsets")
         ts_sb = held("ts_sb", [P, T], F32)
         dy_sb = [held(f"dy{t}", [P, T], F32) for t in range(PACK)]
-        x_sb = {}
-        wm_sb = {(b, h): held(f"wm{b}{h}", [P, PACK, HALF], F32) for b in range(B) for h in range(2)}
+        wm_sb = {(b, h): held(f"wm{b}{h}", [P, PACK, HALF_D], F32) for b in range(B) for h in range(2)}
 
         dy_planes = dyT.rearrange("(p t) c -> t p c", t=PACK)
-
-        def load_wm(b, h):
-            nc.sync.dma_start(
-                out=wm_sb[b, h][:], in_=wm[b].rearrange("(p t) d -> p t d", t=PACK)[:, :, h * HALF : (h + 1) * HALF]
-            )
-
         nc.sync.dma_start(out=ts_sb[:], in_=ts)
         nc.sync.dma_start(offsets[:], offs)
         for t in range(PACK):
             nc.sync.dma_start(out=dy_sb[t][:], in_=dy_planes[t])
 
-        def load_x(j):
-            x_sb[j] = held(f"x{j}", [P, T], F32, {2: "dy1", 3: "ts_sb"}.get(j))
-            nc.sync.dma_start(out=x_sb[j][:], in_=xT[j * P : (j + 1) * P, :])
-
-        def expert_offsets(b):
-            return offsets[:, b * LIST_COLS : (b + 1) * LIST_COLS]
-
         ident = keep.tile([P, P], F32, name="ident")
         make_identity(nc, ident[:])
 
-        windows = {}
-        for j in range(2):
-            windows[j] = keep.tile([P, T], F32, name=f"window{j}")
-            nc.vector.memset(windows[j][:].bitcast(I32), 0)
+        windows = []
+        for w in range(WINDOWS):
+            windows.append(keep.tile([P, T], F32, name=f"window{w}"))
+            nc.vector.memset(windows[w][:].bitcast(I32), 0)
 
         ts_g = held("ts_g", [P, B * N], F32)
         dz = held("dz", [P, PACK, B * N], F32)
         dzt_bf = [held(f"dzt_bf{b}", [P, PACK, P, PACK], BF16) for b in range(B)]
-        dzn_bf, wm_bf = {}, {}
+        x_sb, x_bf, x_g, x_bank, xt_bf, x_q = {}, {}, {}, {}, {}, {}
+        dzn_bf, dzn_q, dzt_q, wm_bf, wm_q, dx_sb = {}, {}, {}, {}, {}, {}
 
-        def quantize(name, src, width, fmt, after=None):
-            codes = held(name + "_codes", [P, width], U32, after)
+        def expert_offsets(b):
+            return offsets[:, b * LIST_COLS : (b + 1) * LIST_COLS]
+
+        def load_wm(b, h):
+            rows = wm[b].rearrange("(p t) d -> p t d", t=PACK)
+            nc.sync.dma_start(out=wm_sb[b, h][:], in_=rows[:, :, h * HALF_D : (h + 1) * HALF_D])
+
+        def load_x(j, reuses=None):
+            x_sb[j] = held(f"x{j}", [P, T], F32, reuses)
+            nc.sync.dma_start(out=x_sb[j][:], in_=xT[j * P : (j + 1) * P, :])
+
+        def quantize(name, src, width, fmt, reuses=None):
+            codes = held(name + "_codes", [P, width], U32, reuses)
             scales = keep.tile([P, width], U8, name=name + "_scales", align_bytes=64)
             nc.vector.quantize_mx(out=codes[:].bitcast(fmt), scales=scales[:], in_=src)
             return codes, scales
 
-        def interleave(dst, src, on_vector):
-            copy = nc.vector.tensor_copy if on_vector else nc.scalar.copy
-            copy(out=dst.rearrange("p (c i) t -> p c t i", i=4), in_=src.rearrange("p t (c i) -> p c t i", i=4))
+        def interleave(copy, dst, src):
+            copy(out=dst.rearrange("p (c i) t -> p c t i", i=LINE), in_=src.rearrange("p t (c i) -> p c t i", i=LINE))
+
+        def gather_dz(t, b):
+            cols = slice(b * N, (b + 1) * N)
+            nc.vector.tensor_tensor(dz[:, t, cols], dy_sb[t][:].indirect(expert_offsets(b)), ts_g[:, cols], MULT)
 
         def turn_dz(t, b):
             bank = turn_banks.tile([P, PACK, P], F32, name="turn_bank")
@@ -94,104 +101,85 @@ def tile_attend_gex_wx_kernel(tc, xT, dyT, ts, wm, offs, out_0, out_1):
                 nc.tensor.transpose(bank[:, place, :], dz[:, t, b * N + r : (b + 1) * N : PACK], ident[:])
             nc.scalar.activation(dzt_bf[b][:, t], bank[:].rearrange("s k p -> s p k"), COPY)
 
-        def interleave_dz(b, h, after=None, on_vector=0):
-            lo, hi = h * (N // 2), (h + 1) * (N // 2)
+        def interleave_dz(b, h, copy):
             if h == 0:
-                dzn_bf[b] = held(f"dzn_bf{b}", [P, N, PACK], BF16, after)
-            interleave(dzn_bf[b][:, lo:hi, :], dz[:, :, b * N + lo : b * N + hi], on_vector)
+                dzn_bf[b] = held(f"dzn_bf{b}", [P, N, PACK], BF16)
+            lo, hi = h * HALF_N, (h + 1) * HALF_N
+            interleave(copy, dzn_bf[b][:, lo:hi, :], dz[:, :, b * N + lo : b * N + hi])
 
-        def interleave_wm(b, h, after=None, on_vector=0):
-            wm_bf[b, h] = held(f"wm_bf{b}{h}", [P, HALF, PACK], BF16, after)
-            interleave(wm_bf[b, h][:], wm_sb[b, h][:], on_vector)
+        def gpsimd_copy(out, in_):
+            nc.gpsimd.tensor_scalar(out=out, in0=in_, scalar1=1.0, scalar2=0.0, op0=MULT, op1=ADD)
 
+        def interleave_wm(b, h, copy, reuses=None):
+            wm_bf[b, h] = held(f"wm_bf{b}{h}", [P, HALF_D, PACK], BF16, reuses)
+            interleave(copy, wm_bf[b, h][:], wm_sb[b, h][:])
 
-        wm_q, dzn_q, dzt_q, x_q, dx_sb, x_g, xt_bf, x_bf, x_bank = {}, {}, {}, {}, {}, {}, {}, {}, {}
+        def quantize_wm(b, h, reuses=None):
+            wm_q[b, h] = quantize(f"wm_q{b}{h}", wm_bf[b, h][:].rearrange("p d t -> p (d t)"), HALF_D, E4M3, reuses)
 
-        def quantize_wm(b, h, after=None):
-            wm_q[b, h] = quantize(f"wm_q{b}{h}", wm_bf[b, h][:].rearrange("p d t -> p (d t)"), HALF, E4M3, after)
+        def quantize_dzn(b, reuses=None):
+            dzn_q[b] = quantize(f"dzn_q{b}", dzn_bf[b][:].rearrange("p i t -> p (i t)"), N, E5M2, reuses)
 
-        def quantize_dzn(b, after=None):
-            dzn_q[b] = quantize(f"dzn_q{b}", dzn_bf[b][:].rearrange("p i t -> p (i t)"), N, E5M2, after)
+        def quantize_dzt(b):
+            dzt_q[b] = quantize(f"dzt_q{b}", dzt_bf[b][:].rearrange("s t p k -> s (t p k)"), DV, E5M2)
 
-        def quantize_dzt(b, after=None):
-            dzt_q[b] = quantize(f"dzt_q{b}", dzt_bf[b][:].rearrange("s t p k -> s (t p k)"), DV, E5M2, after)
-
-        def multiply_dx(j, b, on_vector=0, after=None):
-            codes, scales = wm_q[b, j // 2]
-            cols = slice((j % 2) * P, (j % 2 + 1) * P)
-            bank = dx_banks.tile([P, N], F32, name=f"dx_bank{j}{b}", tag=DX_BANK[j, b])
+        def multiply(bank, stationary, cols, moving):
             nc.tensor.matmul_mx(
                 out=bank[:],
-                lhsT=codes[:, cols].bitcast(E4M3),
-                lhsT_scale=scales[:, cols],
-                rhs=dzn_q[b][0][:].bitcast(E5M2),
-                rhs_scale=dzn_q[b][1][:],
+                lhsT=stationary[0][:, cols].bitcast(E4M3),
+                lhsT_scale=stationary[1][:, cols],
+                rhs=moving[0][:].bitcast(E5M2),
+                rhs_scale=moving[1][:],
                 start=True,
                 stop=True,
             )
-            dx_sb[j, b] = held(f"dx_sb{j}{b}", [P, N], F32, after)
-            copy = nc.vector.tensor_copy if on_vector else nc.scalar.copy
-            copy(out=dx_sb[j, b][:], in_=bank[:])
+
+        def multiply_dx(j, b, reuses=None):
+            bank = product_banks.tile([P, N], F32, name=f"dx_bank{j}{b}", tag=DX_BANK[j, b])
+            multiply(bank, wm_q[b, j // 2], slice((j % 2) * P, (j % 2 + 1) * P), dzn_q[b])
+            dx_sb[j, b] = held(f"dx_sb{j}{b}", [P, N], F32, reuses)
+            nc.scalar.copy(out=dx_sb[j, b][:], in_=bank[:])
 
         def scatter(j, b):
-            nc.vector.tensor_copy(windows[j % 2][:].indirect(expert_offsets(b)), dx_sb[j, b][:])
+            window = windows[j % WINDOWS]
+            nc.vector.tensor_copy(window[:].indirect(expert_offsets(b)), dx_sb[j, b][:])
             if b == B - 1:
-                nc.sync.dma_start(out=out_1[j * P : (j + 1) * P, :], in_=windows[j % 2][:])
+                nc.sync.dma_start(out=out_1[j * P : (j + 1) * P, :], in_=window[:])
 
-        def cast_x(j, after=None, on_vector=0):
-            x_bf[j] = held(f"x_bf{j}", [P, T], BF16, after)
-            if on_vector:
-                nc.vector.tensor_copy(x_bf[j][:], x_sb[j][:])
-            else:
-                nc.scalar.activation(x_bf[j][:], x_sb[j][:], COPY)
+        def cast_x(j, reuses):
+            x_bf[j] = held(f"x_bf{j}", [P, T], BF16, reuses)
+            nc.scalar.activation(x_bf[j][:], x_sb[j][:], COPY)
 
-        def gather_x(j, b, after=None):
-            x_g[j, b] = held(f"x_g{j}{b}", [P, 2, N // 2], BF16, after)
+        def gather_x(j, b, reuses=None):
+            x_g[j, b] = held(f"x_g{j}{b}", [P, 2, HALF_N], BF16, reuses)
             parted = x_g[j, b][:].rearrange("p u c -> p c u")
-            if j in x_bf:
-                nc.scalar.activation(parted, x_bf[j][:].indirect(expert_offsets(b)), COPY)
-            else:
+            if j == 0:
                 nc.vector.tensor_copy(parted, x_sb[j][:].indirect(expert_offsets(b)))
-            if j not in x_bank:
+            else:
+                nc.scalar.activation(parted, x_bf[j][:].indirect(expert_offsets(b)), COPY)
+            if b == 0:
                 x_bank[j] = turn_banks.tile([P, B, 2, P], F32, name="turn_bank")
             for u in range(2):
                 nc.tensor.transpose(x_bank[j][:, b, u, :], x_g[j, b][:, u, :].bitcast(F32), ident[:])
 
-        def turn_x(j, after=None):
-            xt_bf[j] = held(f"xt_bf{j}", [P, B * P * PACK], BF16, after)
+        def copy_out_x(j):
+            xt_bf[j] = held(f"xt_bf{j}", [P, B * P * PACK], BF16)
             nc.scalar.copy(
                 out=xt_bf[j][:].bitcast(F32).rearrange("s (b d u) -> s b d u", b=B, u=2),
                 in_=x_bank[j][:].rearrange("s b u d -> s b d u"),
             )
 
-        def quantize_x(j, after=None):
-            x_q[j] = quantize(f"x_q{j}", xt_bf[j][:], B * P, E4M3, after)
+        def quantize_x(j):
+            x_q[j] = quantize(f"x_q{j}", xt_bf[j][:], B * P, E4M3)
 
-        def multiply_gw(j, b, on_vector=0, after=None, own_queue=0):
-            codes, scales = x_q[j]
-            cols = slice(b * P, (b + 1) * P)
-            bank = dx_banks.tile([P, DV], F32, name=f"gw_bank{j}{b}", tag="pq"[b])
-            nc.tensor.matmul_mx(
-                out=bank[:],
-                lhsT=codes[:, cols].bitcast(E4M3),
-                lhsT_scale=scales[:, cols],
-                rhs=dzt_q[b][0][:].bitcast(E5M2),
-                rhs_scale=dzt_q[b][1][:],
-                start=True,
-                stop=True,
-            )
-            gw_sb = held(f"gw_sb{j}{b}", [P, P, PACK], F32, after)
-            copy = nc.vector.tensor_copy if on_vector else nc.scalar.copy
-            copy(out=gw_sb[:], in_=bank[:].rearrange("d (t p) -> d p t", t=PACK))
-            queue = nc.scalar if own_queue else nc.sync
+        def multiply_gw(j, b, queue, reuses=None):
+            bank = product_banks.tile([P, DV], F32, name=f"gw_bank{j}{b}", tag=GW_BANK[b])
+            multiply(bank, x_q[j], slice(b * P, (b + 1) * P), dzt_q[b])
+            gw_sb = held(f"gw_sb{j}{b}", [P, P, PACK], F32, reuses)
+            nc.scalar.copy(out=gw_sb[:], in_=bank[:].rearrange("d (t p) -> d p t", t=PACK))
             queue.dma_start(out=out_0[b, j * P : (j + 1) * P, :], in_=gw_sb[:].rearrange("d p t -> d (p t)"))
 
         nc.vector.tensor_copy(ts_g[:], ts_sb[:].indirect(offsets[:]))
-
-        def gather_dz(t, b):
-            cols = slice(b * N, (b + 1) * N)
-            nc.vector.tensor_tensor(dz[:, t, cols], dy_sb[t][:].indirect(expert_offsets(b)), ts_g[:, cols], MULT)
-
         for t in range(2):
             nc.vector.tensor_tensor(dz[:, t, :], dy_sb[t][:].indirect(offsets[:]), ts_g[:], MULT)
             for b in range(B):
@@ -201,73 +189,61 @@ def tile_attend_gex_wx_kernel(tc, xT, dyT, ts, wm, offs, out_0, out_1):
         turn_dz(2, 0)
         for b in range(B):
             gather_dz(3, b)
+
         load_wm(0, 0)
         load_wm(1, 0)
         load_x(0)
         load_wm(0, 1)
         load_wm(1, 1)
         load_x(1)
-        load_x(2)
-        load_x(3)
-        interleave_dz(0, 0, on_vector=1)
-        interleave_dz(0, 1)
-        interleave_wm(0, 0)
-        interleave_dz(1, 0, on_vector=1)
+        load_x(2, reuses="dy1")
+        load_x(3, reuses="ts_sb")
+
+        interleave_dz(0, 0, nc.vector.tensor_copy)
+        interleave_dz(0, 1, nc.scalar.copy)
+        interleave_wm(0, 0, nc.scalar.copy)
+        interleave_dz(1, 0, nc.vector.tensor_copy)
         quantize_dzn(0)
-        interleave_dz(1, 1, on_vector=1)
+        interleave_dz(1, 1, nc.scalar.copy)
         quantize_wm(0, 0)
         turn_dz(3, 0)
-        gather_x(0, 0, after="dzn_bf0")
-        quantize_dzn(1)
-        gather_x(0, 1, after="wm_bf00")
+        gather_x(0, 0, reuses="dzn_bf0")
+        quantize_dzn(1, reuses="x_g00")
+        gather_x(0, 1, reuses="wm_bf00")
         turn_dz(3, 1)
-        interleave_wm(1, 0)
+        interleave_wm(1, 0, nc.scalar.copy)
         multiply_dx(0, 0)
         turn_dz(2, 1)
         quantize_dzt(0)
         quantize_wm(1, 0)
         scatter(0, 0)
-        interleave_wm(0, 1, after="wm10")
+
+        interleave_wm(0, 1, gpsimd_copy, reuses="wm_bf10")
         quantize_dzt(1)
-        interleave_wm(1, 1, after="wm01")
-        turn_x(0)
+        copy_out_x(0)
         quantize_x(0)
-        multiply_dx(1, 0, after="x_g01")
+        interleave_wm(1, 1, gpsimd_copy, reuses="xt_bf0")
+        multiply_dx(1, 0, reuses="x_g01")
         scatter(1, 0)
-        multiply_dx(0, 1, after="wm11")
+        multiply_dx(0, 1, reuses="dz")
         scatter(0, 1)
-        cast_x(1, after="x_g00")
-        gather_x(1, 0)
-        gather_x(1, 1)
-        multiply_gw(0, 0, after="x1")
-        multiply_gw(0, 1, after="x_g10")
-        turn_x(1)
-        quantize_wm(0, 1, after="dx_sb01")
-        quantize_wm(1, 1, after="dx_sb10")
-        quantize_x(1)
-        multiply_dx(1, 1, after="x_g11")
-        scatter(1, 1)
-        cast_x(2, after="x_bf1")
-        multiply_dx(2, 0)
-        scatter(2, 0)
-        gather_x(2, 0)
-        gather_x(2, 1)
-        multiply_gw(1, 0, after="x2")
-        multiply_gw(1, 1, after="x_g20")
-        turn_x(2)
-        quantize_x(2)
-        multiply_dx(2, 1, after="x_g21")
-        scatter(2, 1)
-        cast_x(3, after="x_bf2")
-        multiply_dx(3, 0)
-        scatter(3, 0)
-        gather_x(3, 0)
-        gather_x(3, 1)
-        multiply_gw(2, 0, after="x3")
-        multiply_gw(2, 1, after="x_g30")
-        turn_x(3)
-        quantize_x(3)
-        multiply_dx(3, 1, after="x_g31")
-        scatter(3, 1)
-        multiply_gw(3, 0, own_queue=1)
-        multiply_gw(3, 1, own_queue=1)
+
+        for j in range(1, BLOCKS):
+            cast_x(j, reuses="wm10" if j == 1 else f"x_bf{j - 1}")
+            if j > 1:
+                multiply_dx(j, 0)
+                scatter(j, 0)
+            for b in range(B):
+                gather_x(j, b)
+            multiply_gw(j - 1, 0, nc.sync, reuses=f"x{j}")
+            multiply_gw(j - 1, 1, nc.sync, reuses=f"x_g{j}0")
+            copy_out_x(j)
+            if j == 1:
+                quantize_wm(0, 1, reuses="dx_sb01")
+                quantize_wm(1, 1, reuses="dx_sb10")
+            quantize_x(j)
+            multiply_dx(j, 1, reuses=f"x_g{j}1")
+            scatter(j, 1)
+
+        for b in range(B):
+            multiply_gw(BLOCKS - 1, b, nc.scalar)

@@ -25,11 +25,8 @@ HALF_D = D // 2
 HALF_N = N // 2
 LIST_COLS = N // 16
 LINE = 4
-WINDOWS = 2
-TURN_BANKS = 3
-SLOT_OF_PLACE = (0, 2, 1, 3)
-DX_BANK = {(0, 0): "p", (0, 1): "p", (1, 0): "q", (1, 1): "r", (2, 0): "p", (2, 1): "r", (3, 0): "p", (3, 1): "r"}
-GW_BANK = ("p", "q")
+QUADRANT = 32
+TURN_BANKS = 4
 
 
 def tile_attend_gex_wx_kernel(tc, xT, dyT, ts, wm, offs, out_0, out_1):
@@ -49,32 +46,32 @@ def tile_attend_gex_wx_kernel(tc, xT, dyT, ts, wm, offs, out_0, out_1):
         offsets = keep.tile([P, B * LIST_COLS], U16, name="offsets")
         ts_sb = held("ts_sb", [P, T], F32)
         dy_sb = [held(f"dy{t}", [P, T], F32) for t in range(PACK)]
-        wm_sb = {(b, h): held(f"wm{b}{h}", [P, PACK, HALF_D], F32) for b in range(B) for h in range(2)}
-
-        dy_planes = dyT.rearrange("(p t) c -> t p c", t=PACK)
-        nc.sync.dma_start(out=ts_sb[:], in_=ts)
-        nc.sync.dma_start(offsets[:], offs)
-        for t in range(PACK):
-            nc.sync.dma_start(out=dy_sb[t][:], in_=dy_planes[t])
+        wm_sb, x_sb, x_bf, x_g, x_bank, xt_bf, x_q = {}, {}, {}, {}, {}, {}, {}
+        dz, dzt_bf, dzt_q, wm_bf, wm_q, dx_sb, ts_all, gw_sb = {}, {}, {}, {}, {}, {}, {}, {}
 
         ident = keep.tile([P, P], F32, name="ident")
         make_identity(nc, ident[:])
 
-        windows = []
-        for w in range(WINDOWS):
-            windows.append(keep.tile([P, T], F32, name=f"window{w}"))
-            nc.vector.memset(windows[w][:].bitcast(I32), 0)
+        nc.sync.dma_start(out=ts_sb[:QUADRANT, :], in_=ts[:QUADRANT, :])
+        nc.gpsimd.memset(ts_sb[QUADRANT : 2 * QUADRANT, :], 0.0)
+        nc.vector.memset(ts_sb[2 * QUADRANT :, :], 0.0)
+        dy_planes = dyT.rearrange("(p t) c -> t p c", t=PACK)
+        nc.sync.dma_start(offsets[:], offs)
+        x_sb[0] = held("x0", [P, T], F32)
+        nc.sync.dma_start(out=x_sb[0][:], in_=xT[:P, :])
+        for t in range(PACK - 1):
+            nc.sync.dma_start(out=dy_sb[t][:], in_=dy_planes[t])
 
-        ts_g = held("ts_g", [P, B * N], F32)
-        dz = held("dz", [P, PACK, B * N], F32)
-        dzt_bf = [held(f"dzt_bf{b}", [P, PACK, P, PACK], BF16) for b in range(B)]
-        x_sb, x_bf, x_g, x_bank, xt_bf, x_q = {}, {}, {}, {}, {}, {}
-        dzn_bf, dzn_q, dzt_q, wm_bf, wm_q, dx_sb = {}, {}, {}, {}, {}, {}
+        windows = []
+        for j in range(BLOCKS):
+            windows.append(keep.tile([P, T], F32, name=f"window{j}"))
+            nc.gpsimd.memset(windows[j][:].bitcast(I32), 0)
 
         def expert_offsets(b):
             return offsets[:, b * LIST_COLS : (b + 1) * LIST_COLS]
 
-        def load_wm(b, h):
+        def load_wm(b, h, reuses=None):
+            wm_sb[b, h] = held(f"wm{b}{h}", [P, PACK, HALF_D], F32, reuses)
             rows = wm[b].rearrange("(p t) d -> p t d", t=PACK)
             nc.sync.dma_start(out=wm_sb[b, h][:], in_=rows[:, :, h * HALF_D : (h + 1) * HALF_D])
 
@@ -82,46 +79,54 @@ def tile_attend_gex_wx_kernel(tc, xT, dyT, ts, wm, offs, out_0, out_1):
             x_sb[j] = held(f"x{j}", [P, T], F32, reuses)
             nc.sync.dma_start(out=x_sb[j][:], in_=xT[j * P : (j + 1) * P, :])
 
-        def quantize(name, src, width, fmt, reuses=None):
+        def planes(name, width, reuses=None):
             codes = held(name + "_codes", [P, width], U32, reuses)
             scales = keep.tile([P, width], U8, name=name + "_scales", align_bytes=64)
-            nc.vector.quantize_mx(out=codes[:].bitcast(fmt), scales=scales[:], in_=src)
             return codes, scales
+
+        def quantize(dst, cols, src, fmt):
+            nc.vector.quantize_mx(out=dst[0][:, cols].bitcast(fmt), scales=dst[1][:, cols], in_=src)
 
         def interleave(copy, dst, src):
             copy(out=dst.rearrange("p (c i) t -> p c t i", i=LINE), in_=src.rearrange("p t (c i) -> p c t i", i=LINE))
 
+        def gpsimd_copy(out, in_):
+            nc.gpsimd.tensor_scalar(out=out, in0=in_, scalar1=1.0, scalar2=0.0, op0=MULT, op1=ADD)
+
+        def spread_ts(b):
+            row = held(f"ts_row{b}", [P, N], F32)
+            nc.vector.tensor_copy(row[:], ts_sb[:].indirect(expert_offsets(b)))
+            down = turn_banks.tile([P, N // P, P], F32, name="turn_bank")
+            for q in range(N // P):
+                nc.tensor.transpose(down[:, q, :], row[:, q * P : (q + 1) * P], ident[:])
+            cols = held(f"ts_cols{b}", [P, N // P], F32)
+            nc.scalar.copy(out=cols[:], in_=down[:, :, 0])
+            across = product_banks.tile([P, N // P, P], F32, name=f"across{b}", tag=f"gw{b}")
+            for q in range(N // P):
+                nc.tensor.transpose(across[:, q, :], cols[:, q : q + 1].to_broadcast([P, P]), ident[:])
+            nc.scalar.copy(out=ts_g[:, b * N : (b + 1) * N], in_=across[:].rearrange("p q s -> p (q s)"))
+
         def gather_dz(t, b):
             cols = slice(b * N, (b + 1) * N)
-            nc.vector.tensor_tensor(dz[:, t, cols], dy_sb[t][:].indirect(expert_offsets(b)), ts_g[:, cols], MULT)
+            nc.vector.tensor_tensor(dz_all[:, t, cols], dy_sb[t][:].indirect(expert_offsets(b)), ts_g[:, cols], MULT)
 
         def turn_dz(t, b):
             bank = turn_banks.tile([P, PACK, P], F32, name="turn_bank")
-            for place, r in enumerate(SLOT_OF_PLACE):
-                nc.tensor.transpose(bank[:, place, :], dz[:, t, b * N + r : (b + 1) * N : PACK], ident[:])
+            for r in range(PACK):
+                nc.tensor.transpose(bank[:, r, :], dz[b][:, t, r:N:PACK], ident[:])
             nc.scalar.activation(dzt_bf[b][:, t], bank[:].rearrange("s k p -> s p k"), COPY)
-
-        def interleave_dz(b, h, copy):
-            if h == 0:
-                dzn_bf[b] = held(f"dzn_bf{b}", [P, N, PACK], BF16)
-            lo, hi = h * HALF_N, (h + 1) * HALF_N
-            interleave(copy, dzn_bf[b][:, lo:hi, :], dz[:, :, b * N + lo : b * N + hi])
-
-        def gpsimd_copy(out, in_):
-            nc.gpsimd.tensor_scalar(out=out, in0=in_, scalar1=1.0, scalar2=0.0, op0=MULT, op1=ADD)
 
         def interleave_wm(b, h, copy, reuses=None):
             wm_bf[b, h] = held(f"wm_bf{b}{h}", [P, HALF_D, PACK], BF16, reuses)
             interleave(copy, wm_bf[b, h][:], wm_sb[b, h][:])
 
         def quantize_wm(b, h, reuses=None):
-            wm_q[b, h] = quantize(f"wm_q{b}{h}", wm_bf[b, h][:].rearrange("p d t -> p (d t)"), HALF_D, E4M3, reuses)
-
-        def quantize_dzn(b, reuses=None):
-            dzn_q[b] = quantize(f"dzn_q{b}", dzn_bf[b][:].rearrange("p i t -> p (i t)"), N, E5M2, reuses)
+            wm_q[b, h] = planes(f"wm_q{b}{h}", HALF_D, reuses)
+            quantize(wm_q[b, h], slice(0, HALF_D), wm_bf[b, h][:].rearrange("p d t -> p (d t)"), E4M3)
 
         def quantize_dzt(b):
-            dzt_q[b] = quantize(f"dzt_q{b}", dzt_bf[b][:].rearrange("s t p k -> s (t p k)"), DV, E5M2)
+            dzt_q[b] = planes(f"dzt_q{b}", DV)
+            quantize(dzt_q[b], slice(0, DV), dzt_bf[b][:].rearrange("s t p k -> s (t p k)"), E5M2)
 
         def multiply(bank, stationary, cols, moving):
             nc.tensor.matmul_mx(
@@ -135,32 +140,34 @@ def tile_attend_gex_wx_kernel(tc, xT, dyT, ts, wm, offs, out_0, out_1):
             )
 
         def multiply_dx(j, b, reuses=None):
-            bank = product_banks.tile([P, N], F32, name=f"dx_bank{j}{b}", tag=DX_BANK[j, b])
+            bank = product_banks.tile([P, N], F32, name=f"dx_bank{j}{b}", tag=f"dx{j % 2}")
             multiply(bank, wm_q[b, j // 2], slice((j % 2) * P, (j % 2 + 1) * P), dzn_q[b])
             dx_sb[j, b] = held(f"dx_sb{j}{b}", [P, N], F32, reuses)
             nc.scalar.copy(out=dx_sb[j, b][:], in_=bank[:])
 
         def scatter(j, b):
-            window = windows[j % WINDOWS]
-            nc.vector.tensor_copy(window[:].indirect(expert_offsets(b)), dx_sb[j, b][:])
+            nc.vector.tensor_copy(windows[j][:].indirect(expert_offsets(b)), dx_sb[j, b][:])
             if b == B - 1:
-                nc.sync.dma_start(out=out_1[j * P : (j + 1) * P, :], in_=window[:])
+                nc.sync.dma_start(out=out_1[j * P : (j + 1) * P, :], in_=windows[j][:])
 
         def cast_x(j, reuses):
             x_bf[j] = held(f"x_bf{j}", [P, T], BF16, reuses)
             nc.scalar.activation(x_bf[j][:], x_sb[j][:], COPY)
 
-        def gather_x(j, b, reuses=None):
-            x_g[j, b] = held(f"x_g{j}{b}", [P, 2, HALF_N], BF16, reuses)
-            parted = x_g[j, b][:].rearrange("p u c -> p c u")
+        def gather_x(j):
+            x_g[j] = held(f"x_g{j}", [P, B * N], BF16)
             if j == 0:
-                nc.vector.tensor_copy(parted, x_sb[j][:].indirect(expert_offsets(b)))
+                x_bank[j] = product_banks.tile([P, B, 2, P], F32, name="x_bank0", tag="gw1")
             else:
-                nc.scalar.activation(parted, x_bf[j][:].indirect(expert_offsets(b)), COPY)
-            if b == 0:
                 x_bank[j] = turn_banks.tile([P, B, 2, P], F32, name="turn_bank")
-            for u in range(2):
-                nc.tensor.transpose(x_bank[j][:, b, u, :], x_g[j, b][:, u, :].bitcast(F32), ident[:])
+            for b in range(B):
+                if j == 0:
+                    nc.vector.tensor_copy(x_g[j][:, b * N : (b + 1) * N], x_sb[j][:].indirect(expert_offsets(b)))
+                else:
+                    nc.scalar.activation(x_g[j][:, b * N : (b + 1) * N], x_bf[j][:].indirect(expert_offsets(b)), COPY)
+                pairs = x_g[j][:, b * N : (b + 1) * N].bitcast(F32)
+                for u in range(2):
+                    nc.tensor.transpose(x_bank[j][:, b, u, :], pairs[:, u:HALF_N:2], ident[:])
 
         def copy_out_x(j):
             xt_bf[j] = held(f"xt_bf{j}", [P, B * P * PACK], BF16)
@@ -170,80 +177,89 @@ def tile_attend_gex_wx_kernel(tc, xT, dyT, ts, wm, offs, out_0, out_1):
             )
 
         def quantize_x(j):
-            x_q[j] = quantize(f"x_q{j}", xt_bf[j][:], B * P, E4M3)
+            x_q[j] = planes(f"x_q{j}", B * P)
+            quantize(x_q[j], slice(0, B * P), xt_bf[j][:], E4M3)
 
-        def multiply_gw(j, b, queue, reuses=None):
-            bank = product_banks.tile([P, DV], F32, name=f"gw_bank{j}{b}", tag=GW_BANK[b])
-            multiply(bank, x_q[j], slice(b * P, (b + 1) * P), dzt_q[b])
-            gw_sb = held(f"gw_sb{j}{b}", [P, P, PACK], F32, reuses)
-            nc.scalar.copy(out=gw_sb[:], in_=bank[:].rearrange("d (t p) -> d p t", t=PACK))
-            queue.dma_start(out=out_0[b, j * P : (j + 1) * P, :], in_=gw_sb[:].rearrange("d p t -> d (p t)"))
-
-        nc.vector.tensor_copy(ts_g[:], ts_sb[:].indirect(offsets[:]))
-        for t in range(2):
-            nc.vector.tensor_tensor(dz[:, t, :], dy_sb[t][:].indirect(offsets[:]), ts_g[:], MULT)
+        def multiply_gw(j, queue, reuses=None):
+            gw_sb[j] = held(f"gw_sb{j}", [P, B, P, PACK], F32, reuses)
             for b in range(B):
-                turn_dz(t, b)
+                bank = product_banks.tile([P, DV], F32, name=f"gw_bank{j}{b}", tag=f"gw{b}")
+                multiply(bank, x_q[j], slice(b * P, (b + 1) * P), dzt_q[b])
+                nc.scalar.copy(out=gw_sb[j][:, b], in_=bank[:].rearrange("d (t p) -> d p t", t=PACK))
+            queue.dma_start(
+                out=out_0[:, j * P : (j + 1) * P, :].rearrange("b d n -> d b n"),
+                in_=gw_sb[j][:].rearrange("d b p t -> d b (p t)"),
+            )
+
         for b in range(B):
-            gather_dz(2, b)
-        turn_dz(2, 0)
+            dzt_bf[b] = held(f"dzt_bf{b}", [P, PACK, P, PACK], BF16)
+        dzn_q = {0: planes("dzn_q0", N)}
+        ts_g = held("ts_g", [P, B * N], F32)
+        dz_all = held("dz", [P, PACK, B * N], F32)
         for b in range(B):
-            gather_dz(3, b)
+            dz[b] = dz_all[:, :, b * N : (b + 1) * N]
 
         load_wm(0, 0)
-        load_wm(1, 0)
-        load_x(0)
-        load_wm(0, 1)
-        load_wm(1, 1)
-        load_x(1)
-        load_x(2, reuses="dy1")
-        load_x(3, reuses="ts_sb")
-
-        interleave_dz(0, 0, nc.vector.tensor_copy)
-        interleave_dz(0, 1, nc.scalar.copy)
-        interleave_wm(0, 0, nc.scalar.copy)
-        interleave_dz(1, 0, nc.vector.tensor_copy)
-        quantize_dzn(0)
-        interleave_dz(1, 1, nc.scalar.copy)
-        quantize_wm(0, 0)
-        turn_dz(3, 0)
-        gather_x(0, 0, reuses="dzn_bf0")
-        quantize_dzn(1, reuses="x_g00")
-        gather_x(0, 1, reuses="wm_bf00")
-        turn_dz(3, 1)
-        interleave_wm(1, 0, nc.scalar.copy)
-        multiply_dx(0, 0)
-        turn_dz(2, 1)
-        quantize_dzt(0)
-        quantize_wm(1, 0)
-        scatter(0, 0)
-
-        interleave_wm(0, 1, gpsimd_copy, reuses="wm_bf10")
-        quantize_dzt(1)
+        nc.sync.dma_start(out=dy_sb[PACK - 1][:], in_=dy_planes[PACK - 1])
+        for b in range(B):
+            spread_ts(b)
+        load_wm(0, 1, reuses="ts_sb")
+        gather_x(0)
         copy_out_x(0)
         quantize_x(0)
-        interleave_wm(1, 1, gpsimd_copy, reuses="xt_bf0")
-        multiply_dx(1, 0, reuses="x_g01")
-        scatter(1, 0)
-        multiply_dx(0, 1, reuses="dz")
-        scatter(0, 1)
+        for t in range(PACK - 1):
+            if t == 0:
+                for b in range(B):
+                    gather_dz(t, b)
+            else:
+                nc.vector.tensor_tensor(dz_all[:, t, :], dy_sb[t][:].indirect(offsets[:]), ts_g[:], MULT)
+            for b in range(B):
+                turn_dz(t, b)
+        interleave_wm(0, 0, nc.scalar.copy)
+        quantize_wm(0, 0)
+        gather_dz(PACK - 1, 0)
+        dzn_bf0 = held("dzn_bf0", [P, N, PACK], BF16)
+        interleave(nc.vector.tensor_copy, dzn_bf0[:, :HALF_N, :], dz[0][:, :, :HALF_N])
+        interleave(nc.scalar.copy, dzn_bf0[:, HALF_N:, :], dz[0][:, :, HALF_N:])
+        turn_dz(PACK - 1, 0)
+        gather_dz(PACK - 1, 1)
+        load_wm(1, 0, reuses="dy0")
+        load_wm(1, 1, reuses="dy1")
+        load_x(1, reuses="dy2")
+        load_x(2, reuses="wm00")
+        load_x(3, reuses="dy3")
+
+        quantize(dzn_q[0], slice(0, N), dzn_bf0[:].rearrange("p i t -> p (i t)"), E5M2)
+        quantize_dzt(0)
+        interleave_wm(1, 0, nc.scalar.copy)
+        quantize_wm(1, 0)
+        turn_dz(PACK - 1, 1)
+        quantize_dzt(1)
+        multiply_dx(0, 0)
+        scatter(0, 0)
+        interleave_wm(0, 1, gpsimd_copy, reuses="dzt_bf1")
+        quantize_wm(0, 1, reuses="dx_sb00")
+
+        def share(k, reuses=None):
+            multiply_dx(k % BLOCKS, k // BLOCKS, reuses)
+            scatter(k % BLOCKS, k // BLOCKS)
 
         for j in range(1, BLOCKS):
-            cast_x(j, reuses="wm10" if j == 1 else f"x_bf{j - 1}")
-            if j > 1:
-                multiply_dx(j, 0)
-                scatter(j, 0)
-            for b in range(B):
-                gather_x(j, b)
-            multiply_gw(j - 1, 0, nc.sync, reuses=f"x{j}")
-            multiply_gw(j - 1, 1, nc.sync, reuses=f"x_g{j}0")
-            copy_out_x(j)
+            cast_x(j, reuses="dzt_bf0" if j == 1 else f"x_bf{j - 1}")
+            share(2 * j - 1, reuses={1: "wm01", 2: "dz", 3: "wm11"}[j])
             if j == 1:
-                quantize_wm(0, 1, reuses="dx_sb01")
-                quantize_wm(1, 1, reuses="dx_sb10")
+                dzn_bf1 = held("dzn_bf1", [P, N, PACK], BF16, reuses="wm_bf01")
+                interleave(gpsimd_copy, dzn_bf1[:], dz[1])
+            if j == 2:
+                interleave_wm(1, 1, gpsimd_copy, reuses="dzn_bf1")
+                quantize_wm(1, 1, reuses="dx_sb30")
+            gather_x(j)
+            copy_out_x(j)
             quantize_x(j)
-            multiply_dx(j, 1, reuses=f"x_g{j}1")
-            scatter(j, 1)
-
-        for b in range(B):
-            multiply_gw(BLOCKS - 1, b, nc.scalar)
+            share(2 * j, reuses=f"x_g{j}")
+            if j == 1:
+                dzn_q[1] = planes("dzn_q1", N, reuses="dx_sb20")
+                quantize(dzn_q[1], slice(0, N), dzn_bf1[:].rearrange("p i t -> p (i t)"), E5M2)
+            multiply_gw(j - 1, nc.sync, reuses=f"x{j}")
+        share(2 * BLOCKS - 1)
+        multiply_gw(BLOCKS - 1, nc.scalar, reuses="x0")

@@ -231,35 +231,44 @@ def tile_attend_gex_wx_kernel(tc, xT, dyT, ts, wm, offs, out_0, out_1):
 
         quantize(dzn_q[0], slice(0, N), dzn_bf0[:].rearrange("p i t -> p (i t)"), E5M2)
         quantize_dzt(0)
-        interleave_wm(1, 0, nc.scalar.copy)
-        quantize_wm(1, 0)
+        interleave_wm(0, 1, nc.scalar.copy)
+        quantize_wm(0, 1)
         turn_dz(PACK - 1, 1)
         quantize_dzt(1)
-        multiply_dx(0, 0)
-        scatter(0, 0)
-        interleave_wm(0, 1, gpsimd_copy, reuses="dzt_bf1")
-        quantize_wm(0, 1, reuses="dx_sb00")
 
         def share(k, reuses=None):
             multiply_dx(k % BLOCKS, k // BLOCKS, reuses)
             scatter(k % BLOCKS, k // BLOCKS)
 
-        for j in range(1, BLOCKS):
-            cast_x(j, reuses="dzt_bf0" if j == 1 else f"x_bf{j - 1}")
-            share(2 * j - 1, reuses={1: "wm01", 2: "dz", 3: "wm11"}[j])
-            if j == 1:
-                dzn_bf1 = held("dzn_bf1", [P, N, PACK], BF16, reuses="wm_bf01")
-                interleave(gpsimd_copy, dzn_bf1[:], dz[1])
-            if j == 2:
-                interleave_wm(1, 1, gpsimd_copy, reuses="dzn_bf1")
-                quantize_wm(1, 1, reuses="dx_sb30")
-            gather_x(j)
-            copy_out_x(j)
-            quantize_x(j)
-            share(2 * j, reuses=f"x_g{j}")
-            if j == 1:
-                dzn_q[1] = planes("dzn_q1", N, reuses="dx_sb20")
-                quantize(dzn_q[1], slice(0, N), dzn_bf1[:].rearrange("p i t -> p (i t)"), E5M2)
-            multiply_gw(j - 1, nc.sync, reuses=f"x{j}")
-        share(2 * BLOCKS - 1)
-        multiply_gw(BLOCKS - 1, nc.scalar, reuses="x0")
+        dzn_bf1 = held("dzn_bf1", [P, N, PACK], BF16, reuses="dzt_bf1")
+        interleave(gpsimd_copy, dzn_bf1[:], dz[1])
+        interleave_wm(1, 0, gpsimd_copy, reuses="dz")
+        for k in range(3):
+            share(k)
+        cast_x(1, reuses="dzt_bf0")
+        gather_x(1)
+        copy_out_x(1)
+        quantize_x(1)
+        dzn_q[1] = planes("dzn_q1", N, reuses="dx_sb20")
+        quantize(dzn_q[1], slice(0, N), dzn_bf1[:].rearrange("p i t -> p (i t)"), E5M2)
+        quantize_wm(1, 0)
+        interleave_wm(1, 1, gpsimd_copy, reuses="wm_bf10")
+        multiply_gw(0, nc.sync, reuses="x1")
+
+        cast_x(2, reuses="x_bf1")
+        share(3, reuses="wm10")
+        quantize_wm(1, 1, reuses="dx_sb30")
+        gather_x(2)
+        copy_out_x(2)
+        quantize_x(2)
+        share(4, reuses="x_g2")
+        share(5, reuses="xt_bf2")
+        multiply_gw(1, nc.sync, reuses="x2")
+        cast_x(3, reuses="x_bf2")
+        gather_x(3)
+        copy_out_x(3)
+        quantize_x(3)
+        share(6, reuses="x_g3")
+        multiply_gw(2, nc.scalar, reuses="x3")
+        share(7, reuses="xt_bf3")
+        multiply_gw(3, nc.scalar, reuses="x0")

@@ -25,8 +25,7 @@ HALF_D = D // 2
 HALF_N = N // 2
 LIST_COLS = N // 16
 LINE = 4
-QUADRANT = 32
-TURN_BANKS = 4
+LAST = P - 1
 
 
 def tile_attend_gex_wx_kernel(tc, xT, dyT, ts, wm, offs, out_0, out_1):
@@ -34,8 +33,7 @@ def tile_attend_gex_wx_kernel(tc, xT, dyT, ts, wm, offs, out_0, out_1):
 
     with ExitStack() as ctx:
         keep = ctx.enter_context(tc.tile_pool(name="keep", bufs=1))
-        turn_banks = ctx.enter_context(tc.psum_pool(name="turn_banks", bufs=TURN_BANKS))
-        product_banks = ctx.enter_context(tc.psum_pool(name="product_banks", bufs=1))
+        psum = ctx.enter_context(tc.psum_pool(name="psum", bufs=1))
 
         tag_of = {}
 
@@ -43,24 +41,21 @@ def tile_attend_gex_wx_kernel(tc, xT, dyT, ts, wm, offs, out_0, out_1):
             tag_of[name] = tag_of[reuses] if reuses else name
             return keep.tile(shape, dtype, name=name, tag=tag_of[name], align_bytes=64)
 
+        def bank(name, shape, number):
+            return psum.tile(shape, F32, name=name, tag=f"bank{number}")
+
         offsets = keep.tile([P, B * LIST_COLS], U16, name="offsets")
         ts_sb = held("ts_sb", [P, T], F32)
-        dy_sb = [held(f"dy{t}", [P, T], F32) for t in range(PACK)]
-        wm_sb, x_sb, x_bf, x_g, x_bank, xt_bf, x_q = {}, {}, {}, {}, {}, {}, {}
-        dz, dzt_bf, dzt_q, wm_bf, wm_q, dx_sb, ts_all, gw_sb = {}, {}, {}, {}, {}, {}, {}, {}
+        dy_sb, wm_sb, x_sb, x_bf, x_g, x_bank, xt_bf, x_q = {}, {}, {}, {}, {}, {}, {}, {}
+        ts_g, dz, dzt_bf, dzt_q, dzn_q, wm_bf, wm_q = {}, {}, {}, {}, {}, {}, {}
 
         ident = keep.tile([P, P], F32, name="ident")
         make_identity(nc, ident[:])
 
-        nc.sync.dma_start(out=ts_sb[:QUADRANT, :], in_=ts[:QUADRANT, :])
-        nc.gpsimd.memset(ts_sb[QUADRANT : 2 * QUADRANT, :], 0.0)
-        nc.vector.memset(ts_sb[2 * QUADRANT :, :], 0.0)
-        dy_planes = dyT.rearrange("(p t) c -> t p c", t=PACK)
+        nc.sync.dma_start(out=ts_sb[LAST:, :], in_=ts[LAST:, :])
+        nc.gpsimd.memset(ts_sb[:LAST, : T // 2], 0.0)
+        nc.vector.memset(ts_sb[:LAST, T // 2 :], 0.0)
         nc.sync.dma_start(offsets[:], offs)
-        x_sb[0] = held("x0", [P, T], F32)
-        nc.sync.dma_start(out=x_sb[0][:], in_=xT[:P, :])
-        for t in range(PACK - 1):
-            nc.sync.dma_start(out=dy_sb[t][:], in_=dy_planes[t])
 
         windows = []
         for j in range(BLOCKS):
@@ -70,13 +65,17 @@ def tile_attend_gex_wx_kernel(tc, xT, dyT, ts, wm, offs, out_0, out_1):
         def expert_offsets(b):
             return offsets[:, b * LIST_COLS : (b + 1) * LIST_COLS]
 
-        def load_wm(b, h, reuses=None):
-            wm_sb[b, h] = held(f"wm{b}{h}", [P, PACK, HALF_D], F32, reuses)
+        def load_dy(t):
+            dy_sb[t] = held(f"dy{t}", [P, T], F32)
+            nc.sync.dma_start(out=dy_sb[t][:], in_=dyT.rearrange("(p t) c -> t p c", t=PACK)[t])
+
+        def load_wm(b, h):
+            wm_sb[b, h] = held(f"wm{b}{h}", [P, PACK, HALF_D], F32)
             rows = wm[b].rearrange("(p t) d -> p t d", t=PACK)
             nc.sync.dma_start(out=wm_sb[b, h][:], in_=rows[:, :, h * HALF_D : (h + 1) * HALF_D])
 
-        def load_x(j, reuses=None):
-            x_sb[j] = held(f"x{j}", [P, T], F32, reuses)
+        def load_x(j):
+            x_sb[j] = held(f"x{j}", [P, T], F32)
             nc.sync.dma_start(out=x_sb[j][:], in_=xT[j * P : (j + 1) * P, :])
 
         def planes(name, width, reuses=None):
@@ -84,53 +83,73 @@ def tile_attend_gex_wx_kernel(tc, xT, dyT, ts, wm, offs, out_0, out_1):
             scales = keep.tile([P, width], U8, name=name + "_scales", align_bytes=64)
             return codes, scales
 
-        def quantize(dst, cols, src, fmt):
+        def quantize(dst, src, fmt, cols=slice(None)):
             nc.vector.quantize_mx(out=dst[0][:, cols].bitcast(fmt), scales=dst[1][:, cols], in_=src)
 
-        def interleave(copy, dst, src):
-            copy(out=dst.rearrange("p (c i) t -> p c t i", i=LINE), in_=src.rearrange("p t (c i) -> p c t i", i=LINE))
+        def scalar_interleave(dst, src):
+            nc.scalar.copy(
+                out=dst.rearrange("p (c i) t -> p c t i", i=LINE), in_=src.rearrange("p t (c i) -> p c t i", i=LINE)
+            )
 
-        def gpsimd_copy(out, in_):
-            nc.gpsimd.tensor_scalar(out=out, in0=in_, scalar1=1.0, scalar2=0.0, op0=MULT, op1=ADD)
+        def gpsimd_interleave(dst, src):
+            nc.gpsimd.tensor_scalar(
+                out=dst, in0=src.rearrange("p t c -> p c t"), scalar1=1.0, scalar2=0.0, op0=MULT, op1=ADD
+            )
 
-        def spread_ts(b):
+        def spread_ts(b, pieces, down_bank, across_bank):
             row = held(f"ts_row{b}", [P, N], F32)
-            nc.vector.tensor_copy(row[:], ts_sb[:].indirect(expert_offsets(b)))
-            down = turn_banks.tile([P, N // P, P], F32, name="turn_bank")
-            for q in range(N // P):
-                nc.tensor.transpose(down[:, q, :], row[:, q * P : (q + 1) * P], ident[:])
+            down = bank(f"down{b}", [P, N // P, P], down_bank)
+            width = N // pieces
+            for first in range(0, N, width):
+                entries = expert_offsets(b)[:, first // 16 : (first + width) // 16]
+                nc.vector.tensor_copy(row[:, first : first + width], ts_sb[:].indirect(entries))
+                for q in range(first // P, (first + width) // P):
+                    nc.tensor.transpose(down[:, q, :], row[:, q * P : (q + 1) * P], ident[:])
             cols = held(f"ts_cols{b}", [P, N // P], F32)
-            nc.scalar.copy(out=cols[:], in_=down[:, :, 0])
-            across = product_banks.tile([P, N // P, P], F32, name=f"across{b}", tag=f"gw{b}")
+            nc.scalar.copy(out=cols[:], in_=down[:, :, LAST])
+            across = bank(f"across{b}", [P, N // P, P], across_bank)
             for q in range(N // P):
                 nc.tensor.transpose(across[:, q, :], cols[:, q : q + 1].to_broadcast([P, P]), ident[:])
-            nc.scalar.copy(out=ts_g[:, b * N : (b + 1) * N], in_=across[:].rearrange("p q s -> p (q s)"))
+            ts_g[b] = held(f"ts_g{b}", [P, N], F32)
+            nc.scalar.copy(out=ts_g[b][:], in_=across[:].rearrange("p q s -> p (q s)"))
 
         def gather_dz(t, b):
-            cols = slice(b * N, (b + 1) * N)
-            nc.vector.tensor_tensor(dz_all[:, t, cols], dy_sb[t][:].indirect(expert_offsets(b)), ts_g[:, cols], MULT)
+            nc.vector.tensor_tensor(dz[t, b], dy_sb[t][:].indirect(expert_offsets(b)), ts_g[b][:], MULT)
 
-        def turn_dz(t, b):
-            bank = turn_banks.tile([P, PACK, P], F32, name="turn_bank")
+        def turn_dz(t, b, number):
+            copy_out_dz(t, b, turn_planes(t, b, number))
+
+        def turn_planes(t, b, number):
+            turned = bank(f"turned{t}{b}", [P, PACK, P], number)
             for r in range(PACK):
-                nc.tensor.transpose(bank[:, r, :], dz[b][:, t, r:N:PACK], ident[:])
-            nc.scalar.activation(dzt_bf[b][:, t], bank[:].rearrange("s k p -> s p k"), COPY)
+                nc.tensor.transpose(turned[:, r, :], dz[t, b][:, r:N:PACK], ident[:])
+            return turned
 
-        def interleave_wm(b, h, copy, reuses=None):
+        def copy_out_dz(t, b, turned):
+            nc.scalar.activation(dzt_bf[b, t // 2][:, t % 2], turned[:].rearrange("s k p -> s p k"), COPY)
+
+        def interleave_wm(b, h, interleave, reuses=None):
             wm_bf[b, h] = held(f"wm_bf{b}{h}", [P, HALF_D, PACK], BF16, reuses)
-            interleave(copy, wm_bf[b, h][:], wm_sb[b, h][:])
+            interleave(wm_bf[b, h][:], wm_sb[b, h][:])
 
         def quantize_wm(b, h, reuses=None):
             wm_q[b, h] = planes(f"wm_q{b}{h}", HALF_D, reuses)
-            quantize(wm_q[b, h], slice(0, HALF_D), wm_bf[b, h][:].rearrange("p d t -> p (d t)"), E4M3)
+            quantize(wm_q[b, h], wm_bf[b, h][:].rearrange("p d t -> p (d t)"), E4M3)
 
-        def quantize_dzt(b):
-            dzt_q[b] = planes(f"dzt_q{b}", DV)
-            quantize(dzt_q[b], slice(0, DV), dzt_bf[b][:].rearrange("s t p k -> s (t p k)"), E5M2)
+        def turned_tile(b, h, reuses=None):
+            dzt_bf[b, h] = held(f"dzt_bf{b}{h}", [P, 2, P, PACK], BF16, reuses)[:]
 
-        def multiply(bank, stationary, cols, moving):
+        def quantize_dzt(b, h):
+            cols = slice(h * DV // 2, (h + 1) * DV // 2)
+            quantize(dzt_q[b], dzt_bf[b, h].rearrange("s t p k -> s (t p k)"), E5M2, cols)
+
+        def quantize_dzn(b, src, reuses=None):
+            dzn_q[b] = planes(f"dzn_q{b}", N, reuses)
+            quantize(dzn_q[b], src[:].rearrange("p i t -> p (i t)"), E5M2)
+
+        def multiply(out, stationary, cols, moving):
             nc.tensor.matmul_mx(
-                out=bank[:],
+                out=out[:],
                 lhsT=stationary[0][:, cols].bitcast(E4M3),
                 lhsT_scale=stationary[1][:, cols],
                 rhs=moving[0][:].bitcast(E5M2),
@@ -139,14 +158,13 @@ def tile_attend_gex_wx_kernel(tc, xT, dyT, ts, wm, offs, out_0, out_1):
                 stop=True,
             )
 
-        def multiply_dx(j, b, reuses=None):
-            bank = product_banks.tile([P, N], F32, name=f"dx_bank{j}{b}", tag=f"dx{j % 2}")
-            multiply(bank, wm_q[b, j // 2], slice((j % 2) * P, (j % 2 + 1) * P), dzn_q[b])
-            dx_sb[j, b] = held(f"dx_sb{j}{b}", [P, N], F32, reuses)
-            nc.scalar.copy(out=dx_sb[j, b][:], in_=bank[:])
-
-        def scatter(j, b):
-            nc.vector.tensor_copy(windows[j][:].indirect(expert_offsets(b)), dx_sb[j, b][:])
+        def share(k, number, reuses=None):
+            j, b = k % BLOCKS, k // BLOCKS
+            product = bank(f"dx{k}", [P, N], number)
+            multiply(product, wm_q[b, j // 2], slice((j % 2) * P, (j % 2 + 1) * P), dzn_q[b])
+            dx_sb = held(f"dx_sb{k}", [P, N], F32, reuses)
+            nc.scalar.copy(out=dx_sb[:], in_=product[:])
+            nc.vector.tensor_copy(windows[j][:].indirect(expert_offsets(b)), dx_sb[:])
             if b == B - 1:
                 nc.sync.dma_start(out=out_1[j * P : (j + 1) * P, :], in_=windows[j][:])
 
@@ -154,20 +172,17 @@ def tile_attend_gex_wx_kernel(tc, xT, dyT, ts, wm, offs, out_0, out_1):
             x_bf[j] = held(f"x_bf{j}", [P, T], BF16, reuses)
             nc.scalar.activation(x_bf[j][:], x_sb[j][:], COPY)
 
-        def gather_x(j):
-            x_g[j] = held(f"x_g{j}", [P, B * N], BF16)
-            if j == 0:
-                x_bank[j] = product_banks.tile([P, B, 2, P], F32, name="x_bank0", tag="gw1")
-            else:
-                x_bank[j] = turn_banks.tile([P, B, 2, P], F32, name="turn_bank")
+        def turn_x(j, b):
+            pairs = x_g[j, b].bitcast(F32)
+            for u in range(2):
+                nc.tensor.transpose(x_bank[j][:, b, u, :], pairs[:, u:HALF_N:2], ident[:])
+
+        def gather_x(j, number):
+            x_bank[j] = bank(f"x_bank{j}", [P, B, 2, P], number)
             for b in range(B):
-                if j == 0:
-                    nc.vector.tensor_copy(x_g[j][:, b * N : (b + 1) * N], x_sb[j][:].indirect(expert_offsets(b)))
-                else:
-                    nc.scalar.activation(x_g[j][:, b * N : (b + 1) * N], x_bf[j][:].indirect(expert_offsets(b)), COPY)
-                pairs = x_g[j][:, b * N : (b + 1) * N].bitcast(F32)
-                for u in range(2):
-                    nc.tensor.transpose(x_bank[j][:, b, u, :], pairs[:, u:HALF_N:2], ident[:])
+                x_g[j, b] = held(f"x_g{j}{b}", [P, N], BF16)[:]
+                nc.scalar.activation(x_g[j, b], x_bf[j][:].indirect(expert_offsets(b)), COPY)
+                turn_x(j, b)
 
         def copy_out_x(j):
             xt_bf[j] = held(f"xt_bf{j}", [P, B * P * PACK], BF16)
@@ -176,99 +191,129 @@ def tile_attend_gex_wx_kernel(tc, xT, dyT, ts, wm, offs, out_0, out_1):
                 in_=x_bank[j][:].rearrange("s b u d -> s b d u"),
             )
 
-        def quantize_x(j):
-            x_q[j] = planes(f"x_q{j}", B * P)
-            quantize(x_q[j], slice(0, B * P), xt_bf[j][:], E4M3)
+        def quantize_x(j, reuses=None):
+            x_q[j] = planes(f"x_q{j}", B * P, reuses)
+            quantize(x_q[j], xt_bf[j][:], E4M3)
 
-        def multiply_gw(j, queue, reuses=None):
-            gw_sb[j] = held(f"gw_sb{j}", [P, B, P, PACK], F32, reuses)
-            for b in range(B):
-                bank = product_banks.tile([P, DV], F32, name=f"gw_bank{j}{b}", tag=f"gw{b}")
-                multiply(bank, x_q[j], slice(b * P, (b + 1) * P), dzt_q[b])
-                nc.scalar.copy(out=gw_sb[j][:, b], in_=bank[:].rearrange("d (t p) -> d p t", t=PACK))
-            queue.dma_start(
-                out=out_0[:, j * P : (j + 1) * P, :].rearrange("b d n -> d b n"),
-                in_=gw_sb[j][:].rearrange("d b p t -> d b (p t)"),
-            )
+        def multiply_gw(j, b, number, queue, reuses=None):
+            product = bank(f"gw{j}{b}", [P, DV], number)
+            multiply(product, x_q[j], slice(b * P, (b + 1) * P), dzt_q[b])
+            gw_sb = held(f"gw_sb{j}{b}", [P, P, PACK], F32, reuses)
+            nc.scalar.copy(out=gw_sb[:], in_=product[:].rearrange("d (t p) -> d p t", t=PACK))
+            queue.dma_start(out=out_0[b, j * P : (j + 1) * P, :], in_=gw_sb[:].rearrange("d p t -> d (p t)"))
 
-        for b in range(B):
-            dzt_bf[b] = held(f"dzt_bf{b}", [P, PACK, P, PACK], BF16)
-        dzn_q = {0: planes("dzn_q0", N)}
-        ts_g = held("ts_g", [P, B * N], F32)
-        dz_all = held("dz", [P, PACK, B * N], F32)
-        for b in range(B):
-            dz[b] = dz_all[:, :, b * N : (b + 1) * N]
-
+        load_x(0)
+        load_dy(0)
         load_wm(0, 0)
-        nc.sync.dma_start(out=dy_sb[PACK - 1][:], in_=dy_planes[PACK - 1])
+        load_dy(1)
+        load_dy(2)
+        load_dy(3)
+        load_wm(0, 1)
+        load_wm(1, 0)
+        load_x(1)
+        load_wm(1, 1)
+        load_x(2)
+        load_x(3)
+
+        def pair_tile(b, h, reuses=None):
+            pair = held(f"dz{b}{h}", [P, 2, N], F32, reuses)
+            for e in range(2):
+                dz[2 * h + e, b] = pair[:, e, :]
+            return pair
+
+        def interleave_pair(interleave, dst, h, pair):
+            interleave(dst[:, :, 2 * h : 2 * h + 2], pair[:])
+
+        def scalar_pair(dst, src):
+            nc.scalar.copy(out=dst, in_=src.rearrange("p t i -> p i t"))
+
+        pairs = {(b, h): pair_tile(b, h) for b, h in ((0, 0), (1, 0), (0, 1))}
+
+        spread_ts(0, 2, 0, 1)
+        spread_ts(1, 1, 0, 3)
+        x_g0 = held("x_g0", [P, B * N], BF16)
+        x_bank[0] = bank("x_bank0", [P, B, 2, P], 0)
+        nc.vector.tensor_copy(x_g0[:], x_sb[0][:].indirect(offsets[:]))
         for b in range(B):
-            spread_ts(b)
-        load_wm(0, 1, reuses="ts_sb")
-        gather_x(0)
+            x_g[0, b] = x_g0[:, b * N : (b + 1) * N]
+            turn_x(0, b)
         copy_out_x(0)
-        quantize_x(0)
-        for t in range(PACK - 1):
-            if t == 0:
-                for b in range(B):
-                    gather_dz(t, b)
-            else:
-                nc.vector.tensor_tensor(dz_all[:, t, :], dy_sb[t][:].indirect(offsets[:]), ts_g[:], MULT)
-            for b in range(B):
-                turn_dz(t, b)
-        interleave_wm(0, 0, nc.scalar.copy)
+        interleave_wm(0, 0, scalar_interleave, reuses="x_g0")
+        first_turned = held("first_turned", [P, B, 2, P, PACK], BF16, reuses="wm00")
+        for b in range(B):
+            dzt_bf[b, 0] = first_turned[:, b]
+        gather_dz(0, 0)
+        turn_dz(0, 0, 4)
+        gather_dz(0, 1)
+        turn_dz(0, 1, 5)
+        quantize_x(0, reuses="dy0")
         quantize_wm(0, 0)
-        gather_dz(PACK - 1, 0)
+        gather_dz(1, 0)
         dzn_bf0 = held("dzn_bf0", [P, N, PACK], BF16)
-        interleave(nc.vector.tensor_copy, dzn_bf0[:, :HALF_N, :], dz[0][:, :, :HALF_N])
-        interleave(nc.scalar.copy, dzn_bf0[:, HALF_N:, :], dz[0][:, :, HALF_N:])
-        turn_dz(PACK - 1, 0)
-        gather_dz(PACK - 1, 1)
-        load_wm(1, 0, reuses="dy0")
-        load_wm(1, 1, reuses="dy1")
-        load_x(1, reuses="dy2")
-        load_x(2, reuses="wm00")
-        load_x(3, reuses="dy3")
-
-        quantize(dzn_q[0], slice(0, N), dzn_bf0[:].rearrange("p i t -> p (i t)"), E5M2)
-        quantize_dzt(0)
-        interleave_wm(0, 1, nc.scalar.copy)
+        interleave_pair(scalar_pair, dzn_bf0, 0, pairs[0, 0])
+        turn_dz(1, 0, 6)
+        gather_dz(1, 1)
+        turn_dz(1, 1, 7)
+        gather_dz(2, 0)
+        turned20 = turn_planes(2, 0, 1)
+        gather_dz(3, 0)
+        interleave_pair(scalar_pair, dzn_bf0, 1, pairs[0, 1])
+        turned30 = turn_planes(3, 0, 2)
+        pairs[1, 1] = pair_tile(1, 1, reuses="ts_g0")
+        gather_dz(2, 1)
+        interleave_wm(0, 1, scalar_interleave, reuses="dy2")
+        turned_tile(0, 1, reuses="dz01")
+        copy_out_dz(2, 0, turned20)
+        copy_out_dz(3, 0, turned30)
+        gather_dz(3, 1)
+        quantize_dzn(0, dzn_bf0)
+        dzt_q[0] = planes("dzt_q0", DV, reuses="wm01")
+        dzt_q[1] = planes("dzt_q1", DV, reuses="dzn_bf0")
+        quantize_dzt(0, 0)
+        quantize_dzt(1, 0)
         quantize_wm(0, 1)
-        turn_dz(PACK - 1, 1)
-        quantize_dzt(1)
+        quantize_dzt(0, 1)
 
-        def share(k, reuses=None):
-            multiply_dx(k % BLOCKS, k // BLOCKS, reuses)
-            scatter(k % BLOCKS, k // BLOCKS)
+        interleave_wm(1, 0, gpsimd_interleave, reuses="dzt_bf01")
+        dzn_bf1 = held("dzn_bf1", [P, N, PACK], BF16, reuses="wm10")
+        for h in range(2):
+            interleave_pair(gpsimd_interleave, dzn_bf1, h, pairs[1, h])
+        share(0, 5)
+        share(1, 6)
 
-        dzn_bf1 = held("dzn_bf1", [P, N, PACK], BF16, reuses="dzt_bf1")
-        interleave(gpsimd_copy, dzn_bf1[:], dz[1])
-        interleave_wm(1, 0, gpsimd_copy, reuses="dz")
-        for k in range(3):
-            share(k)
-        cast_x(1, reuses="dzt_bf0")
-        gather_x(1)
+        cast_x(1, reuses="wm_q00_codes")
+        turned_tile(1, 1, reuses="x1")
+        turn_dz(2, 1, 5)
+        turn_dz(3, 1, 6)
+        quantize_dzt(1, 1)
+        quantize_dzn(1, dzn_bf1)
+        gather_x(1, 1)
+        quantize_wm(1, 0, reuses="x_g10")
+        share(2, 0, reuses="x_bf1")
         copy_out_x(1)
         quantize_x(1)
-        dzn_q[1] = planes("dzn_q1", N, reuses="dx_sb20")
-        quantize(dzn_q[1], slice(0, N), dzn_bf1[:].rearrange("p i t -> p (i t)"), E5M2)
-        quantize_wm(1, 0)
-        interleave_wm(1, 1, gpsimd_copy, reuses="wm_bf10")
-        multiply_gw(0, nc.sync, reuses="x1")
+        interleave_wm(1, 1, gpsimd_interleave, reuses="xt_bf1")
 
-        cast_x(2, reuses="x_bf1")
-        share(3, reuses="wm10")
-        quantize_wm(1, 1, reuses="dx_sb30")
-        gather_x(2)
+        cast_x(2, reuses="x_g11")
+        share(3, 7, reuses="x2")
+        gather_x(2, 4)
+        quantize_wm(1, 1, reuses="x_g20")
+        multiply_gw(0, 0, 2, nc.sync, reuses="x_bf2")
         copy_out_x(2)
         quantize_x(2)
-        share(4, reuses="x_g2")
-        share(5, reuses="xt_bf2")
-        multiply_gw(1, nc.sync, reuses="x2")
-        cast_x(3, reuses="x_bf2")
-        gather_x(3)
+        share(4, 0, reuses="x_g21")
+        share(5, 2)
+        multiply_gw(0, 1, 4, nc.scalar)
+        multiply_gw(1, 0, 0, nc.scalar)
+        multiply_gw(1, 1, 2, nc.scalar)
+
+        cast_x(3, reuses="x_q1_codes")
+        share(6, 4, reuses="x3")
+        gather_x(3, 5)
+        multiply_gw(2, 0, 2, nc.scalar, reuses="x_bf3")
         copy_out_x(3)
         quantize_x(3)
-        share(6, reuses="x_g3")
-        multiply_gw(2, nc.scalar, reuses="x3")
-        share(7, reuses="xt_bf3")
-        multiply_gw(3, nc.scalar, reuses="x0")
+        share(7, 0, reuses="x_g31")
+        multiply_gw(2, 1, 2, nc.scalar)
+        multiply_gw(3, 0, 7, nc.scalar)
+        multiply_gw(3, 1, 6, nc.scalar)

@@ -58,9 +58,10 @@ def tile_attend_gex_wx_kernel(tc, xT, dyT, ts, wm, offs, out_0, out_1):
         nc.sync.dma_start(offsets[:], offs)
 
         windows = []
-        for j in range(BLOCKS):
+        for j in range(BLOCKS - 1):
             windows.append(keep.tile([P, T], F32, name=f"window{j}"))
             nc.gpsimd.memset(windows[j][:].bitcast(I32), 0)
+        windows.append(windows[0])
 
         def expert_offsets(b):
             return offsets[:, b * LIST_COLS : (b + 1) * LIST_COLS]
@@ -159,7 +160,7 @@ def tile_attend_gex_wx_kernel(tc, xT, dyT, ts, wm, offs, out_0, out_1):
             )
 
         def share(k, number, reuses=None):
-            j, b = k % BLOCKS, k // BLOCKS
+            j, b = (k % (BLOCKS - 1), k // (BLOCKS - 1)) if k < B * (BLOCKS - 1) else (BLOCKS - 1, k % B)
             product = bank(f"dx{k}", [P, N], number)
             multiply(product, wm_q[b, j // 2], slice((j % 2) * P, (j % 2 + 1) * P), dzn_q[b])
             dx_sb = held(f"dx_sb{k}", [P, N], F32, reuses)
@@ -204,8 +205,8 @@ def tile_attend_gex_wx_kernel(tc, xT, dyT, ts, wm, offs, out_0, out_1):
 
         load_x(0)
         load_dy(0)
-        load_wm(0, 0)
         load_dy(1)
+        load_wm(0, 0)
         load_dy(2)
         load_dy(3)
         load_wm(0, 1)
@@ -227,7 +228,7 @@ def tile_attend_gex_wx_kernel(tc, xT, dyT, ts, wm, offs, out_0, out_1):
         def scalar_pair(dst, src):
             nc.scalar.copy(out=dst, in_=src.rearrange("p t i -> p i t"))
 
-        pairs = {(b, h): pair_tile(b, h) for b, h in ((0, 0), (1, 0), (0, 1))}
+        pairs = {(b, 0): pair_tile(b, 0) for b in range(B)}
 
         spread_ts(0, 2, 0, 1)
         spread_ts(1, 1, 0, 3)
@@ -239,21 +240,22 @@ def tile_attend_gex_wx_kernel(tc, xT, dyT, ts, wm, offs, out_0, out_1):
             turn_x(0, b)
         copy_out_x(0)
         interleave_wm(0, 0, scalar_interleave, reuses="x_g0")
-        first_turned = held("first_turned", [P, B, 2, P, PACK], BF16, reuses="wm00")
+        first_turned = held("first_turned", [P, B, 2, P, PACK], BF16)
         for b in range(B):
             dzt_bf[b, 0] = first_turned[:, b]
         gather_dz(0, 0)
         turn_dz(0, 0, 4)
         gather_dz(0, 1)
         turn_dz(0, 1, 5)
-        quantize_x(0, reuses="dy0")
-        quantize_wm(0, 0)
         gather_dz(1, 0)
-        dzn_bf0 = held("dzn_bf0", [P, N, PACK], BF16)
+        dzn_bf0 = held("dzn_bf0", [P, N, PACK], BF16, reuses="wm00")
         interleave_pair(scalar_pair, dzn_bf0, 0, pairs[0, 0])
         turn_dz(1, 0, 6)
         gather_dz(1, 1)
         turn_dz(1, 1, 7)
+        quantize_x(0)
+        quantize_wm(0, 0)
+        pairs[0, 1] = pair_tile(0, 1, reuses="dy0")
         gather_dz(2, 0)
         turned20 = turn_planes(2, 0, 1)
         gather_dz(3, 0)
@@ -295,25 +297,25 @@ def tile_attend_gex_wx_kernel(tc, xT, dyT, ts, wm, offs, out_0, out_1):
         interleave_wm(1, 1, gpsimd_interleave, reuses="xt_bf1")
 
         cast_x(2, reuses="x_g11")
-        share(3, 7, reuses="x2")
+        share(3, 0, reuses="x2")
         gather_x(2, 4)
         quantize_wm(1, 1, reuses="x_g20")
         multiply_gw(0, 0, 2, nc.sync, reuses="x_bf2")
         copy_out_x(2)
         quantize_x(2)
         share(4, 0, reuses="x_g21")
-        share(5, 2)
-        multiply_gw(0, 1, 4, nc.scalar)
-        multiply_gw(1, 0, 0, nc.scalar)
-        multiply_gw(1, 1, 2, nc.scalar)
+        multiply_gw(0, 1, 2, nc.sync)
+        multiply_gw(1, 0, 4, nc.sync)
+        share(5, 0)
 
-        cast_x(3, reuses="x_q1_codes")
+        cast_x(3, reuses="x_q0_codes")
         share(6, 4, reuses="x3")
         gather_x(3, 5)
-        multiply_gw(2, 0, 2, nc.scalar, reuses="x_bf3")
+        multiply_gw(2, 0, 2, nc.sync, reuses="x_bf3")
         copy_out_x(3)
         quantize_x(3)
         share(7, 0, reuses="x_g31")
         multiply_gw(2, 1, 2, nc.scalar)
+        multiply_gw(1, 1, 5, nc.scalar)
         multiply_gw(3, 0, 7, nc.scalar)
         multiply_gw(3, 1, 6, nc.scalar)

@@ -47,14 +47,14 @@ def tile_attend_gex_wx_kernel(tc, xT, dyT, ts, wm, offs, out_0, out_1):
         offsets = keep.tile([P, B * LIST_COLS], U16, name="offsets")
         ts_sb = held("ts_sb", [P, T], F32)
         dy_sb, wm_sb, x_sb, x_bf, x_g, x_bank, xt_bf, x_q = {}, {}, {}, {}, {}, {}, {}, {}
-        ts_g, dz, dzt_bf, dzt_q, dzn_q, wm_bf, wm_q = {}, {}, {}, {}, {}, {}, {}
+        ts_g, dz, turned, dzt_bf, dzt_q, dzn_q, wm_q, product = {}, {}, {}, {}, {}, {}, {}, {}
 
         ident = keep.tile([P, P], F32, name="ident")
         make_identity(nc, ident[:])
 
         nc.sync.dma_start(out=ts_sb[LAST:, :], in_=ts[LAST:, :])
-        nc.gpsimd.memset(ts_sb[:LAST, : T // 2], 0.0)
-        nc.vector.memset(ts_sb[:LAST, T // 2 :], 0.0)
+        nc.gpsimd.memset(ts_sb[:LAST, : T // 4], 0.0)
+        nc.vector.memset(ts_sb[:LAST, T // 4 :], 0.0)
         nc.sync.dma_start(offsets[:], offs)
 
         windows = []
@@ -70,10 +70,12 @@ def tile_attend_gex_wx_kernel(tc, xT, dyT, ts, wm, offs, out_0, out_1):
             dy_sb[t] = held(f"dy{t}", [P, T], F32)
             nc.sync.dma_start(out=dy_sb[t][:], in_=dyT.rearrange("(p t) c -> t p c", t=PACK)[t])
 
-        def load_wm(b, h):
-            wm_sb[b, h] = held(f"wm{b}{h}", [P, PACK, HALF_D], F32)
+        def load_wm(b, first, count):
+            tile = held(f"wm{b}{first}", [P, PACK, count * P], F32)
             rows = wm[b].rearrange("(p t) d -> p t d", t=PACK)
-            nc.sync.dma_start(out=wm_sb[b, h][:], in_=rows[:, :, h * HALF_D : (h + 1) * HALF_D])
+            nc.sync.dma_start(out=tile[:], in_=rows[:, :, first * P : (first + count) * P])
+            for k in range(count):
+                wm_sb[b, first + k] = tile[:, :, k * P : (k + 1) * P]
 
         def load_x(j):
             x_sb[j] = held(f"x{j}", [P, T], F32)
@@ -92,53 +94,69 @@ def tile_attend_gex_wx_kernel(tc, xT, dyT, ts, wm, offs, out_0, out_1):
                 out=dst.rearrange("p (c i) t -> p c t i", i=LINE), in_=src.rearrange("p t (c i) -> p c t i", i=LINE)
             )
 
+        def scalar_pair(dst, src):
+            nc.scalar.copy(out=dst, in_=src.rearrange("p t i -> p i t"))
+
         def gpsimd_interleave(dst, src):
             nc.gpsimd.tensor_scalar(
                 out=dst, in0=src.rearrange("p t c -> p c t"), scalar1=1.0, scalar2=0.0, op0=MULT, op1=ADD
             )
 
-        def spread_ts(b, pieces, down_bank, across_bank):
-            row = held(f"ts_row{b}", [P, N], F32)
-            down = bank(f"down{b}", [P, N // P, P], down_bank)
-            width = N // pieces
-            for first in range(0, N, width):
-                entries = expert_offsets(b)[:, first // 16 : (first + width) // 16]
-                nc.vector.tensor_copy(row[:, first : first + width], ts_sb[:].indirect(entries))
-                for q in range(first // P, (first + width) // P):
-                    nc.tensor.transpose(down[:, q, :], row[:, q * P : (q + 1) * P], ident[:])
-            cols = held(f"ts_cols{b}", [P, N // P], F32)
+        def ts_down(b, first, width, number):
+            name = f"{b}_{first}"
+            row = held("ts_row" + name, [P, width], F32)
+            entries = expert_offsets(b)[:, first // 16 : (first + width) // 16]
+            nc.vector.tensor_copy(row[:], ts_sb[:].indirect(entries))
+            down = bank("down" + name, [P, width // P, P], number)
+            for q in range(width // P):
+                nc.tensor.transpose(down[:, q, :], row[:, q * P : (q + 1) * P], ident[:])
+            cols = held("ts_cols" + name, [P, width // P], F32)
             nc.scalar.copy(out=cols[:], in_=down[:, :, LAST])
-            across = bank(f"across{b}", [P, N // P, P], across_bank)
-            for q in range(N // P):
+            return cols
+
+        def ts_across(b, first, width, number, cols):
+            across = bank(f"across{b}_{first}", [P, width // P, P], number)
+            for q in range(width // P):
                 nc.tensor.transpose(across[:, q, :], cols[:, q : q + 1].to_broadcast([P, P]), ident[:])
-            ts_g[b] = held(f"ts_g{b}", [P, N], F32)
-            nc.scalar.copy(out=ts_g[b][:], in_=across[:].rearrange("p q s -> p (q s)"))
+            nc.scalar.copy(out=ts_g[b][:, first : first + width], in_=across[:].rearrange("p q s -> p (q s)"))
 
         def gather_dz(t, b):
             nc.vector.tensor_tensor(dz[t, b], dy_sb[t][:].indirect(expert_offsets(b)), ts_g[b][:], MULT)
 
         def turn_dz(t, b, number):
-            copy_out_dz(t, b, turn_planes(t, b, number))
-
-        def turn_planes(t, b, number):
-            turned = bank(f"turned{t}{b}", [P, PACK, P], number)
+            turned[t, b] = bank(f"turned{t}{b}", [P, PACK, P], number)
             for r in range(PACK):
-                nc.tensor.transpose(turned[:, r, :], dz[t, b][:, r:N:PACK], ident[:])
-            return turned
+                nc.tensor.transpose(turned[t, b][:, r, :], dz[t, b][:, r:N:PACK], ident[:])
 
-        def copy_out_dz(t, b, turned):
-            nc.scalar.activation(dzt_bf[b, t // 2][:, t % 2], turned[:].rearrange("s k p -> s p k"), COPY)
+        def copy_out_dz(t, b):
+            nc.scalar.activation(dzt_bf[b, t // 2][:, t % 2], turned[t, b][:].rearrange("s k p -> s p k"), COPY)
 
-        def interleave_wm(b, h, interleave, reuses=None):
-            wm_bf[b, h] = held(f"wm_bf{b}{h}", [P, HALF_D, PACK], BF16, reuses)
-            interleave(wm_bf[b, h][:], wm_sb[b, h][:])
+        HALF = HALF_D * PACK
 
-        def quantize_wm(b, h, reuses=None):
-            wm_q[b, h] = planes(f"wm_q{b}{h}", HALF_D, reuses)
-            quantize(wm_q[b, h], wm_bf[b, h][:].rearrange("p d t -> p (d t)"), E4M3)
+        def as_turned(part):
+            return part.rearrange("s (t p k) -> s t p k", t=2, k=PACK)
 
-        def turned_tile(b, h, reuses=None):
-            dzt_bf[b, h] = held(f"dzt_bf{b}{h}", [P, 2, P, PACK], BF16, reuses)[:]
+        def interleave_wm(part, blocks, interleave):
+            for k, (b, j) in enumerate(blocks):
+                dst = part[:, k * P * PACK : (k + 1) * P * PACK].rearrange("p (d t) -> p d t", t=PACK)
+                interleave(dst, wm_sb[b, j])
+
+        def vector_interleave(dst, src):
+            nc.vector.tensor_copy(
+                out=dst.rearrange("p (c i) t -> p c t i", i=LINE), in_=src.rearrange("p t (c i) -> p c t i", i=LINE)
+            )
+
+        def gpsimd_pair(dst, src):
+            gpsimd_interleave(dst, src)
+
+        def quantize_e4m3(name, part, blocks, x_block=None, reuses=None):
+            width = len(blocks) * P + (0 if x_block is None else B * P)
+            dst = planes(name, width, reuses)
+            quantize(dst, part, E4M3)
+            for k, block in enumerate(blocks):
+                wm_q[block] = dst, slice(k * P, (k + 1) * P)
+            if x_block is not None:
+                x_q[x_block] = dst, len(blocks) * P
 
         def quantize_dzt(b, h):
             cols = slice(h * DV // 2, (h + 1) * DV // 2)
@@ -146,7 +164,7 @@ def tile_attend_gex_wx_kernel(tc, xT, dyT, ts, wm, offs, out_0, out_1):
 
         def quantize_dzn(b, src, reuses=None):
             dzn_q[b] = planes(f"dzn_q{b}", N, reuses)
-            quantize(dzn_q[b], src[:].rearrange("p i t -> p (i t)"), E5M2)
+            quantize(dzn_q[b], src.rearrange("p i t -> p (i t)"), E5M2)
 
         def multiply(out, stationary, cols, moving):
             nc.tensor.matmul_mx(
@@ -159,62 +177,54 @@ def tile_attend_gex_wx_kernel(tc, xT, dyT, ts, wm, offs, out_0, out_1):
                 stop=True,
             )
 
-        def share(k, number, reuses=None):
-            j, b = (k % (BLOCKS - 1), k // (BLOCKS - 1)) if k < B * (BLOCKS - 1) else (BLOCKS - 1, k % B)
-            product = bank(f"dx{k}", [P, N], number)
-            multiply(product, wm_q[b, j // 2], slice((j % 2) * P, (j % 2 + 1) * P), dzn_q[b])
-            dx_sb = held(f"dx_sb{k}", [P, N], F32, reuses)
-            nc.scalar.copy(out=dx_sb[:], in_=product[:])
-            nc.vector.tensor_copy(windows[j][:].indirect(expert_offsets(b)), dx_sb[:])
+        dx_sb = {}
+
+        def multiply_dx(b, j, number):
+            product[b, j] = bank(f"dx{b}{j}", [P, N], number)
+            multiply(product[b, j], *wm_q[b, j], dzn_q[b])
+
+        def copy_out_dx(b, j, reuses=None):
+            dx_sb[b, j] = held(f"dx_sb{b}{j}", [P, N], F32, reuses)
+            nc.scalar.copy(out=dx_sb[b, j][:], in_=product[b, j][:])
+
+        def scatter(b, j):
+            nc.vector.tensor_copy(windows[j][:].indirect(expert_offsets(b)), dx_sb[b, j][:])
             if b == B - 1:
                 nc.sync.dma_start(out=out_1[j * P : (j + 1) * P, :], in_=windows[j][:])
 
-        def cast_x(j, reuses):
+        def cast_x(j, copy, reuses=None):
             x_bf[j] = held(f"x_bf{j}", [P, T], BF16, reuses)
-            nc.scalar.activation(x_bf[j][:], x_sb[j][:], COPY)
+            copy(out=x_bf[j][:], in_=x_sb[j][:])
 
-        def turn_x(j, b):
+        def scalar_cast(out, in_):
+            nc.scalar.activation(out, in_, COPY)
+
+        def gather_x(j, b, number, reuses=None):
+            if b == 0:
+                x_bank[j] = bank(f"x_bank{j}", [P, B, 2, P], number)
+            x_g[j, b] = held(f"x_g{j}{b}", [P, N], BF16, reuses)[:]
+            nc.scalar.activation(x_g[j, b], x_bf[j][:].indirect(expert_offsets(b)), COPY)
             pairs = x_g[j, b].bitcast(F32)
             for u in range(2):
                 nc.tensor.transpose(x_bank[j][:, b, u, :], pairs[:, u:HALF_N:2], ident[:])
 
-        def gather_x(j, number):
-            x_bank[j] = bank(f"x_bank{j}", [P, B, 2, P], number)
-            for b in range(B):
-                x_g[j, b] = held(f"x_g{j}{b}", [P, N], BF16)[:]
-                nc.scalar.activation(x_g[j, b], x_bf[j][:].indirect(expert_offsets(b)), COPY)
-                turn_x(j, b)
-
-        def copy_out_x(j):
-            xt_bf[j] = held(f"xt_bf{j}", [P, B * P * PACK], BF16)
+        def copy_out_x(j, part):
             nc.scalar.copy(
-                out=xt_bf[j][:].bitcast(F32).rearrange("s (b d u) -> s b d u", b=B, u=2),
+                out=part.bitcast(F32).rearrange("s (b d u) -> s b d u", b=B, u=2),
                 in_=x_bank[j][:].rearrange("s b u d -> s b d u"),
             )
 
-        def quantize_x(j, reuses=None):
-            x_q[j] = planes(f"x_q{j}", B * P, reuses)
-            quantize(x_q[j], xt_bf[j][:], E4M3)
+        gw = {}
 
-        def multiply_gw(j, b, number, queue, reuses=None):
-            product = bank(f"gw{j}{b}", [P, DV], number)
-            multiply(product, x_q[j], slice(b * P, (b + 1) * P), dzt_q[b])
+        def multiply_gw(j, b, number):
+            gw[j, b] = bank(f"gw{j}{b}", [P, DV], number)
+            codes, first = x_q[j]
+            multiply(gw[j, b], codes, slice(first + b * P, first + (b + 1) * P), dzt_q[b])
+
+        def store_gw(j, b, reuses=None, queue=nc.sync):
             gw_sb = held(f"gw_sb{j}{b}", [P, P, PACK], F32, reuses)
-            nc.scalar.copy(out=gw_sb[:], in_=product[:].rearrange("d (t p) -> d p t", t=PACK))
+            nc.scalar.copy(out=gw_sb[:], in_=gw[j, b][:].rearrange("d (t p) -> d p t", t=PACK))
             queue.dma_start(out=out_0[b, j * P : (j + 1) * P, :], in_=gw_sb[:].rearrange("d p t -> d (p t)"))
-
-        load_x(0)
-        load_dy(0)
-        load_dy(1)
-        load_wm(0, 0)
-        load_dy(2)
-        load_dy(3)
-        load_wm(0, 1)
-        load_wm(1, 0)
-        load_x(1)
-        load_wm(1, 1)
-        load_x(2)
-        load_x(3)
 
         def pair_tile(b, h, reuses=None):
             pair = held(f"dz{b}{h}", [P, 2, N], F32, reuses)
@@ -222,100 +232,146 @@ def tile_attend_gex_wx_kernel(tc, xT, dyT, ts, wm, offs, out_0, out_1):
                 dz[2 * h + e, b] = pair[:, e, :]
             return pair
 
-        def interleave_pair(interleave, dst, h, pair):
-            interleave(dst[:, :, 2 * h : 2 * h + 2], pair[:])
+        for t in range(PACK):
+            load_dy(t)
+        load_wm(0, 0, 2)
+        load_x(0)
+        load_wm(0, 2, 2)
+        load_wm(1, 0, 1)
+        load_x(1)
+        load_wm(1, 1, 1)
+        load_wm(1, 2, 2)
+        load_x(2)
+        load_x(3)
 
-        def scalar_pair(dst, src):
-            nc.scalar.copy(out=dst, in_=src.rearrange("p t i -> p i t"))
+        for b in range(B):
+            ts_g[b] = held(f"ts_g{b}", [P, N], F32)
+        cols = [ts_down(0, h * HALF_N, HALF_N, h) for h in range(2)]
+        for h in range(2):
+            ts_across(0, h * HALF_N, HALF_N, 2 + h, cols[h])
+        ts_across(1, 0, N, 5, ts_down(1, 0, N, 1))
 
         pairs = {(b, 0): pair_tile(b, 0) for b in range(B)}
+        dzt_bf[0, 0] = as_turned(held("dzt_bf00", [P, HALF], BF16)[:])
+        dzt_bf1 = held("dzt_bf1", [P, 2 * HALF], BF16)
+        for h in range(2):
+            dzt_bf[1, h] = as_turned(dzt_bf1[:, h * HALF : (h + 1) * HALF])
+        dzn_bf0 = held("dzn_bf0", [P, N, PACK], BF16, reuses="ts_cols1_0")
+        dzt_q[0] = planes("dzt_q0", DV)
 
-        spread_ts(0, 2, 0, 1)
-        spread_ts(1, 1, 0, 3)
-        x_g0 = held("x_g0", [P, B * N], BF16)
-        x_bank[0] = bank("x_bank0", [P, B, 2, P], 0)
-        nc.vector.tensor_copy(x_g0[:], x_sb[0][:].indirect(offsets[:]))
-        for b in range(B):
-            x_g[0, b] = x_g0[:, b * N : (b + 1) * N]
-            turn_x(0, b)
-        copy_out_x(0)
-        interleave_wm(0, 0, scalar_interleave, reuses="x_g0")
-        first_turned = held("first_turned", [P, B, 2, P, PACK], BF16)
-        for b in range(B):
-            dzt_bf[b, 0] = first_turned[:, b]
         gather_dz(0, 0)
-        turn_dz(0, 0, 4)
-        gather_dz(0, 1)
-        turn_dz(0, 1, 5)
+        turn_dz(0, 0, 1)
+        copy_out_dz(0, 0)
         gather_dz(1, 0)
-        dzn_bf0 = held("dzn_bf0", [P, N, PACK], BF16, reuses="wm00")
-        interleave_pair(scalar_pair, dzn_bf0, 0, pairs[0, 0])
-        turn_dz(1, 0, 6)
-        gather_dz(1, 1)
-        turn_dz(1, 1, 7)
-        quantize_x(0)
-        quantize_wm(0, 0)
+        scalar_pair(dzn_bf0[:, :, 0:2], pairs[0, 0][:])
+        turn_dz(1, 0, 7)
+        copy_out_dz(1, 0)
+        for t in range(2):
+            gather_dz(t, 1)
+            turn_dz(t, 1, 6 * t)
+            copy_out_dz(t, 1)
         pairs[0, 1] = pair_tile(0, 1, reuses="dy0")
         gather_dz(2, 0)
-        turned20 = turn_planes(2, 0, 1)
         gather_dz(3, 0)
-        interleave_pair(scalar_pair, dzn_bf0, 1, pairs[0, 1])
-        turned30 = turn_planes(3, 0, 2)
+        scalar_pair(dzn_bf0[:, :, 2:4], pairs[0, 1][:])
+        turn_dz(2, 0, 2)
+        turn_dz(3, 0, 3)
+        quantize_dzt(0, 0)
         pairs[1, 1] = pair_tile(1, 1, reuses="ts_g0")
         gather_dz(2, 1)
-        interleave_wm(0, 1, scalar_interleave, reuses="dy2")
-        turned_tile(0, 1, reuses="dz01")
-        copy_out_dz(2, 0, turned20)
-        copy_out_dz(3, 0, turned30)
+        stage0 = held("stage0", [P, 3 * P * PACK + HALF], BF16, reuses="dy2")
+        wm_a, wm_b = stage0[:, : P * PACK], stage0[:, P * PACK : 3 * P * PACK]
+        dzt_bf[0, 1] = as_turned(stage0[:, 3 * P * PACK :])
+        interleave_wm(wm_a, [(0, 0)], vector_interleave)
+        quantize_e4m3("wm_a_q", wm_a, [(0, 0)])
+        quantize_dzn(0, dzn_bf0[:])
+        multiply_dx(0, 0, 4)
         gather_dz(3, 1)
-        quantize_dzn(0, dzn_bf0)
-        dzt_q[0] = planes("dzt_q0", DV, reuses="wm01")
-        dzt_q[1] = planes("dzt_q1", DV, reuses="dzn_bf0")
-        quantize_dzt(0, 0)
-        quantize_dzt(1, 0)
-        quantize_wm(0, 1)
+        interleave_wm(wm_b[:, : P * PACK], [(0, 1)], scalar_interleave)
+        copy_out_dz(2, 0)
+        interleave_wm(wm_b[:, P * PACK :], [(0, 2)], scalar_interleave)
+        copy_out_dz(3, 0)
+        turn_dz(2, 1, 6)
+        copy_out_dz(2, 1)
+        copy_out_dx(0, 0)
+        cast_x(0, nc.vector.tensor_copy, reuses="dz01")
+        quantize_e4m3("wm_b_q", wm_b, [(0, 1), (0, 2)])
         quantize_dzt(0, 1)
+        multiply_dx(0, 1, 5)
+        multiply_dx(0, 2, 2)
 
-        interleave_wm(1, 0, gpsimd_interleave, reuses="dzt_bf01")
-        dzn_bf1 = held("dzn_bf1", [P, N, PACK], BF16, reuses="wm10")
+        scatter(0, 0)
+        stage1 = held("stage1", [P, P * PACK + N * PACK], BF16, reuses="stage0")
+        wm_c = stage1[:, : P * PACK]
+        dzn_bf1 = stage1[:, P * PACK :].rearrange("p (i t) -> p i t", t=PACK)
         for h in range(2):
-            interleave_pair(gpsimd_interleave, dzn_bf1, h, pairs[1, h])
-        share(0, 5)
-        share(1, 6)
-
-        cast_x(1, reuses="wm_q00_codes")
-        turned_tile(1, 1, reuses="x1")
-        turn_dz(2, 1, 5)
-        turn_dz(3, 1, 6)
-        quantize_dzt(1, 1)
+            gpsimd_pair(dzn_bf1[:, :, 2 * h : 2 * h + 2], pairs[1, h][:])
+        interleave_wm(wm_c, [(1, 0)], gpsimd_interleave)
+        copy_out_dx(0, 1)
+        gather_x(0, 0, 0)
+        gather_x(0, 1, 0)
+        scatter(0, 1)
+        cast_x(1, scalar_cast, reuses="x_g00")
+        gather_x(1, 0, 1)
+        copy_out_dx(0, 2, reuses="wm10")
+        turn_dz(3, 1, 2)
+        gather_x(1, 1, 1)
         quantize_dzn(1, dzn_bf1)
-        gather_x(1, 1)
-        quantize_wm(1, 0, reuses="x_g10")
-        share(2, 0, reuses="x_bf1")
-        copy_out_x(1)
-        quantize_x(1)
-        interleave_wm(1, 1, gpsimd_interleave, reuses="xt_bf1")
+        quantize_e4m3("wm_c_q", wm_c, [(1, 0)])
+        multiply_dx(1, 0, 3)
 
-        cast_x(2, reuses="x_g11")
-        share(3, 0, reuses="x2")
-        gather_x(2, 4)
-        quantize_wm(1, 1, reuses="x_g20")
-        multiply_gw(0, 0, 2, nc.sync, reuses="x_bf2")
-        copy_out_x(2)
-        quantize_x(2)
-        share(4, 0, reuses="x_g21")
-        multiply_gw(0, 1, 2, nc.sync)
-        multiply_gw(1, 0, 4, nc.sync)
-        share(5, 0)
+        scatter(0, 2)
+        stage2 = held("stage2", [P, 2 * HALF], BF16, reuses="stage1")
+        interleave_wm(stage2[:, :HALF], [(1, 2), (1, 1)], gpsimd_interleave)
+        copy_out_x(0, stage2[:, HALF:])
+        copy_out_dz(3, 1)
+        copy_out_dx(1, 0, reuses="wm11")
+        cast_x(2, scalar_cast, reuses="x_bf1")
+        quantize_e4m3("q_d", stage2[:], [(1, 2), (1, 1)], 0)
+        multiply_dx(1, 1, 4)
+        multiply_dx(1, 2, 5)
 
-        cast_x(3, reuses="x_q0_codes")
-        share(6, 4, reuses="x3")
-        gather_x(3, 5)
-        multiply_gw(2, 0, 2, nc.sync, reuses="x_bf3")
-        copy_out_x(3)
-        quantize_x(3)
-        share(7, 0, reuses="x_g31")
-        multiply_gw(2, 1, 2, nc.scalar)
-        multiply_gw(1, 1, 5, nc.scalar)
-        multiply_gw(3, 0, 7, nc.scalar)
-        multiply_gw(3, 1, 6, nc.scalar)
+        scatter(1, 0)
+        stage3 = held("stage3", [P, 2 * HALF], BF16, reuses="stage2")
+        interleave_wm(stage3[:, :HALF], [(0, 3), (1, 3)], gpsimd_interleave)
+        copy_out_x(1, stage3[:, HALF:])
+        gather_x(2, 0, 2)
+        copy_out_dx(1, 1, reuses="wm12")
+        gather_x(2, 1, 2)
+        quantize_e4m3("q_e", stage3[:], [(0, 3), (1, 3)], 1)
+        dzt_q[1] = planes("dzt_q1", DV, reuses="dx_sb10")
+        quantize(dzt_q[1], dzt_bf1[:], E5M2)
+        multiply_gw(0, 0, 6)
+        store_gw(0, 0, reuses="x_bf2")
+
+        scatter(1, 1)
+        xt_bf2 = held("xt_bf2", [P, HALF], BF16)
+        copy_out_x(2, xt_bf2[:])
+        copy_out_dx(1, 2, reuses="x_g21")
+        quantize_e4m3("q_x2", xt_bf2[:], [], 2)
+        multiply_dx(0, 3, 6)
+        multiply_gw(0, 1, 2)
+        scatter(1, 2)
+        copy_out_dx(0, 3)
+        cast_x(3, scalar_cast, reuses="q_d_codes")
+        gather_x(3, 0, 0)
+        gather_x(3, 1, 0)
+        multiply_dx(1, 3, 5)
+        multiply_gw(1, 1, 6)
+        store_gw(0, 1, reuses="x_bf3")
+        multiply_gw(1, 0, 2)
+        scatter(0, 3)
+        xt_bf3 = held("xt_bf3", [P, HALF], BF16)
+        copy_out_x(3, xt_bf3[:])
+        store_gw(1, 1)
+        store_gw(1, 0)
+        copy_out_dx(1, 3, reuses="x_g31")
+        quantize_e4m3("q_x3", xt_bf3[:], [], 3)
+        multiply_gw(2, 0, 3)
+        multiply_gw(2, 1, 7)
+        multiply_gw(3, 0, 1)
+        multiply_gw(3, 1, 0)
+        for j in (2, 3):
+            for b in range(B):
+                store_gw(j, b, queue=nc.scalar)
+        scatter(1, 3)

@@ -76,6 +76,7 @@ def tile_attend_gex_wx_kernel(tc, xT, dyT, ts, wm, offs, out_0, out_1):
             nc.sync.dma_start(out=tile[:], in_=rows[:, :, first * P : (first + count) * P])
             for k in range(count):
                 wm_sb[b, first + k] = tile[:, :, k * P : (k + 1) * P]
+            return tile[:]
 
         def load_x(j):
             x_sb[j] = held(f"x{j}", [P, T], F32)
@@ -120,8 +121,10 @@ def tile_attend_gex_wx_kernel(tc, xT, dyT, ts, wm, offs, out_0, out_1):
                 nc.tensor.transpose(across[:, q, :], cols[:, q : q + 1].to_broadcast([P, P]), ident[:])
             nc.scalar.copy(out=ts_g[b][:, first : first + width], in_=across[:].rearrange("p q s -> p (q s)"))
 
-        def gather_dz(t, b):
-            nc.vector.tensor_tensor(dz[t, b], dy_sb[t][:].indirect(expert_offsets(b)), ts_g[b][:], MULT)
+        def gather_dz(t, b, first=0, width=N):
+            entries = expert_offsets(b)[:, first // 16 : (first + width) // 16]
+            slots = slice(first, first + width)
+            nc.vector.tensor_tensor(dz[t, b][:, slots], dy_sb[t][:].indirect(entries), ts_g[b][:, slots], MULT)
 
         def turn_dz(t, b, number):
             turned[t, b] = bank(f"turned{t}{b}", [P, PACK, P], number)
@@ -192,9 +195,10 @@ def tile_attend_gex_wx_kernel(tc, xT, dyT, ts, wm, offs, out_0, out_1):
             if b == B - 1:
                 nc.sync.dma_start(out=out_1[j * P : (j + 1) * P, :], in_=windows[j][:])
 
-        def cast_x(j, copy, reuses=None):
-            x_bf[j] = held(f"x_bf{j}", [P, T], BF16, reuses)
-            copy(out=x_bf[j][:], in_=x_sb[j][:])
+        def cast_x(j, copy, reuses=None, cols=slice(0, T)):
+            if cols.start == 0:
+                x_bf[j] = held(f"x_bf{j}", [P, T], BF16, reuses)
+            copy(out=x_bf[j][:, cols], in_=x_sb[j][:, cols])
 
         def scalar_cast(out, in_):
             nc.scalar.activation(out, in_, COPY)
@@ -246,55 +250,59 @@ def tile_attend_gex_wx_kernel(tc, xT, dyT, ts, wm, offs, out_0, out_1):
 
         for b in range(B):
             ts_g[b] = held(f"ts_g{b}", [P, N], F32)
-        cols = [ts_down(0, h * HALF_N, HALF_N, h) for h in range(2)]
-        for h in range(2):
-            ts_across(0, h * HALF_N, HALF_N, 2 + h, cols[h])
-        ts_across(1, 0, N, 5, ts_down(1, 0, N, 1))
+        halves = [(b, h * HALF_N) for b in range(B) for h in range(2)]
+        cols = ts_down(*halves[0], HALF_N, 0)
+        for k, (b, first) in enumerate(halves):
+            ahead = ts_down(*halves[k + 1], HALF_N, (k + 1) % 2) if k + 1 < len(halves) else None
+            ts_across(b, first, HALF_N, 2 + k, cols)
+            cols = ahead
 
-        pairs = {(b, 0): pair_tile(b, 0) for b in range(B)}
+        pairs = {(b, 0): pair_tile(b, 0)[:] for b in range(B)}
         dzt_bf[0, 0] = as_turned(held("dzt_bf00", [P, HALF], BF16)[:])
         dzt_bf1 = held("dzt_bf1", [P, 2 * HALF], BF16)
         for h in range(2):
             dzt_bf[1, h] = as_turned(dzt_bf1[:, h * HALF : (h + 1) * HALF])
-        dzn_bf0 = held("dzn_bf0", [P, N, PACK], BF16, reuses="ts_cols1_0")
+        dzn_bf0 = held("dzn_bf0", [P, N, PACK], BF16, reuses="ts_cols1_256")
         dzt_q[0] = planes("dzt_q0", DV)
 
-        gather_dz(0, 0)
+        for first in (0, HALF_N):
+            gather_dz(0, 0, first, HALF_N)
         turn_dz(0, 0, 1)
         copy_out_dz(0, 0)
         gather_dz(1, 0)
-        scalar_pair(dzn_bf0[:, :, 0:2], pairs[0, 0][:])
+        scalar_pair(dzn_bf0[:, :, 0:2], pairs[0, 0])
         turn_dz(1, 0, 7)
         copy_out_dz(1, 0)
         for t in range(2):
             gather_dz(t, 1)
             turn_dz(t, 1, 6 * t)
             copy_out_dz(t, 1)
-        pairs[0, 1] = pair_tile(0, 1, reuses="dy0")
+        late = held("late", [P, 3, N], F32, reuses="dy0")
+        dz[2, 0], dz[3, 0], dz[2, 1], dz[3, 1] = late[:, 0, :], late[:, 1, :], late[:, 1, :], late[:, 2, :]
+        pairs[0, 1], pairs[1, 1] = late[:, 0:2, :], late[:, 1:3, :]
         gather_dz(2, 0)
         gather_dz(3, 0)
-        scalar_pair(dzn_bf0[:, :, 2:4], pairs[0, 1][:])
+        scalar_pair(dzn_bf0[:, :, 2:4], pairs[0, 1])
         turn_dz(2, 0, 2)
         turn_dz(3, 0, 3)
+        gather_dz(3, 1)
+        turn_dz(3, 1, 6)
         quantize_dzt(0, 0)
-        pairs[1, 1] = pair_tile(1, 1, reuses="ts_g0")
-        gather_dz(2, 1)
-        stage0 = held("stage0", [P, 3 * P * PACK + HALF], BF16, reuses="dy2")
+        stage0 = held("stage0", [P, 3 * P * PACK + HALF], BF16, reuses="dy3")
         wm_a, wm_b = stage0[:, : P * PACK], stage0[:, P * PACK : 3 * P * PACK]
         dzt_bf[0, 1] = as_turned(stage0[:, 3 * P * PACK :])
         interleave_wm(wm_a, [(0, 0)], vector_interleave)
         quantize_e4m3("wm_a_q", wm_a, [(0, 0)])
         quantize_dzn(0, dzn_bf0[:])
         multiply_dx(0, 0, 4)
-        gather_dz(3, 1)
+        gather_dz(2, 1)
         interleave_wm(wm_b[:, : P * PACK], [(0, 1)], scalar_interleave)
         copy_out_dz(2, 0)
         interleave_wm(wm_b[:, P * PACK :], [(0, 2)], scalar_interleave)
         copy_out_dz(3, 0)
-        turn_dz(2, 1, 6)
-        copy_out_dz(2, 1)
+        copy_out_dz(3, 1)
         copy_out_dx(0, 0)
-        cast_x(0, nc.vector.tensor_copy, reuses="dz01")
+        cast_x(0, nc.vector.tensor_copy, reuses="dzn_bf0")
         quantize_e4m3("wm_b_q", wm_b, [(0, 1), (0, 2)])
         quantize_dzt(0, 1)
         multiply_dx(0, 1, 5)
@@ -305,28 +313,29 @@ def tile_attend_gex_wx_kernel(tc, xT, dyT, ts, wm, offs, out_0, out_1):
         wm_c = stage1[:, : P * PACK]
         dzn_bf1 = stage1[:, P * PACK :].rearrange("p (i t) -> p i t", t=PACK)
         for h in range(2):
-            gpsimd_pair(dzn_bf1[:, :, 2 * h : 2 * h + 2], pairs[1, h][:])
+            gpsimd_pair(dzn_bf1[:, :, 2 * h : 2 * h + 2], pairs[1, h])
         interleave_wm(wm_c, [(1, 0)], gpsimd_interleave)
-        copy_out_dx(0, 1)
         gather_x(0, 0, 0)
+        copy_out_dx(0, 1)
         gather_x(0, 1, 0)
         scatter(0, 1)
-        cast_x(1, scalar_cast, reuses="x_g00")
+        cast_x(1, scalar_cast, reuses="wm_b_q_codes")
         gather_x(1, 0, 1)
         copy_out_dx(0, 2, reuses="wm10")
-        turn_dz(3, 1, 2)
+        turn_dz(2, 1, 2)
         gather_x(1, 1, 1)
         quantize_dzn(1, dzn_bf1)
         quantize_e4m3("wm_c_q", wm_c, [(1, 0)])
-        multiply_dx(1, 0, 3)
 
         scatter(0, 2)
         stage2 = held("stage2", [P, 2 * HALF], BF16, reuses="stage1")
         interleave_wm(stage2[:, :HALF], [(1, 2), (1, 1)], gpsimd_interleave)
         copy_out_x(0, stage2[:, HALF:])
-        copy_out_dz(3, 1)
+        multiply_dx(1, 0, 0)
+        copy_out_dz(2, 1)
+        cast_x(2, scalar_cast, reuses="x_bf1", cols=slice(0, T // 2))
         copy_out_dx(1, 0, reuses="wm11")
-        cast_x(2, scalar_cast, reuses="x_bf1")
+        cast_x(2, scalar_cast, cols=slice(T // 2, T))
         quantize_e4m3("q_d", stage2[:], [(1, 2), (1, 1)], 0)
         multiply_dx(1, 1, 4)
         multiply_dx(1, 2, 5)
@@ -339,7 +348,7 @@ def tile_attend_gex_wx_kernel(tc, xT, dyT, ts, wm, offs, out_0, out_1):
         copy_out_dx(1, 1, reuses="wm12")
         gather_x(2, 1, 2)
         quantize_e4m3("q_e", stage3[:], [(0, 3), (1, 3)], 1)
-        dzt_q[1] = planes("dzt_q1", DV, reuses="dx_sb10")
+        dzt_q[1] = planes("dzt_q1", DV, reuses="x_g20")
         quantize(dzt_q[1], dzt_bf1[:], E5M2)
         multiply_gw(0, 0, 6)
         store_gw(0, 0, reuses="x_bf2")
@@ -354,24 +363,24 @@ def tile_attend_gex_wx_kernel(tc, xT, dyT, ts, wm, offs, out_0, out_1):
         scatter(1, 2)
         copy_out_dx(0, 3)
         cast_x(3, scalar_cast, reuses="q_d_codes")
-        gather_x(3, 0, 0)
-        gather_x(3, 1, 0)
-        multiply_dx(1, 3, 5)
+        multiply_gw(1, 0, 5)
         multiply_gw(1, 1, 6)
-        store_gw(0, 1, reuses="x_bf3")
-        multiply_gw(1, 0, 2)
+        store_gw(0, 1, reuses="x3")
+        multiply_gw(2, 1, 2)
+        gather_x(3, 0, 3)
+        gather_x(3, 1, 3)
+        store_gw(1, 1, reuses="x_bf3")
+        store_gw(1, 0, reuses="x_g30")
+        multiply_gw(2, 0, 6)
+        multiply_dx(1, 3, 5)
         scatter(0, 3)
         xt_bf3 = held("xt_bf3", [P, HALF], BF16)
         copy_out_x(3, xt_bf3[:])
-        store_gw(1, 1)
-        store_gw(1, 0)
-        copy_out_dx(1, 3, reuses="x_g31")
         quantize_e4m3("q_x3", xt_bf3[:], [], 3)
-        multiply_gw(2, 0, 3)
-        multiply_gw(2, 1, 7)
+        store_gw(2, 1, reuses="x_g31")
+        copy_out_dx(1, 3)
         multiply_gw(3, 0, 1)
-        multiply_gw(3, 1, 0)
-        for j in (2, 3):
-            for b in range(B):
-                store_gw(j, b, queue=nc.scalar)
+        multiply_gw(3, 1, 4)
+        for j, b in ((2, 0), (3, 0), (3, 1)):
+            store_gw(j, b, queue=nc.scalar)
         scatter(1, 3)

@@ -78,9 +78,11 @@ def tile_attend_gex_wx_kernel(tc, xT, dyT, ts, wm, offs, out_0, out_1):
                 wm_sb[b, first + k] = tile[:, :, k * P : (k + 1) * P]
             return tile[:]
 
-        def load_x(j):
+        def load_x(j, pieces=1):
             x_sb[j] = held(f"x{j}", [P, T], F32)
-            nc.sync.dma_start(out=x_sb[j][:], in_=xT[j * P : (j + 1) * P, :])
+            for first in range(0, T, T // pieces):
+                cols = slice(first, first + T // pieces)
+                nc.sync.dma_start(out=x_sb[j][:, cols], in_=xT[j * P : (j + 1) * P, cols])
 
         def planes(name, width, reuses=None):
             codes = held(name + "_codes", [P, width], U32, reuses)
@@ -203,14 +205,16 @@ def tile_attend_gex_wx_kernel(tc, xT, dyT, ts, wm, offs, out_0, out_1):
         def scalar_cast(out, in_):
             nc.scalar.activation(out, in_, COPY)
 
-        def gather_x(j, b, number, reuses=None):
-            if b == 0:
+        def gather_x(j, experts, number, reuses=None):
+            if experts[0] == 0:
                 x_bank[j] = bank(f"x_bank{j}", [P, B, 2, P], number)
-            x_g[j, b] = held(f"x_g{j}{b}", [P, N], BF16, reuses)[:]
-            nc.scalar.activation(x_g[j, b], x_bf[j][:].indirect(expert_offsets(b)), COPY)
-            pairs = x_g[j, b].bitcast(F32)
-            for u in range(2):
-                nc.tensor.transpose(x_bank[j][:, b, u, :], pairs[:, u:HALF_N:2], ident[:])
+            picked = held(f"x_g{j}{experts[0]}", [P, len(experts) * N], BF16, reuses)
+            entries = offsets[:, experts[0] * LIST_COLS : (experts[-1] + 1) * LIST_COLS]
+            nc.scalar.activation(picked[:], x_bf[j][:].indirect(entries), COPY)
+            words = picked[:].bitcast(F32)
+            for k, b in enumerate(experts):
+                for u in range(2):
+                    nc.tensor.transpose(x_bank[j][:, b, u, :], words[:, k * HALF_N + u : (k + 1) * HALF_N : 2], ident[:])
 
         def copy_out_x(j, part):
             nc.scalar.copy(
@@ -238,13 +242,14 @@ def tile_attend_gex_wx_kernel(tc, xT, dyT, ts, wm, offs, out_0, out_1):
 
         for t in range(PACK):
             load_dy(t)
-        load_wm(0, 0, 2)
-        load_x(0)
-        load_wm(0, 2, 2)
+        load_wm(0, 0, 1)
+        load_x(0, pieces=2)
+        wm_next = load_wm(0, 1, 2)
         load_wm(1, 0, 1)
         load_x(1)
         load_wm(1, 1, 1)
         load_wm(1, 2, 2)
+        load_wm(0, 3, 1)
         load_x(2)
         load_x(3)
 
@@ -265,6 +270,8 @@ def tile_attend_gex_wx_kernel(tc, xT, dyT, ts, wm, offs, out_0, out_1):
         dzn_bf0 = held("dzn_bf0", [P, N, PACK], BF16, reuses="ts_cols1_256")
         dzt_q[0] = planes("dzt_q0", DV)
 
+        plain = held("plain", [P, N], F32)
+        nc.vector.tensor_copy(plain[:], dy_sb[0][:].indirect(expert_offsets(1)))
         for first in (0, HALF_N):
             gather_dz(0, 0, first, HALF_N)
         turn_dz(0, 0, 1)
@@ -273,11 +280,12 @@ def tile_attend_gex_wx_kernel(tc, xT, dyT, ts, wm, offs, out_0, out_1):
         scalar_pair(dzn_bf0[:, :, 0:2], pairs[0, 0])
         turn_dz(1, 0, 7)
         copy_out_dz(1, 0)
+        nc.vector.tensor_tensor(dz[0, 1], plain[:], ts_g[1][:], MULT)
+        gather_dz(1, 1)
         for t in range(2):
-            gather_dz(t, 1)
             turn_dz(t, 1, 6 * t)
             copy_out_dz(t, 1)
-        late = held("late", [P, 3, N], F32, reuses="dy0")
+        late = held("late", [P, 3, N], F32, reuses="plain")
         dz[2, 0], dz[3, 0], dz[2, 1], dz[3, 1] = late[:, 0, :], late[:, 1, :], late[:, 1, :], late[:, 2, :]
         pairs[0, 1], pairs[1, 1] = late[:, 0:2, :], late[:, 1:3, :]
         gather_dz(2, 0)
@@ -287,24 +295,25 @@ def tile_attend_gex_wx_kernel(tc, xT, dyT, ts, wm, offs, out_0, out_1):
         turn_dz(3, 0, 3)
         gather_dz(3, 1)
         turn_dz(3, 1, 6)
-        quantize_dzt(0, 0)
-        stage0 = held("stage0", [P, 3 * P * PACK + HALF], BF16, reuses="dy3")
-        wm_a, wm_b = stage0[:, : P * PACK], stage0[:, P * PACK : 3 * P * PACK]
-        dzt_bf[0, 1] = as_turned(stage0[:, 3 * P * PACK :])
+        cast_x(0, nc.vector.tensor_copy, reuses="ts_g0", cols=slice(0, T // 2))
+        wm_a = held("wm_a", [P, P * PACK], BF16, reuses="dy3")[:]
         interleave_wm(wm_a, [(0, 0)], vector_interleave)
+        quantize_dzt(0, 0)
         quantize_e4m3("wm_a_q", wm_a, [(0, 0)])
         quantize_dzn(0, dzn_bf0[:])
         multiply_dx(0, 0, 4)
         gather_dz(2, 1)
-        interleave_wm(wm_b[:, : P * PACK], [(0, 1)], scalar_interleave)
+        stage0 = held("stage0", [P, 2 * HALF], BF16, reuses="dzn_bf0")
+        wm_b = stage0[:, :HALF]
+        dzt_bf[0, 1] = as_turned(stage0[:, HALF:])
+        vector_interleave(wm_b.rearrange("p (d t) -> p d t", t=PACK), wm_next)
+        cast_x(0, scalar_cast, cols=slice(T // 2, T))
         copy_out_dz(2, 0)
-        interleave_wm(wm_b[:, P * PACK :], [(0, 2)], scalar_interleave)
         copy_out_dz(3, 0)
         copy_out_dz(3, 1)
         copy_out_dx(0, 0)
-        cast_x(0, nc.vector.tensor_copy, reuses="dzn_bf0")
-        quantize_e4m3("wm_b_q", wm_b, [(0, 1), (0, 2)])
         quantize_dzt(0, 1)
+        quantize_e4m3("wm_b_q", wm_b, [(0, 1), (0, 2)])
         multiply_dx(0, 1, 5)
         multiply_dx(0, 2, 2)
 
@@ -315,24 +324,23 @@ def tile_attend_gex_wx_kernel(tc, xT, dyT, ts, wm, offs, out_0, out_1):
         for h in range(2):
             gpsimd_pair(dzn_bf1[:, :, 2 * h : 2 * h + 2], pairs[1, h])
         interleave_wm(wm_c, [(1, 0)], gpsimd_interleave)
-        gather_x(0, 0, 0)
+        turn_dz(2, 1, 4)
+        gather_x(0, [0, 1], 0, reuses="wm_a_q_codes")
         copy_out_dx(0, 1)
-        gather_x(0, 1, 0)
         scatter(0, 1)
         cast_x(1, scalar_cast, reuses="wm_b_q_codes")
-        gather_x(1, 0, 1)
+        copy_out_dz(2, 1)
         copy_out_dx(0, 2, reuses="wm10")
-        turn_dz(2, 1, 2)
-        gather_x(1, 1, 1)
+        gather_x(1, [0], 1)
+        gather_x(1, [1], 1)
         quantize_dzn(1, dzn_bf1)
         quantize_e4m3("wm_c_q", wm_c, [(1, 0)])
+        multiply_dx(1, 0, 3)
 
         scatter(0, 2)
         stage2 = held("stage2", [P, 2 * HALF], BF16, reuses="stage1")
         interleave_wm(stage2[:, :HALF], [(1, 2), (1, 1)], gpsimd_interleave)
         copy_out_x(0, stage2[:, HALF:])
-        multiply_dx(1, 0, 0)
-        copy_out_dz(2, 1)
         cast_x(2, scalar_cast, reuses="x_bf1", cols=slice(0, T // 2))
         copy_out_dx(1, 0, reuses="wm11")
         cast_x(2, scalar_cast, cols=slice(T // 2, T))
@@ -344,9 +352,9 @@ def tile_attend_gex_wx_kernel(tc, xT, dyT, ts, wm, offs, out_0, out_1):
         stage3 = held("stage3", [P, 2 * HALF], BF16, reuses="stage2")
         interleave_wm(stage3[:, :HALF], [(0, 3), (1, 3)], gpsimd_interleave)
         copy_out_x(1, stage3[:, HALF:])
-        gather_x(2, 0, 2)
+        gather_x(2, [0], 2)
+        gather_x(2, [1], 2)
         copy_out_dx(1, 1, reuses="wm12")
-        gather_x(2, 1, 2)
         quantize_e4m3("q_e", stage3[:], [(0, 3), (1, 3)], 1)
         dzt_q[1] = planes("dzt_q1", DV, reuses="x_g20")
         quantize(dzt_q[1], dzt_bf1[:], E5M2)
@@ -358,7 +366,7 @@ def tile_attend_gex_wx_kernel(tc, xT, dyT, ts, wm, offs, out_0, out_1):
         copy_out_x(2, xt_bf2[:])
         copy_out_dx(1, 2, reuses="x_g21")
         quantize_e4m3("q_x2", xt_bf2[:], [], 2)
-        multiply_dx(0, 3, 6)
+        multiply_dx(0, 3, 4)
         multiply_gw(0, 1, 2)
         scatter(1, 2)
         copy_out_dx(0, 3)
@@ -366,21 +374,21 @@ def tile_attend_gex_wx_kernel(tc, xT, dyT, ts, wm, offs, out_0, out_1):
         multiply_gw(1, 0, 5)
         multiply_gw(1, 1, 6)
         store_gw(0, 1, reuses="x3")
-        multiply_gw(2, 1, 2)
-        gather_x(3, 0, 3)
-        gather_x(3, 1, 3)
+        multiply_dx(1, 3, 2)
+        gather_x(3, [0], 0)
+        gather_x(3, [1], 0)
         store_gw(1, 1, reuses="x_bf3")
         store_gw(1, 0, reuses="x_g30")
-        multiply_gw(2, 0, 6)
-        multiply_dx(1, 3, 5)
+        multiply_gw(2, 0, 5)
+        multiply_gw(2, 1, 6)
         scatter(0, 3)
         xt_bf3 = held("xt_bf3", [P, HALF], BF16)
         copy_out_x(3, xt_bf3[:])
         quantize_e4m3("q_x3", xt_bf3[:], [], 3)
-        store_gw(2, 1, reuses="x_g31")
-        copy_out_dx(1, 3)
+        copy_out_dx(1, 3, reuses="x_g31")
         multiply_gw(3, 0, 1)
         multiply_gw(3, 1, 4)
-        for j, b in ((2, 0), (3, 0), (3, 1)):
-            store_gw(j, b, queue=nc.scalar)
+        for j in (2, 3):
+            for b in range(B):
+                store_gw(j, b, queue=nc.scalar)
         scatter(1, 3)

@@ -296,37 +296,37 @@ def tile_attend_gex_wx_kernel(tc, xT, dyT, ts, wm, offs, out_0, out_1):
         gather_dz(3, 1)
         turn_dz(3, 1, 6)
         cast_x(0, nc.vector.tensor_copy, reuses="ts_g0", cols=slice(0, T // 2))
-        wm_a = held("wm_a", [P, P * PACK], BF16, reuses="dy3")[:]
+        stage0 = held("stage0", [P, P * PACK + HALF], BF16, reuses="dy3")
+        wm_a = stage0[:, : P * PACK]
+        dzt_bf[0, 1] = as_turned(stage0[:, P * PACK :])
         interleave_wm(wm_a, [(0, 0)], vector_interleave)
         quantize_dzt(0, 0)
         quantize_e4m3("wm_a_q", wm_a, [(0, 0)])
         quantize_dzn(0, dzn_bf0[:])
         multiply_dx(0, 0, 4)
         gather_dz(2, 1)
-        stage0 = held("stage0", [P, 2 * HALF], BF16, reuses="dzn_bf0")
-        wm_b = stage0[:, :HALF]
-        dzt_bf[0, 1] = as_turned(stage0[:, HALF:])
+        wm_b = held("wm_b", [P, HALF], BF16, reuses="dzn_bf0")[:]
         vector_interleave(wm_b.rearrange("p (d t) -> p d t", t=PACK), wm_next)
-        cast_x(0, scalar_cast, cols=slice(T // 2, T))
         copy_out_dz(2, 0)
         copy_out_dz(3, 0)
-        copy_out_dz(3, 1)
+        cast_x(0, scalar_cast, cols=slice(T // 2, T))
         copy_out_dx(0, 0)
+        copy_out_dz(3, 1)
         quantize_dzt(0, 1)
         quantize_e4m3("wm_b_q", wm_b, [(0, 1), (0, 2)])
         multiply_dx(0, 1, 5)
         multiply_dx(0, 2, 2)
 
         scatter(0, 0)
-        stage1 = held("stage1", [P, P * PACK + N * PACK], BF16, reuses="stage0")
+        stage1 = held("stage1", [P, P * PACK + N * PACK], BF16, reuses="wm_b")
         wm_c = stage1[:, : P * PACK]
         dzn_bf1 = stage1[:, P * PACK :].rearrange("p (i t) -> p i t", t=PACK)
         for h in range(2):
             gpsimd_pair(dzn_bf1[:, :, 2 * h : 2 * h + 2], pairs[1, h])
         interleave_wm(wm_c, [(1, 0)], gpsimd_interleave)
-        turn_dz(2, 1, 4)
         gather_x(0, [0, 1], 0, reuses="wm_a_q_codes")
         copy_out_dx(0, 1)
+        turn_dz(2, 1, 5)
         scatter(0, 1)
         cast_x(1, scalar_cast, reuses="wm_b_q_codes")
         copy_out_dz(2, 1)
@@ -364,31 +364,31 @@ def tile_attend_gex_wx_kernel(tc, xT, dyT, ts, wm, offs, out_0, out_1):
         scatter(1, 1)
         xt_bf2 = held("xt_bf2", [P, HALF], BF16)
         copy_out_x(2, xt_bf2[:])
+        multiply_gw(1, 0, 4)
+        store_gw(1, 0)
         copy_out_dx(1, 2, reuses="x_g21")
         quantize_e4m3("q_x2", xt_bf2[:], [], 2)
-        multiply_dx(0, 3, 4)
+        multiply_dx(0, 3, 6)
         multiply_gw(0, 1, 2)
         scatter(1, 2)
         copy_out_dx(0, 3)
         cast_x(3, scalar_cast, reuses="q_d_codes")
-        multiply_gw(1, 0, 5)
-        multiply_gw(1, 1, 6)
+        multiply_gw(1, 1, 4)
+        multiply_gw(2, 0, 5)
         store_gw(0, 1, reuses="x3")
         multiply_dx(1, 3, 2)
         gather_x(3, [0], 0)
         gather_x(3, [1], 0)
         store_gw(1, 1, reuses="x_bf3")
-        store_gw(1, 0, reuses="x_g30")
-        multiply_gw(2, 0, 5)
-        multiply_gw(2, 1, 6)
+        store_gw(2, 0, reuses="x_g30")
+        multiply_gw(2, 1, 4)
         scatter(0, 3)
         xt_bf3 = held("xt_bf3", [P, HALF], BF16)
         copy_out_x(3, xt_bf3[:])
         quantize_e4m3("q_x3", xt_bf3[:], [], 3)
         copy_out_dx(1, 3, reuses="x_g31")
         multiply_gw(3, 0, 1)
-        multiply_gw(3, 1, 4)
-        for j in (2, 3):
-            for b in range(B):
-                store_gw(j, b, queue=nc.scalar)
+        multiply_gw(3, 1, 6)
+        for j, b in ((2, 1), (3, 0), (3, 1)):
+            store_gw(j, b, queue=nc.scalar)
         scatter(1, 3)

@@ -296,16 +296,15 @@ def tile_attend_gex_wx_kernel(tc, xT, dyT, ts, wm, offs, out_0, out_1):
         gather_dz(3, 1)
         turn_dz(3, 1, 6)
         cast_x(0, nc.vector.tensor_copy, reuses="ts_g0", cols=slice(0, T // 2))
-        stage0 = held("stage0", [P, P * PACK + HALF], BF16, reuses="dy3")
-        wm_a = stage0[:, : P * PACK]
-        dzt_bf[0, 1] = as_turned(stage0[:, P * PACK :])
+        stage0 = held("stage0", [P, 2 * HALF], BF16, reuses="dy3")
+        wm_a, wm_b = stage0[:, : P * PACK], stage0[:, :HALF]
+        dzt_bf[0, 1] = as_turned(stage0[:, HALF:])
         interleave_wm(wm_a, [(0, 0)], vector_interleave)
         quantize_dzt(0, 0)
         quantize_e4m3("wm_a_q", wm_a, [(0, 0)])
         quantize_dzn(0, dzn_bf0[:])
         multiply_dx(0, 0, 4)
         gather_dz(2, 1)
-        wm_b = held("wm_b", [P, HALF], BF16, reuses="dzn_bf0")[:]
         vector_interleave(wm_b.rearrange("p (d t) -> p d t", t=PACK), wm_next)
         copy_out_dz(2, 0)
         copy_out_dz(3, 0)
@@ -318,7 +317,7 @@ def tile_attend_gex_wx_kernel(tc, xT, dyT, ts, wm, offs, out_0, out_1):
         multiply_dx(0, 2, 2)
 
         scatter(0, 0)
-        stage1 = held("stage1", [P, P * PACK + N * PACK], BF16, reuses="wm_b")
+        stage1 = held("stage1", [P, P * PACK + N * PACK], BF16, reuses="stage0")
         wm_c = stage1[:, : P * PACK]
         dzn_bf1 = stage1[:, P * PACK :].rearrange("p (i t) -> p i t", t=PACK)
         for h in range(2):
@@ -333,8 +332,8 @@ def tile_attend_gex_wx_kernel(tc, xT, dyT, ts, wm, offs, out_0, out_1):
         copy_out_dx(0, 2, reuses="wm10")
         gather_x(1, [0], 1)
         gather_x(1, [1], 1)
-        quantize_dzn(1, dzn_bf1)
-        quantize_e4m3("wm_c_q", wm_c, [(1, 0)])
+        quantize_dzn(1, dzn_bf1, reuses="late")
+        quantize_e4m3("wm_c_q", wm_c, [(1, 0)], reuses="x1")
         multiply_dx(1, 0, 3)
 
         scatter(0, 2)

@@ -1,3 +1,4 @@
+import math
 from contextlib import ExitStack
 
 import concourse.mybir as mybir
@@ -21,11 +22,12 @@ ADD = mybir.AluOpType.add
 P = 128
 PACK = 4
 BLOCKS = D // P
-HALF_D = D // 2
 HALF_N = N // 2
 LIST_COLS = N // 16
 LINE = 4
 LAST = P - 1
+THIRD = 384
+WIDE = 2 * P * PACK
 
 
 def tile_attend_gex_wx_kernel(tc, xT, dyT, ts, wm, offs, out_0, out_1):
@@ -35,67 +37,76 @@ def tile_attend_gex_wx_kernel(tc, xT, dyT, ts, wm, offs, out_0, out_1):
         keep = ctx.enter_context(tc.tile_pool(name="keep", bufs=1))
         psum = ctx.enter_context(tc.psum_pool(name="psum", bufs=1))
 
-        tag_of = {}
+        shared = ctx.enter_context(tc.tile_pool(name="shared", bufs=1))
+        start_of = {"end": 0}
+        size_of = {F32: 4, U32: 4, BF16: 2}
 
-        def held(name, shape, dtype, reuses=None):
-            tag_of[name] = tag_of[reuses] if reuses else name
-            return keep.tile(shape, dtype, name=name, tag=tag_of[name], align_bytes=64)
+        def held(name, shape, dtype, over=None, skip=0, across=None):
+            size = size_of[dtype] * math.prod(shape[1:])
+            if over:
+                start_of[name] = start_of[over] + skip
+            elif across:
+                start_of[name] = start_of[across] - size // 2
+            else:
+                start_of[name] = start_of["end"]
+                start_of["end"] = start_of["end"] + -(-size // 64) * 64
+            return shared.tile(shape, dtype, name=name, offset=start_of[name], align_bytes=64)
+
+        def room(name, size):
+            start_of[name] = start_of["end"]
+            start_of["end"] = start_of["end"] + size
 
         def bank(name, shape, number):
             return psum.tile(shape, F32, name=name, tag=f"bank{number}")
 
         offsets = keep.tile([P, B * LIST_COLS], U16, name="offsets")
         ts_sb = held("ts_sb", [P, T], F32)
-        dy_sb, wm_sb, x_sb, x_bf, x_g, x_bank, xt_bf, x_q = {}, {}, {}, {}, {}, {}, {}, {}
-        ts_g, dz, turned, dzt_bf, dzt_q, dzn_q, wm_q, product = {}, {}, {}, {}, {}, {}, {}, {}
+        dy_sb, wm_sb, x_sb, picked, x_bank, x_q = {}, {}, {}, {}, {}, {}
+        ts_g, dz, turned, dzt_bf, dzt_q, dzn_q, wm_q, product, dx_sb, gw, windows = {}, {}, {}, {}, {}, {}, {}, {}, {}, {}, {}
 
-        ident = keep.tile([P, P], F32, name="ident")
-        make_identity(nc, ident[:])
+        def entries(b, first=0, width=N):
+            start = b * N + first
+            return offsets[:, start // 16 : (start + width) // 16]
 
-        nc.sync.dma_start(out=ts_sb[LAST:, :], in_=ts[LAST:, :])
-        nc.gpsimd.memset(ts_sb[:LAST, : T // 4], 0.0)
-        nc.vector.memset(ts_sb[:LAST, T // 4 :], 0.0)
-        nc.sync.dma_start(offsets[:], offs)
+        def vector_copy(out, in_):
+            nc.vector.tensor_copy(out, in_)
 
-        windows = []
-        for j in range(BLOCKS - 1):
-            windows.append(keep.tile([P, T], F32, name=f"window{j}"))
-            nc.gpsimd.memset(windows[j][:].bitcast(I32), 0)
-        windows.append(windows[0])
+        def scalar_copy(out, in_):
+            nc.scalar.activation(out, in_, COPY)
 
-        def expert_offsets(b):
-            return offsets[:, b * LIST_COLS : (b + 1) * LIST_COLS]
-
-        def load_dy(t):
-            dy_sb[t] = held(f"dy{t}", [P, T], F32)
+        def load_dy(t, **place):
+            dy_sb[t] = held(f"dy{t}", [P, T], F32, **place)
             nc.sync.dma_start(out=dy_sb[t][:], in_=dyT.rearrange("(p t) c -> t p c", t=PACK)[t])
 
-        def load_wm(b, first, count):
-            tile = held(f"wm{b}{first}", [P, PACK, count * P], F32)
+        def load_wm(b, first, count, **place):
+            wm_sb[b, first] = held(f"wm{b}{first}", [P, PACK, count * P], F32, **place)
             rows = wm[b].rearrange("(p t) d -> p t d", t=PACK)
-            nc.sync.dma_start(out=tile[:], in_=rows[:, :, first * P : (first + count) * P])
-            for k in range(count):
-                wm_sb[b, first + k] = tile[:, :, k * P : (k + 1) * P]
-            return tile[:]
+            nc.sync.dma_start(out=wm_sb[b, first][:], in_=rows[:, :, first * P : (first + count) * P])
 
-        def load_x(j, pieces=1):
-            x_sb[j] = held(f"x{j}", [P, T], F32)
-            for first in range(0, T, T // pieces):
-                cols = slice(first, first + T // pieces)
-                nc.sync.dma_start(out=x_sb[j][:, cols], in_=xT[j * P : (j + 1) * P, cols])
+        def load_x(j, **place):
+            x_sb[j] = held(f"x{j}", [P, T], F32, **place)
+            nc.sync.dma_start(out=x_sb[j][:], in_=xT[j * P : (j + 1) * P, :])
 
-        def planes(name, width, reuses=None):
-            codes = held(name + "_codes", [P, width], U32, reuses)
+        def planes(name, width, **place):
+            codes = held(name + "_codes", [P, width], U32, **place)
             scales = keep.tile([P, width], U8, name=name + "_scales", align_bytes=64)
             return codes, scales
 
         def quantize(dst, src, fmt, cols=slice(None)):
             nc.vector.quantize_mx(out=dst[0][:, cols].bitcast(fmt), scales=dst[1][:, cols], in_=src)
 
+        def vector_interleave(dst, src):
+            nc.vector.tensor_copy(
+                out=dst.rearrange("p (c i) t -> p c t i", i=LINE), in_=src.rearrange("p t (c i) -> p c t i", i=LINE)
+            )
+
         def scalar_interleave(dst, src):
             nc.scalar.copy(
                 out=dst.rearrange("p (c i) t -> p c t i", i=LINE), in_=src.rearrange("p t (c i) -> p c t i", i=LINE)
             )
+
+        def vector_pair(dst, src):
+            nc.vector.tensor_copy(out=dst, in_=src.rearrange("p t i -> p i t"))
 
         def scalar_pair(dst, src):
             nc.scalar.copy(out=dst, in_=src.rearrange("p t i -> p i t"))
@@ -105,58 +116,48 @@ def tile_attend_gex_wx_kernel(tc, xT, dyT, ts, wm, offs, out_0, out_1):
                 out=dst, in0=src.rearrange("p t c -> p c t"), scalar1=1.0, scalar2=0.0, op0=MULT, op1=ADD
             )
 
-        def ts_down(b, first, width, number):
-            name = f"{b}_{first}"
-            row = held("ts_row" + name, [P, width], F32)
-            entries = expert_offsets(b)[:, first // 16 : (first + width) // 16]
-            nc.vector.tensor_copy(row[:], ts_sb[:].indirect(entries))
-            down = bank("down" + name, [P, width // P, P], number)
-            for q in range(width // P):
-                nc.tensor.transpose(down[:, q, :], row[:, q * P : (q + 1) * P], ident[:])
-            cols = held("ts_cols" + name, [P, width // P], F32)
-            nc.scalar.copy(out=cols[:], in_=down[:, :, LAST])
-            return cols
+        def ts_gather(b, first, width, copy):
+            row = held(f"ts_row{b}_{first}", [P, width], F32)
+            copy(row[:], ts_sb[:].indirect(entries(b, first, width)))
+            return row
 
-        def ts_across(b, first, width, number, cols):
-            across = bank(f"across{b}_{first}", [P, width // P, P], number)
-            for q in range(width // P):
+        def ts_down(row, k, number, copy):
+            count = row.shape[1] // P
+            down = bank(f"down{k}", [P, count, P], number)
+            for q in range(count):
+                nc.tensor.transpose(down[:, q, :], row[:, q * P : (q + 1) * P], ident[:])
+            copy(columns[k], down[:, :, LAST])
+            return columns[k]
+
+        def ts_across(cols, b, first, number, copy):
+            count = cols.shape[1]
+            across = bank(f"across{b}_{first}", [P, count, P], number)
+            for q in range(count):
                 nc.tensor.transpose(across[:, q, :], cols[:, q : q + 1].to_broadcast([P, P]), ident[:])
-            nc.scalar.copy(out=ts_g[b][:, first : first + width], in_=across[:].rearrange("p q s -> p (q s)"))
+            copy(ts_g[b][:, first : first + count * P], across[:].rearrange("p q s -> p (q s)"))
 
         def gather_dz(t, b, first=0, width=N):
-            entries = expert_offsets(b)[:, first // 16 : (first + width) // 16]
             slots = slice(first, first + width)
-            nc.vector.tensor_tensor(dz[t, b][:, slots], dy_sb[t][:].indirect(entries), ts_g[b][:, slots], MULT)
+            window = dy_sb[t][:].indirect(entries(b, first, width))
+            nc.vector.tensor_tensor(dz[t, b][:, slots], window, ts_g[b][:, slots], MULT)
 
         def turn_dz(t, b, number):
             turned[t, b] = bank(f"turned{t}{b}", [P, PACK, P], number)
             for r in range(PACK):
                 nc.tensor.transpose(turned[t, b][:, r, :], dz[t, b][:, r:N:PACK], ident[:])
 
-        def copy_out_dz(t, b):
-            nc.scalar.activation(dzt_bf[b, t // 2][:, t % 2], turned[t, b][:].rearrange("s k p -> s p k"), COPY)
-
-        HALF = HALF_D * PACK
+        def copy_out_dz(t, b, copy=scalar_copy):
+            copy(dzt_bf[b, t // 2][:, t % 2], turned[t, b][:].rearrange("s k p -> s p k"))
 
         def as_turned(part):
             return part.rearrange("s (t p k) -> s t p k", t=2, k=PACK)
 
-        def interleave_wm(part, blocks, interleave):
-            for k, (b, j) in enumerate(blocks):
-                dst = part[:, k * P * PACK : (k + 1) * P * PACK].rearrange("p (d t) -> p d t", t=PACK)
-                interleave(dst, wm_sb[b, j])
+        def as_words(part):
+            return part.rearrange("p (c t) -> p c t", t=PACK)
 
-        def vector_interleave(dst, src):
-            nc.vector.tensor_copy(
-                out=dst.rearrange("p (c i) t -> p c t i", i=LINE), in_=src.rearrange("p t (c i) -> p c t i", i=LINE)
-            )
-
-        def gpsimd_pair(dst, src):
-            gpsimd_interleave(dst, src)
-
-        def quantize_e4m3(name, part, blocks, x_block=None, reuses=None):
+        def quantize_e4m3(name, part, blocks, x_block=None, **place):
             width = len(blocks) * P + (0 if x_block is None else B * P)
-            dst = planes(name, width, reuses)
+            dst = planes(name, width, **place)
             quantize(dst, part, E4M3)
             for k, block in enumerate(blocks):
                 wm_q[block] = dst, slice(k * P, (k + 1) * P)
@@ -167,9 +168,9 @@ def tile_attend_gex_wx_kernel(tc, xT, dyT, ts, wm, offs, out_0, out_1):
             cols = slice(h * DV // 2, (h + 1) * DV // 2)
             quantize(dzt_q[b], dzt_bf[b, h].rearrange("s t p k -> s (t p k)"), E5M2, cols)
 
-        def quantize_dzn(b, src, reuses=None):
-            dzn_q[b] = planes(f"dzn_q{b}", N, reuses)
-            quantize(dzn_q[b], src.rearrange("p i t -> p (i t)"), E5M2)
+        def quantize_dzn(b, src, **place):
+            dzn_q[b] = planes(f"dzn_q{b}", N, **place)
+            quantize(dzn_q[b], src, E5M2)
 
         def multiply(out, stationary, cols, moving):
             nc.tensor.matmul_mx(
@@ -182,39 +183,42 @@ def tile_attend_gex_wx_kernel(tc, xT, dyT, ts, wm, offs, out_0, out_1):
                 stop=True,
             )
 
-        dx_sb = {}
-
         def multiply_dx(b, j, number):
             product[b, j] = bank(f"dx{b}{j}", [P, N], number)
             multiply(product[b, j], *wm_q[b, j], dzn_q[b])
 
-        def copy_out_dx(b, j, reuses=None):
-            dx_sb[b, j] = held(f"dx_sb{b}{j}", [P, N], F32, reuses)
-            nc.scalar.copy(out=dx_sb[b, j][:], in_=product[b, j][:])
+        def copy_out_dx(b, j, dst, first=0):
+            dx_sb[b, j, first] = dst
+            nc.scalar.copy(out=dst, in_=product[b, j][:, first : first + dst.shape[1]])
 
-        def scatter(b, j):
-            nc.vector.tensor_copy(windows[j][:].indirect(expert_offsets(b)), dx_sb[b, j][:])
-            if b == B - 1:
-                nc.sync.dma_start(out=out_1[j * P : (j + 1) * P, :], in_=windows[j][:])
+        def scatter(b, j, first=0):
+            values = dx_sb[b, j, first]
+            nc.vector.tensor_copy(windows[j][:].indirect(entries(b, first, values.shape[1])), values)
 
-        def cast_x(j, copy, reuses=None, cols=slice(0, T)):
-            if cols.start == 0:
-                x_bf[j] = held(f"x_bf{j}", [P, T], BF16, reuses)
-            copy(out=x_bf[j][:, cols], in_=x_sb[j][:, cols])
+        def scalar_scatter(b, j, first, values):
+            scalar_copy(windows[j][:].indirect(entries(b, first, values.shape[1])), values)
 
-        def scalar_cast(out, in_):
-            nc.scalar.activation(out, in_, COPY)
+        def share(name, width=N, **place):
+            return held(name, [P, width], F32, **place)[:]
 
-        def gather_x(j, experts, number, reuses=None):
-            if experts[0] == 0:
-                x_bank[j] = bank(f"x_bank{j}", [P, B, 2, P], number)
-            picked = held(f"x_g{j}{experts[0]}", [P, len(experts) * N], BF16, reuses)
-            entries = offsets[:, experts[0] * LIST_COLS : (experts[-1] + 1) * LIST_COLS]
-            nc.scalar.activation(picked[:], x_bf[j][:].indirect(entries), COPY)
-            words = picked[:].bitcast(F32)
-            for k, b in enumerate(experts):
+        def store_window(j, queue=nc.sync):
+            queue.dma_start(out=out_1[j * P : (j + 1) * P, :], in_=windows[j][:])
+
+        def gather_x(j, first, last, copy):
+            dst, start = picked[j, first // N]
+            copy(dst[:, first - start : last - start], x_sb[j][:].indirect(entries(0, first, last - first)))
+
+        def pick_into(j, dst, experts=(0, 1)):
+            for b in experts:
+                picked[j, b] = dst, experts[0] * N
+
+        def turn_x(j, number):
+            x_bank[j] = bank(f"x_bank{j}", [P, B, 2, P], number)
+            for b in range(B):
+                dst, start = picked[j, b]
+                words = dst[:, b * N - start : (b + 1) * N - start].bitcast(F32)
                 for u in range(2):
-                    nc.tensor.transpose(x_bank[j][:, b, u, :], words[:, k * HALF_N + u : (k + 1) * HALF_N : 2], ident[:])
+                    nc.tensor.transpose(x_bank[j][:, b, u, :], words[:, u:HALF_N:2], ident[:])
 
         def copy_out_x(j, part):
             nc.scalar.copy(
@@ -222,172 +226,187 @@ def tile_attend_gex_wx_kernel(tc, xT, dyT, ts, wm, offs, out_0, out_1):
                 in_=x_bank[j][:].rearrange("s b u d -> s b d u"),
             )
 
-        gw = {}
-
         def multiply_gw(j, b, number):
             gw[j, b] = bank(f"gw{j}{b}", [P, DV], number)
             codes, first = x_q[j]
             multiply(gw[j, b], codes, slice(first + b * P, first + (b + 1) * P), dzt_q[b])
 
-        def store_gw(j, b, reuses=None, queue=nc.sync):
-            gw_sb = held(f"gw_sb{j}{b}", [P, P, PACK], F32, reuses)
-            nc.scalar.copy(out=gw_sb[:], in_=gw[j, b][:].rearrange("d (t p) -> d p t", t=PACK))
+        def store_gw(j, b, queue=nc.sync, copy=nc.scalar.copy, **place):
+            gw_sb = held(f"gw_sb{j}{b}", [P, P, PACK], F32, **place)
+            copy(out=gw_sb[:], in_=gw[j, b][:].rearrange("d (t p) -> d p t", t=PACK))
             queue.dma_start(out=out_0[b, j * P : (j + 1) * P, :], in_=gw_sb[:].rearrange("d p t -> d (p t)"))
 
-        def pair_tile(b, h, reuses=None):
-            pair = held(f"dz{b}{h}", [P, 2, N], F32, reuses)
-            for e in range(2):
-                dz[2 * h + e, b] = pair[:, e, :]
-            return pair
+        ident = keep.tile([P, P], F32, name="ident")
+        make_identity(nc, ident[:])
 
-        for t in range(PACK):
-            load_dy(t)
-        load_wm(0, 0, 1)
-        load_x(0, pieces=2)
-        wm_next = load_wm(0, 1, 2)
-        load_wm(1, 0, 1)
+        nc.sync.dma_start(out=ts_sb[LAST:, :], in_=ts[LAST:, :])
+        nc.gpsimd.memset(ts_sb[:LAST, : T // 4], 0.0)
+        nc.vector.memset(ts_sb[:LAST, T // 4 :], 0.0)
+        nc.sync.dma_start(offsets[:], offs)
+
+        for j in range(BLOCKS):
+            windows[j] = keep.tile([P, T], F32, name=f"window{j}")
+            nc.gpsimd.memset(windows[j][:].bitcast(I32), 0)
+
+        PLANE = 4 * N
+        room("late", PLANE + 4 * T)
+        load_dy(0, over="late", skip=PLANE)
+        load_dy(1)
+        load_dy(2)
+        load_dy(3)
+        load_wm(0, 0, BLOCKS)
+        room("x0_wm1", 2 * 4 * T + 2 * PLANE)
+        load_x(0, over="x0_wm1")
         load_x(1)
-        load_wm(1, 1, 1)
-        load_wm(1, 2, 2)
-        load_wm(0, 3, 1)
+        load_wm(1, 0, BLOCKS, over="x0_wm1", skip=4 * T)
         load_x(2)
         load_x(3)
 
         for b in range(B):
-            ts_g[b] = held(f"ts_g{b}", [P, N], F32)
-        halves = [(b, h * HALF_N) for b in range(B) for h in range(2)]
-        cols = ts_down(*halves[0], HALF_N, 0)
-        for k, (b, first) in enumerate(halves):
-            ahead = ts_down(*halves[k + 1], HALF_N, (k + 1) % 2) if k + 1 < len(halves) else None
-            ts_across(b, first, HALF_N, 2 + k, cols)
+            ts_g[b] = held(f"ts_g{b}", [P, N], F32)[:]
+        room("dzn1", 2 * PLANE)
+        room("plain0", PLANE)
+        columns = [held(f"ts_cols{k}", [P, 2], F32)[:] for k in range(2)]
+        columns.append(held("ts_cols2", [P, 2], F32, over="plain0")[:])
+        columns.append(held("ts_cols3", [P, 2], F32, over="dzn1", skip=PLANE)[:])
+        quarters = [(b, h * HALF_N) for b in range(B) for h in range(2)]
+        rows = [ts_gather(b, first, HALF_N, vector_copy) for b, first in quarters]
+        cols = ts_down(rows[0], 0, 0, nc.scalar.copy)
+        for k, (b, first) in enumerate(quarters):
+            ahead = ts_down(rows[k + 1], k + 1, (k + 1) % 2, nc.scalar.copy) if k + 1 < len(quarters) else None
+            ts_across(cols, b, first, 2 + k, vector_copy if b == 0 else nc.scalar.copy)
             cols = ahead
 
-        pairs = {(b, 0): pair_tile(b, 0)[:] for b in range(B)}
-        dzt_bf[0, 0] = as_turned(held("dzt_bf00", [P, HALF], BF16)[:])
-        dzt_bf1 = held("dzt_bf1", [P, 2 * HALF], BF16)
+        early = held("early", [P, 2, N], F32)
+        dz[0, 0], dz[1, 0] = early[:, 0, :], early[:, 1, :]
+        dzn_bf0 = held("dzn_bf0", [P, 2 * WIDE], BF16)
+        dzt_bf[0, 0] = as_turned(held("dzt_bf00", [P, WIDE], BF16)[:])
+        dzt_bf[0, 1] = as_turned(held("dzt_bf01", [P, WIDE], BF16, over="dzn1")[:])
+        dzt_bf1 = held("dzt_bf1", [P, 2 * WIDE], BF16)[:]
         for h in range(2):
-            dzt_bf[1, h] = as_turned(dzt_bf1[:, h * HALF : (h + 1) * HALF])
-        dzn_bf0 = held("dzn_bf0", [P, N, PACK], BF16, reuses="ts_cols1_256")
-        dzt_q[0] = planes("dzt_q0", DV)
+            dzt_bf[1, h] = as_turned(dzt_bf1[:, h * WIDE : (h + 1) * WIDE])
+        plain0 = held("plain0", [P, N], F32, over="plain0")[:]
+        plain2 = held("plain2", [P, N], F32, over="ts_cols3")[:]
 
-        plain = held("plain", [P, N], F32)
-        nc.vector.tensor_copy(plain[:], dy_sb[0][:].indirect(expert_offsets(1)))
-        for first in (0, HALF_N):
-            gather_dz(0, 0, first, HALF_N)
-        turn_dz(0, 0, 1)
-        copy_out_dz(0, 0)
+
+        gather_dz(0, 0)
+        turn_dz(0, 0, 6)
+        scalar_copy(plain0, dy_sb[0][:].indirect(entries(1)))
         gather_dz(1, 0)
-        scalar_pair(dzn_bf0[:, :, 0:2], pairs[0, 0])
+        copy_out_dz(0, 0)
         turn_dz(1, 0, 7)
-        copy_out_dz(1, 0)
-        nc.vector.tensor_tensor(dz[0, 1], plain[:], ts_g[1][:], MULT)
+        late = held("late", [P, PACK + 1, N], F32, over="late")
+        dz[2, 0], dz[3, 0] = late[:, 3, :], late[:, 4, :]
+        for t in range(PACK):
+            dz[t, 1] = late[:, t, :]
+        nc.vector.tensor_tensor(dz[0, 1], plain0, ts_g[1], MULT)
+        scalar_copy(plain2, dy_sb[2][:].indirect(entries(1)))
+        turn_dz(0, 1, 0)
         gather_dz(1, 1)
-        for t in range(2):
-            turn_dz(t, 1, 6 * t)
-            copy_out_dz(t, 1)
-        late = held("late", [P, 3, N], F32, reuses="plain")
-        dz[2, 0], dz[3, 0], dz[2, 1], dz[3, 1] = late[:, 0, :], late[:, 1, :], late[:, 1, :], late[:, 2, :]
-        pairs[0, 1], pairs[1, 1] = late[:, 0:2, :], late[:, 1:3, :]
         gather_dz(2, 0)
-        gather_dz(3, 0)
-        scalar_pair(dzn_bf0[:, :, 2:4], pairs[0, 1])
+        copy_out_dz(1, 0)
+        scalar_pair(as_words(dzn_bf0[:])[:, :, 0:2], early[:])
+        turn_dz(1, 1, 1)
         turn_dz(2, 0, 2)
-        turn_dz(3, 0, 3)
-        gather_dz(3, 1)
-        turn_dz(3, 1, 6)
-        cast_x(0, nc.vector.tensor_copy, reuses="ts_g0", cols=slice(0, T // 2))
-        stage0 = held("stage0", [P, 2 * HALF], BF16, reuses="dy3")
-        wm_a, wm_b = stage0[:, : P * PACK], stage0[:, :HALF]
-        dzt_bf[0, 1] = as_turned(stage0[:, HALF:])
-        interleave_wm(wm_a, [(0, 0)], vector_interleave)
-        quantize_dzt(0, 0)
-        quantize_e4m3("wm_a_q", wm_a, [(0, 0)])
-        quantize_dzn(0, dzn_bf0[:])
-        multiply_dx(0, 0, 4)
-        gather_dz(2, 1)
-        vector_interleave(wm_b.rearrange("p (d t) -> p d t", t=PACK), wm_next)
+        gather_dz(3, 0)
+        nc.vector.tensor_tensor(dz[2, 1], plain2, ts_g[1], MULT)
+        copy_out_dz(0, 1)
+        copy_out_dz(1, 1)
         copy_out_dz(2, 0)
+        turn_dz(3, 0, 4)
+        turn_dz(2, 1, 3)
+        vector_pair(as_words(dzn_bf0[:])[:, :, 2:4], late[:, 3:5, :])
+        stage0 = held("stage0", [P, WIDE], BF16, over="ts_g0")[:]
+        vector_interleave(as_words(stage0), wm_sb[0, 0][:, :, : 2 * P])
+        quantize_dzn(0, dzn_bf0[:])
+        quantize_e4m3("q_a", stage0, [(0, 0), (0, 1)])
         copy_out_dz(3, 0)
-        cast_x(0, scalar_cast, cols=slice(T // 2, T))
-        copy_out_dx(0, 0)
-        copy_out_dz(3, 1)
+        stage1 = held("stage1", [P, WIDE], BF16, over="plain2")[:]
+        scalar_interleave(as_words(stage1), wm_sb[0, 0][:, :, 2 * P :])
+        copy_out_dz(2, 1)
+        multiply_dx(0, 0, 5)
+        multiply_dx(0, 1, 6)
+        gather_dz(3, 1)
+        dzt_q[0] = planes("dzt_q0", DV, over="dzn_bf0")
+        quantize_dzt(0, 0)
         quantize_dzt(0, 1)
-        quantize_e4m3("wm_b_q", wm_b, [(0, 1), (0, 2)])
-        multiply_dx(0, 1, 5)
-        multiply_dx(0, 2, 2)
+        quantize_e4m3("q_b", stage1, [(0, 2), (0, 3)], over="dzn_bf0", skip=PLANE)
+        copy_out_dx(0, 0, share("dx_sb00", over="wm10", skip=4 * T))
+        copy_out_dx(0, 1, share("dx_sb01"))
+        turn_dz(3, 1, 5)
 
         scatter(0, 0)
-        stage1 = held("stage1", [P, P * PACK + N * PACK], BF16, reuses="stage0")
-        wm_c = stage1[:, : P * PACK]
-        dzn_bf1 = stage1[:, P * PACK :].rearrange("p (i t) -> p i t", t=PACK)
-        for h in range(2):
-            gpsimd_pair(dzn_bf1[:, :, 2 * h : 2 * h + 2], pairs[1, h])
-        interleave_wm(wm_c, [(1, 0)], gpsimd_interleave)
-        gather_x(0, [0, 1], 0, reuses="wm_a_q_codes")
-        copy_out_dx(0, 1)
-        turn_dz(2, 1, 5)
+        dzn_bf1 = held("dzn_bf1", [P, 2 * WIDE], BF16, over="dzn1")[:]
+        gpsimd_interleave(as_words(dzn_bf1), late[:, :PACK, :])
+        stage2 = held("stage2", [P, 2 * WIDE], BF16, over="late")
+        gpsimd_interleave(as_words(stage2[:]), wm_sb[1, 0][:])
+        pick_into(0, held("x_g0", [P, B * N], BF16, over="dzt_bf00")[:])
+        gather_x(0, 0, B * N, scalar_copy)
+        multiply_dx(0, 2, 6)
+        turn_x(0, 7)
+        copy_out_dz(3, 1)
         scatter(0, 1)
-        cast_x(1, scalar_cast, reuses="wm_b_q_codes")
-        copy_out_dz(2, 1)
-        copy_out_dx(0, 2, reuses="wm10")
-        gather_x(1, [0], 1)
-        gather_x(1, [1], 1)
-        quantize_dzn(1, dzn_bf1, reuses="late")
-        quantize_e4m3("wm_c_q", wm_c, [(1, 0)], reuses="x1")
-        multiply_dx(1, 0, 3)
+        pick_into(1, held("x_g10", [P, N], BF16, over="x0", skip=7 * PLANE // 2)[:], (0,))
+        pick_into(1, held("x_g11", [P, N], BF16, over="dx_sb00", skip=PLANE // 2)[:], (1,))
+        gather_x(1, 0, N, scalar_copy)
+        gather_x(1, N, B * N, scalar_copy)
+        turn_x(1, 0)
+        xt01 = held("xt01", [P, 2 * WIDE], BF16)
+        copy_out_x(0, xt01[:, :WIDE])
+        copy_out_dx(0, 2, share("dx_sb02", across="wm10"))
+        copy_out_x(1, xt01[:, WIDE:])
+        pick_into(2, held("x_g2", [P, B * N], BF16, over="x_g11", skip=-3 * PLANE // 4)[:])
+        gather_x(2, 0, B * N, scalar_copy)
+        quantize_dzn(1, dzn_bf1, over="wm10", skip=PLANE // 2)
+        quantize_e4m3("q_x0", xt01[:, :WIDE], [], 0, over="wm10", skip=5 * PLANE // 2)
+        quantize_e4m3("q_c", stage2[:], [(1, j) for j in range(BLOCKS)])
+        quantize_e4m3("q_x1", xt01[:, WIDE:], [], 1, over="wm10", skip=3 * PLANE)
+        dzt_q[1] = planes("dzt_q1", DV, over="wm10", skip=3 * PLANE // 2)
+        quantize(dzt_q[1], dzt_bf1, E5M2)
+        multiply_gw(0, 0, 6)
+        multiply_dx(1, 0, 0)
+        multiply_gw(1, 0, 7)
+        turn_x(2, 4)
 
         scatter(0, 2)
-        stage2 = held("stage2", [P, 2 * HALF], BF16, reuses="stage1")
-        interleave_wm(stage2[:, :HALF], [(1, 2), (1, 1)], gpsimd_interleave)
-        copy_out_x(0, stage2[:, HALF:])
-        cast_x(2, scalar_cast, reuses="x_bf1", cols=slice(0, T // 2))
-        copy_out_dx(1, 0, reuses="wm11")
-        cast_x(2, scalar_cast, cols=slice(T // 2, T))
-        quantize_e4m3("q_d", stage2[:], [(1, 2), (1, 1)], 0)
-        multiply_dx(1, 1, 4)
-        multiply_dx(1, 2, 5)
-
+        store_gw(0, 0, over="dy1")
+        copy_out_dx(1, 0, share("dx_sb10"))
+        multiply_dx(1, 1, 6)
+        multiply_dx(1, 2, 0)
+        store_gw(1, 0, over="dy1", skip=PLANE)
+        copy_out_dx(1, 1, share("dx_sb11"))
+        copy_out_dx(1, 2, share("dx_sb12"))
+        scalar_scatter(1, 1, 0, dx_sb[1, 1, 0][:, :HALF_N])
+        xt2 = held("xt2", [P, WIDE], BF16)
+        copy_out_x(2, xt2[:])
+        scalar_scatter(1, 1, HALF_N, dx_sb[1, 1, 0][:, HALF_N:])
         scatter(1, 0)
-        stage3 = held("stage3", [P, 2 * HALF], BF16, reuses="stage2")
-        interleave_wm(stage3[:, :HALF], [(0, 3), (1, 3)], gpsimd_interleave)
-        copy_out_x(1, stage3[:, HALF:])
-        gather_x(2, [0], 2)
-        gather_x(2, [1], 2)
-        copy_out_dx(1, 1, reuses="wm12")
-        quantize_e4m3("q_e", stage3[:], [(0, 3), (1, 3)], 1)
-        dzt_q[1] = planes("dzt_q1", DV, reuses="x_g20")
-        quantize(dzt_q[1], dzt_bf1[:], E5M2)
-        multiply_gw(0, 0, 6)
-        store_gw(0, 0, reuses="x_bf2")
-
-        scatter(1, 1)
-        xt_bf2 = held("xt_bf2", [P, HALF], BF16)
-        copy_out_x(2, xt_bf2[:])
-        multiply_gw(1, 0, 4)
-        store_gw(1, 0)
-        copy_out_dx(1, 2, reuses="x_g21")
-        quantize_e4m3("q_x2", xt_bf2[:], [], 2)
-        multiply_dx(0, 3, 6)
-        multiply_gw(0, 1, 2)
+        store_window(0)
         scatter(1, 2)
-        copy_out_dx(0, 3)
-        cast_x(3, scalar_cast, reuses="q_d_codes")
-        multiply_gw(1, 1, 4)
-        multiply_gw(2, 0, 5)
-        store_gw(0, 1, reuses="x3")
-        multiply_dx(1, 3, 2)
-        gather_x(3, [0], 0)
-        gather_x(3, [1], 0)
-        store_gw(1, 1, reuses="x_bf3")
-        store_gw(2, 0, reuses="x_g30")
-        multiply_gw(2, 1, 4)
+        multiply_dx(0, 3, 6)
+        copy_out_dx(0, 3, share("dx_sb03"))
+        store_window(1, nc.scalar)
+        pick_into(3, held("x_g3", [P, B * N], BF16, over="dx_sb11")[:])
+        gather_x(3, 0, B * N, scalar_copy)
+        multiply_gw(0, 1, 4)
+        multiply_gw(1, 1, 6)
+        turn_x(3, 2)
+        multiply_dx(1, 3, 7)
+        quantize_e4m3("q_x2", xt2[:], [], 2)
+        store_window(2)
+
         scatter(0, 3)
-        xt_bf3 = held("xt_bf3", [P, HALF], BF16)
-        copy_out_x(3, xt_bf3[:])
-        quantize_e4m3("q_x3", xt_bf3[:], [], 3)
-        copy_out_dx(1, 3, reuses="x_g31")
-        multiply_gw(3, 0, 1)
-        multiply_gw(3, 1, 6)
-        for j, b in ((2, 1), (3, 0), (3, 1)):
-            store_gw(j, b, queue=nc.scalar)
+        store_gw(0, 1, nc.scalar, over="dy1", skip=2 * PLANE)
+        store_gw(1, 1, nc.scalar, over="dy1", skip=3 * PLANE)
+        xt3 = held("xt3", [P, WIDE], BF16)
+        copy_out_x(3, xt3[:])
+        copy_out_dx(1, 3, share("dx_sb13", over="x_g3"))
+        multiply_gw(2, 0, 4)
+        multiply_gw(2, 1, 6)
+        quantize_e4m3("q_x3", xt3[:], [], 3)
+        multiply_gw(3, 0, 5)
+        multiply_gw(3, 1, 1)
         scatter(1, 3)
+        for k, (j, b) in enumerate(((2, 0), (2, 1), (3, 0), (3, 1))):
+            store_gw(j, b, nc.scalar, over="dy2", skip=k * PLANE)
+        store_window(3)

@@ -249,12 +249,14 @@ def tile_attend_gex_wx_kernel(tc, xT, dyT, ts, wm, offs, out_0, out_1):
             nc.gpsimd.memset(windows[j][:].bitcast(I32), 0)
 
         PLANE = 4 * N
-        room("late", PLANE + 4 * T)
-        load_dy(0, over="late", skip=PLANE)
+        room("late", 5 * PLANE + 4 * T)
+        load_dy(0, over="late", skip=5 * PLANE)
         load_dy(1)
         load_dy(2)
         load_dy(3)
-        load_wm(0, 0, BLOCKS)
+        room("wm0", 4 * PLANE)
+        load_wm(0, 0, 2, over="wm0")
+        load_wm(0, 2, 2)
         room("x0_wm1", 2 * 4 * T + 2 * PLANE)
         load_x(0, over="x0_wm1")
         load_x(1)
@@ -264,8 +266,8 @@ def tile_attend_gex_wx_kernel(tc, xT, dyT, ts, wm, offs, out_0, out_1):
 
         for b in range(B):
             ts_g[b] = held(f"ts_g{b}", [P, N], F32)[:]
-        room("dzn1", 2 * PLANE)
-        room("plain0", PLANE)
+        start_of["dzn1"] = start_of["wm0"] + 3 * PLANE // 2
+        room("plain0", 2 * PLANE)
         columns = [held(f"ts_cols{k}", [P, 2], F32)[:] for k in range(2)]
         columns.append(held("ts_cols2", [P, 2], F32, over="plain0")[:])
         columns.append(held("ts_cols3", [P, 2], F32, over="dzn1", skip=PLANE)[:])
@@ -279,68 +281,74 @@ def tile_attend_gex_wx_kernel(tc, xT, dyT, ts, wm, offs, out_0, out_1):
 
         early = held("early", [P, 2, N], F32)
         dz[0, 0], dz[1, 0] = early[:, 0, :], early[:, 1, :]
-        dzn_bf0 = held("dzn_bf0", [P, 2 * WIDE], BF16)
         dzt_bf[0, 0] = as_turned(held("dzt_bf00", [P, WIDE], BF16)[:])
-        dzt_bf[0, 1] = as_turned(held("dzt_bf01", [P, WIDE], BF16, over="dzn1")[:])
         dzt_bf1 = held("dzt_bf1", [P, 2 * WIDE], BF16)[:]
         for h in range(2):
             dzt_bf[1, h] = as_turned(dzt_bf1[:, h * WIDE : (h + 1) * WIDE])
-        plain0 = held("plain0", [P, N], F32, over="plain0")[:]
+        plain01 = held("plain01", [P, 2, N], F32, over="plain0")
+        plain0, plain1 = plain01[:, 0, :], plain01[:, 1, :]
         plain2 = held("plain2", [P, N], F32, over="ts_cols3")[:]
 
 
-        gather_dz(0, 0)
+        for first in (0, HALF_N):
+            gather_dz(0, 0, first, HALF_N)
         turn_dz(0, 0, 6)
         scalar_copy(plain0, dy_sb[0][:].indirect(entries(1)))
         gather_dz(1, 0)
-        copy_out_dz(0, 0)
         turn_dz(1, 0, 7)
-        late = held("late", [P, PACK + 1, N], F32, over="late")
-        dz[2, 0], dz[3, 0] = late[:, 3, :], late[:, 4, :]
+        late = held("late", [P, 9 * N], F32, over="late")
+        rows = late[:, : 2 * PACK * N].rearrange("p (r e n) -> p e r n", e=2, n=N)
+        dz1, last_pair = rows[:, 0], rows[:, 1, :2]
+        dz[2, 0], dz[3, 0] = last_pair[:, 0, :], last_pair[:, 1, :]
+        stage0 = late[:, 11 * HALF_N : 13 * HALF_N].bitcast(BF16)
+        dzn_bf0 = late[:, 13 * HALF_N : 17 * HALF_N].bitcast(BF16)
         for t in range(PACK):
-            dz[t, 1] = late[:, t, :]
+            dz[t, 1] = dz1[:, t, :]
         nc.vector.tensor_tensor(dz[0, 1], plain0, ts_g[1], MULT)
+        scalar_copy(plain1, dy_sb[1][:].indirect(entries(1)))
         scalar_copy(plain2, dy_sb[2][:].indirect(entries(1)))
         turn_dz(0, 1, 0)
-        gather_dz(1, 1)
         gather_dz(2, 0)
+        nc.vector.tensor_tensor(dz[1, 1], plain1, ts_g[1], MULT)
+        copy_out_dz(0, 0)
         copy_out_dz(1, 0)
-        scalar_pair(as_words(dzn_bf0[:])[:, :, 0:2], early[:])
-        turn_dz(1, 1, 1)
+        scalar_pair(as_words(dzn_bf0)[:, :, 0:2], early[:])
         turn_dz(2, 0, 2)
-        gather_dz(3, 0)
+        turn_dz(1, 1, 1)
         nc.vector.tensor_tensor(dz[2, 1], plain2, ts_g[1], MULT)
+        gather_dz(3, 0)
         copy_out_dz(0, 1)
         copy_out_dz(1, 1)
-        copy_out_dz(2, 0)
-        turn_dz(3, 0, 4)
         turn_dz(2, 1, 3)
-        vector_pair(as_words(dzn_bf0[:])[:, :, 2:4], late[:, 3:5, :])
-        stage0 = held("stage0", [P, WIDE], BF16, over="ts_g0")[:]
-        vector_interleave(as_words(stage0), wm_sb[0, 0][:, :, : 2 * P])
-        quantize_dzn(0, dzn_bf0[:])
-        quantize_e4m3("q_a", stage0, [(0, 0), (0, 1)])
-        copy_out_dz(3, 0)
+        turn_dz(3, 0, 4)
+        dzt_q[0] = planes("dzt_q0", DV, over="ts_g0")
+        quantize_dzt(0, 0)
+        vector_pair(as_words(dzn_bf0)[:, :, 2:4], last_pair)
+        vector_interleave(as_words(stage0), wm_sb[0, 0][:])
+        quantize_dzn(0, dzn_bf0, over="wm00", skip=PLANE // 2)
+        room("q_a", PLANE)
+        quantize_e4m3("q_a", stage0, [(0, 0), (0, 1)], over="q_a")
         stage1 = held("stage1", [P, WIDE], BF16, over="plain2")[:]
-        scalar_interleave(as_words(stage1), wm_sb[0, 0][:, :, 2 * P :])
-        copy_out_dz(2, 1)
+        scalar_interleave(as_words(stage1), wm_sb[0, 2][:])
+        dzt_bf[0, 1] = as_turned(held("dzt_bf01", [P, WIDE], BF16, over="dzn1")[:])
+        copy_out_dz(2, 0)
+        copy_out_dz(3, 0)
         multiply_dx(0, 0, 5)
         multiply_dx(0, 1, 6)
         gather_dz(3, 1)
-        dzt_q[0] = planes("dzt_q0", DV, over="dzn_bf0")
-        quantize_dzt(0, 0)
+        quantize_e4m3("q_b", stage1, [(0, 2), (0, 3)], over="dy3")
         quantize_dzt(0, 1)
-        quantize_e4m3("q_b", stage1, [(0, 2), (0, 3)], over="dzn_bf0", skip=PLANE)
         copy_out_dx(0, 0, share("dx_sb00", over="wm10", skip=4 * T))
+        copy_out_dz(2, 1)
         copy_out_dx(0, 1, share("dx_sb01"))
         turn_dz(3, 1, 5)
 
         scatter(0, 0)
         dzn_bf1 = held("dzn_bf1", [P, 2 * WIDE], BF16, over="dzn1")[:]
-        gpsimd_interleave(as_words(dzn_bf1), late[:, :PACK, :])
+        gpsimd_interleave(as_words(dzn_bf1), dz1)
         stage2 = held("stage2", [P, 2 * WIDE], BF16, over="late")
         gpsimd_interleave(as_words(stage2[:]), wm_sb[1, 0][:])
-        pick_into(0, held("x_g0", [P, B * N], BF16, over="dzt_bf00")[:])
+        pick_into(0, held("x_g0", [P, B * N], BF16, over="q_a")[:])
         gather_x(0, 0, B * N, scalar_copy)
         multiply_dx(0, 2, 6)
         turn_x(0, 7)
@@ -351,7 +359,7 @@ def tile_attend_gex_wx_kernel(tc, xT, dyT, ts, wm, offs, out_0, out_1):
         gather_x(1, 0, N, scalar_copy)
         gather_x(1, N, B * N, scalar_copy)
         turn_x(1, 0)
-        xt01 = held("xt01", [P, 2 * WIDE], BF16)
+        xt01 = held("xt01", [P, 2 * WIDE], BF16, over="x1")
         copy_out_x(0, xt01[:, :WIDE])
         copy_out_dx(0, 2, share("dx_sb02", across="wm10"))
         copy_out_x(1, xt01[:, WIDE:])
@@ -369,11 +377,11 @@ def tile_attend_gex_wx_kernel(tc, xT, dyT, ts, wm, offs, out_0, out_1):
         turn_x(2, 4)
 
         scatter(0, 2)
-        store_gw(0, 0, over="dy1")
-        copy_out_dx(1, 0, share("dx_sb10"))
+        store_gw(0, 0, over="x2")
+        copy_out_dx(1, 0, share("dx_sb10", over="x2", skip=PLANE))
         multiply_dx(1, 1, 6)
         multiply_dx(1, 2, 0)
-        store_gw(1, 0, over="dy1", skip=PLANE)
+        store_gw(1, 0, over="x2", skip=2 * PLANE)
         copy_out_dx(1, 1, share("dx_sb11"))
         copy_out_dx(1, 2, share("dx_sb12"))
         scalar_scatter(1, 1, 0, dx_sb[1, 1, 0][:, :HALF_N])
@@ -396,8 +404,8 @@ def tile_attend_gex_wx_kernel(tc, xT, dyT, ts, wm, offs, out_0, out_1):
         store_window(2)
 
         scatter(0, 3)
-        store_gw(0, 1, nc.scalar, over="dy1", skip=2 * PLANE)
-        store_gw(1, 1, nc.scalar, over="dy1", skip=3 * PLANE)
+        store_gw(0, 1, nc.scalar, over="x3")
+        store_gw(1, 1, nc.scalar, over="x3", skip=PLANE)
         xt3 = held("xt3", [P, WIDE], BF16)
         copy_out_x(3, xt3[:])
         copy_out_dx(1, 3, share("dx_sb13", over="x_g3"))

@@ -249,13 +249,14 @@ def tile_attend_gex_wx_kernel(tc, xT, dyT, ts, wm, offs, out_0, out_1):
             nc.gpsimd.memset(windows[j][:].bitcast(I32), 0)
 
         PLANE = 4 * N
-        room("late", 5 * PLANE + 4 * T)
-        load_dy(0, over="late", skip=5 * PLANE)
+        room("late", 4 * T)
+        load_dy(0, over="late")
         load_dy(1)
         load_dy(2)
         load_dy(3)
-        room("wm0", 4 * PLANE)
-        load_wm(0, 0, 2, over="wm0")
+        room("wm0", 5 * PLANE)
+        load_wm(0, 0, 1, over="wm0")
+        load_wm(0, 1, 1)
         load_wm(0, 2, 2)
         room("x0_wm1", 2 * 4 * T + 2 * PLANE)
         load_x(0, over="x0_wm1")
@@ -266,120 +267,122 @@ def tile_attend_gex_wx_kernel(tc, xT, dyT, ts, wm, offs, out_0, out_1):
 
         for b in range(B):
             ts_g[b] = held(f"ts_g{b}", [P, N], F32)[:]
-        start_of["dzn1"] = start_of["wm0"] + 3 * PLANE // 2
+        start_of["dzn1"] = start_of["wm0"] + PLANE // 2
         room("plain0", 2 * PLANE)
-        columns = [held(f"ts_cols{k}", [P, 2], F32)[:] for k in range(2)]
-        columns.append(held("ts_cols2", [P, 2], F32, over="plain0")[:])
-        columns.append(held("ts_cols3", [P, 2], F32, over="dzn1", skip=PLANE)[:])
+        columns = [held(f"ts_cols{k}", [P, 2], F32, **({"over": "plain0"} if k == 1 else {}))[:] for k in range(2 * B)]
         quarters = [(b, h * HALF_N) for b in range(B) for h in range(2)]
         rows = [ts_gather(b, first, HALF_N, vector_copy) for b, first in quarters]
-        cols = ts_down(rows[0], 0, 0, nc.scalar.copy)
-        for k, (b, first) in enumerate(quarters):
-            ahead = ts_down(rows[k + 1], k + 1, (k + 1) % 2, nc.scalar.copy) if k + 1 < len(quarters) else None
-            ts_across(cols, b, first, 2 + k, vector_copy if b == 0 else nc.scalar.copy)
-            cols = ahead
+        ts_down(rows[0], 0, 0, nc.scalar.copy)
+        ts_down(rows[1], 1, 1, nc.scalar.copy)
+        ts_across(columns[0], *quarters[0], 2, vector_copy)
+        ts_down(rows[2], 2, 0, nc.scalar.copy)
+        ts_across(columns[1], *quarters[1], 3, vector_copy)
+        plain01 = held("plain01", [P, 2, N], F32, over="plain0")
+        scalar_copy(plain01[:, 0, :], dy_sb[0][:].indirect(entries(1)))
+        ts_down(rows[3], 3, 1, nc.scalar.copy)
+        ts_across(columns[2], *quarters[2], 4, nc.scalar.copy)
+        ts_across(columns[3], *quarters[3], 5, nc.scalar.copy)
 
-        early = held("early", [P, 2, N], F32)
-        dz[0, 0], dz[1, 0] = early[:, 0, :], early[:, 1, :]
+        dz0 = held("dz0", [P, PACK, N], F32)
+        for t in range(PACK):
+            dz[t, 0] = dz0[:, t, :]
         dzt_bf[0, 0] = as_turned(held("dzt_bf00", [P, WIDE], BF16)[:])
         dzt_bf1 = held("dzt_bf1", [P, 2 * WIDE], BF16)[:]
         for h in range(2):
             dzt_bf[1, h] = as_turned(dzt_bf1[:, h * WIDE : (h + 1) * WIDE])
-        plain01 = held("plain01", [P, 2, N], F32, over="plain0")
-        plain0, plain1 = plain01[:, 0, :], plain01[:, 1, :]
-        plain2 = held("plain2", [P, N], F32, over="ts_cols3")[:]
-
+        plain3 = held("plain3", [P, N], F32)
+        dzt_q[0] = planes("dzt_q0", DV)
 
         for first in (0, HALF_N):
             gather_dz(0, 0, first, HALF_N)
         turn_dz(0, 0, 6)
-        scalar_copy(plain0, dy_sb[0][:].indirect(entries(1)))
         gather_dz(1, 0)
         turn_dz(1, 0, 7)
-        late = held("late", [P, 9 * N], F32, over="late")
-        rows = late[:, : 2 * PACK * N].rearrange("p (r e n) -> p e r n", e=2, n=N)
-        dz1, last_pair = rows[:, 0], rows[:, 1, :2]
-        dz[2, 0], dz[3, 0] = last_pair[:, 0, :], last_pair[:, 1, :]
-        stage0 = late[:, 11 * HALF_N : 13 * HALF_N].bitcast(BF16)
-        dzn_bf0 = late[:, 13 * HALF_N : 17 * HALF_N].bitcast(BF16)
+        late = held("late", [P, PACK * N], F32, over="late")
+        dz1 = late[:].rearrange("p (t n) -> p t n", n=N)
+        dzn_bf0 = late[:, 2 * N :].bitcast(BF16)
         for t in range(PACK):
             dz[t, 1] = dz1[:, t, :]
-        nc.vector.tensor_tensor(dz[0, 1], plain0, ts_g[1], MULT)
-        scalar_copy(plain1, dy_sb[1][:].indirect(entries(1)))
-        scalar_copy(plain2, dy_sb[2][:].indirect(entries(1)))
+        nc.vector.tensor_tensor(dz[0, 1], plain01[:, 0, :], ts_g[1], MULT)
+        scalar_copy(plain01[:, 1, :], dy_sb[1][:].indirect(entries(1)))
         turn_dz(0, 1, 0)
         gather_dz(2, 0)
-        nc.vector.tensor_tensor(dz[1, 1], plain1, ts_g[1], MULT)
+        nc.vector.tensor_tensor(dz[1, 1], plain01[:, 1, :], ts_g[1], MULT)
         copy_out_dz(0, 0)
         copy_out_dz(1, 0)
-        scalar_pair(as_words(dzn_bf0)[:, :, 0:2], early[:])
         turn_dz(2, 0, 2)
         turn_dz(1, 1, 1)
-        nc.vector.tensor_tensor(dz[2, 1], plain2, ts_g[1], MULT)
+        quantize_dzt(0, 0)
         gather_dz(3, 0)
+        scalar_pair(as_words(dzn_bf0)[:, :, 0:2], dz0[:, 0:2, :])
+        scalar_copy(plain3[:], dy_sb[3][:].indirect(entries(1)))
         copy_out_dz(0, 1)
         copy_out_dz(1, 1)
-        turn_dz(2, 1, 3)
         turn_dz(3, 0, 4)
-        dzt_q[0] = planes("dzt_q0", DV, over="ts_g0")
-        quantize_dzt(0, 0)
-        vector_pair(as_words(dzn_bf0)[:, :, 2:4], last_pair)
+        vector_pair(as_words(dzn_bf0)[:, :, 2:4], dz0[:, 2:4, :])
+        stage0 = held("stage0", [P, WIDE // 2], BF16)[:]
         vector_interleave(as_words(stage0), wm_sb[0, 0][:])
-        quantize_dzn(0, dzn_bf0, over="wm00", skip=PLANE // 2)
+        quantize_dzn(0, dzn_bf0)
         room("q_a", PLANE)
-        quantize_e4m3("q_a", stage0, [(0, 0), (0, 1)], over="q_a")
-        stage1 = held("stage1", [P, WIDE], BF16, over="plain2")[:]
-        scalar_interleave(as_words(stage1), wm_sb[0, 2][:])
+        quantize_e4m3("q_a", stage0, [(0, 0)], over="q_a")
+        stage1 = held("stage1", [P, 3 * WIDE // 2], BF16, over="dzn1", skip=PLANE)[:]
+        scalar_interleave(as_words(stage1[:, WIDE // 2 :]), wm_sb[0, 2][:])
         dzt_bf[0, 1] = as_turned(held("dzt_bf01", [P, WIDE], BF16, over="dzn1")[:])
         copy_out_dz(2, 0)
         copy_out_dz(3, 0)
         multiply_dx(0, 0, 5)
-        multiply_dx(0, 1, 6)
-        gather_dz(3, 1)
-        quantize_e4m3("q_b", stage1, [(0, 2), (0, 3)], over="dy3")
+        vector_interleave(as_words(stage1[:, : WIDE // 2]), wm_sb[0, 1][:])
+        gather_dz(2, 1)
+        nc.vector.tensor_tensor(dz[3, 1], plain3[:], ts_g[1], MULT)
+        quantize_e4m3("q_b", stage1, [(0, 1), (0, 2), (0, 3)])
         quantize_dzt(0, 1)
         copy_out_dx(0, 0, share("dx_sb00", over="wm10", skip=4 * T))
-        copy_out_dz(2, 1)
-        copy_out_dx(0, 1, share("dx_sb01"))
-        turn_dz(3, 1, 5)
+        multiply_dx(0, 1, 6)
+        turn_dz(2, 1, 5)
 
         scatter(0, 0)
         dzn_bf1 = held("dzn_bf1", [P, 2 * WIDE], BF16, over="dzn1")[:]
         gpsimd_interleave(as_words(dzn_bf1), dz1)
-        stage2 = held("stage2", [P, 2 * WIDE], BF16, over="late")
+        stage2 = held("stage2", [P, 2 * WIDE], BF16, over="dzn1", skip=2 * PLANE)
         gpsimd_interleave(as_words(stage2[:]), wm_sb[1, 0][:])
         pick_into(0, held("x_g0", [P, B * N], BF16, over="q_a")[:])
         gather_x(0, 0, B * N, scalar_copy)
-        multiply_dx(0, 2, 6)
+        copy_out_dx(0, 1, share("dx_sb01"))
+        turn_dz(3, 1, 6)
+        multiply_dx(0, 2, 3)
         turn_x(0, 7)
-        copy_out_dz(3, 1)
+        copy_out_dz(2, 1)
         scatter(0, 1)
         pick_into(1, held("x_g10", [P, N], BF16, over="x0", skip=7 * PLANE // 2)[:], (0,))
         pick_into(1, held("x_g11", [P, N], BF16, over="dx_sb00", skip=PLANE // 2)[:], (1,))
         gather_x(1, 0, N, scalar_copy)
+        copy_out_dz(3, 1)
         gather_x(1, N, B * N, scalar_copy)
         turn_x(1, 0)
-        xt01 = held("xt01", [P, 2 * WIDE], BF16, over="x1")
-        copy_out_x(0, xt01[:, :WIDE])
-        copy_out_dx(0, 2, share("dx_sb02", across="wm10"))
-        copy_out_x(1, xt01[:, WIDE:])
-        pick_into(2, held("x_g2", [P, B * N], BF16, over="x_g11", skip=-3 * PLANE // 4)[:])
-        gather_x(2, 0, B * N, scalar_copy)
-        quantize_dzn(1, dzn_bf1, over="wm10", skip=PLANE // 2)
-        quantize_e4m3("q_x0", xt01[:, :WIDE], [], 0, over="wm10", skip=5 * PLANE // 2)
+        xt0 = held("xt0", [P, WIDE], BF16, over="x_g10", skip=-3 * PLANE // 4)
+        copy_out_x(0, xt0[:])
+        copy_out_dx(0, 2, share("dx_sb02", over="wm10", skip=-PLANE // 4))
+        xt1 = held("xt1", [P, WIDE], BF16)
+        copy_out_x(1, xt1[:])
+        pick_into(2, held("x_g20", [P, N], BF16, over="x_g11")[:], (0,))
+        pick_into(2, held("x_g21", [P, N], BF16)[:], (1,))
+        gather_x(2, 0, N, scalar_copy)
+        gather_x(2, N, B * N, scalar_copy)
+        quantize_dzn(1, dzn_bf1, over="wm10", skip=3 * PLANE // 4)
+        quantize_e4m3("q_x0", xt0[:], [], 0, over="wm10", skip=11 * PLANE // 4)
         quantize_e4m3("q_c", stage2[:], [(1, j) for j in range(BLOCKS)])
-        quantize_e4m3("q_x1", xt01[:, WIDE:], [], 1, over="wm10", skip=3 * PLANE)
-        dzt_q[1] = planes("dzt_q1", DV, over="wm10", skip=3 * PLANE // 2)
+        quantize_e4m3("q_x1", xt1[:], [], 1, over="wm10", skip=13 * PLANE // 4)
+        dzt_q[1] = planes("dzt_q1", DV, over="wm10", skip=7 * PLANE // 4)
         quantize(dzt_q[1], dzt_bf1, E5M2)
-        multiply_gw(0, 0, 6)
+        multiply_gw(0, 0, 3)
         multiply_dx(1, 0, 0)
         multiply_gw(1, 0, 7)
         turn_x(2, 4)
 
         scatter(0, 2)
-        store_gw(0, 0, over="x2")
+        store_gw(0, 0, over="x_g20")
         copy_out_dx(1, 0, share("dx_sb10", over="x2", skip=PLANE))
-        multiply_dx(1, 1, 6)
+        multiply_dx(1, 1, 3)
         multiply_dx(1, 2, 0)
         store_gw(1, 0, over="x2", skip=2 * PLANE)
         copy_out_dx(1, 1, share("dx_sb11"))
@@ -391,26 +394,27 @@ def tile_attend_gex_wx_kernel(tc, xT, dyT, ts, wm, offs, out_0, out_1):
         scatter(1, 0)
         store_window(0)
         scatter(1, 2)
-        multiply_dx(0, 3, 6)
+        multiply_dx(0, 3, 3)
         copy_out_dx(0, 3, share("dx_sb03"))
         store_window(1, nc.scalar)
         pick_into(3, held("x_g3", [P, B * N], BF16, over="dx_sb11")[:])
-        gather_x(3, 0, B * N, scalar_copy)
+        gather_x(3, 0, N, scalar_copy)
+        gather_x(3, N, B * N, scalar_copy)
         multiply_gw(0, 1, 4)
-        multiply_gw(1, 1, 6)
+        multiply_gw(1, 1, 3)
         turn_x(3, 2)
         multiply_dx(1, 3, 7)
         quantize_e4m3("q_x2", xt2[:], [], 2)
         store_window(2)
 
         scatter(0, 3)
-        store_gw(0, 1, nc.scalar, over="x3")
-        store_gw(1, 1, nc.scalar, over="x3", skip=PLANE)
+        store_gw(0, 1, over="dy1")
+        store_gw(1, 1, over="dy1", skip=PLANE)
         xt3 = held("xt3", [P, WIDE], BF16)
         copy_out_x(3, xt3[:])
         copy_out_dx(1, 3, share("dx_sb13", over="x_g3"))
         multiply_gw(2, 0, 4)
-        multiply_gw(2, 1, 6)
+        multiply_gw(2, 1, 3)
         quantize_e4m3("q_x3", xt3[:], [], 3)
         multiply_gw(3, 0, 5)
         multiply_gw(3, 1, 1)

@@ -149,6 +149,19 @@ def tile_attend_gex_wx_kernel(tc, xT, dyT, ts, wm, offs, out_0, out_1):
         def copy_out_dz(t, b, copy=scalar_copy):
             copy(dzt_bf[b, t // 2][:, t % 2], turned[t, b][:].rearrange("s k p -> s p k"))
 
+        def turn_words(h, number):
+            turned[h] = bank(f"turned_words{h}", [P, 2, 2, P], number)
+            for e in range(2):
+                words = dz1[:, 2 * h + e, :].bitcast(F32)
+                for u in range(2):
+                    nc.tensor.transpose(turned[h][:, e, u, :], words[:, u:HALF_N:2], ident[:])
+
+        def copy_out_words(h):
+            nc.scalar.copy(
+                out=dzt_bf1[:, h * WIDE : (h + 1) * WIDE].bitcast(F32).rearrange("s (e p u) -> s e p u", e=2, u=2),
+                in_=turned[h][:].rearrange("s e u p -> s e p u"),
+            )
+
         def as_turned(part):
             return part.rearrange("s (t p k) -> s t p k", t=2, k=PACK)
 
@@ -257,19 +270,21 @@ def tile_attend_gex_wx_kernel(tc, xT, dyT, ts, wm, offs, out_0, out_1):
         room("wm0", 5 * PLANE)
         load_wm(0, 0, 1, over="wm0")
         load_wm(0, 1, 1)
-        load_wm(0, 2, 2)
-        room("x0_wm1", 2 * 4 * T + 2 * PLANE)
+        room("wm02", 4 * PLANE)
+        load_wm(0, 2, 2, over="wm02")
+        room("x0_wm1", 2 * 4 * T)
         load_x(0, over="x0_wm1")
-        load_x(1)
         load_wm(1, 0, BLOCKS, over="x0_wm1", skip=4 * T)
+        load_x(1)
         load_x(2)
         load_x(3)
 
         for b in range(B):
             ts_g[b] = held(f"ts_g{b}", [P, N], F32)[:]
-        start_of["dzn1"] = start_of["wm0"] + PLANE // 2
+        start_of["dzn1"] = start_of["wm0"] + PLANE
         room("plain0", 2 * PLANE)
-        columns = [held(f"ts_cols{k}", [P, 2], F32, **({"over": "plain0"} if k == 1 else {}))[:] for k in range(2 * B)]
+        room("plain2", 2 * PLANE)
+        columns = [held(f"ts_cols{k}", [P, 2], F32, **place)[:] for k, place in enumerate(({}, {"over": "plain0"}, {}, {"over": "plain2"}))]
         quarters = [(b, h * HALF_N) for b in range(B) for h in range(2)]
         rows = [ts_gather(b, first, HALF_N, vector_copy) for b, first in quarters]
         ts_down(rows[0], 0, 0, nc.scalar.copy)
@@ -286,81 +301,77 @@ def tile_attend_gex_wx_kernel(tc, xT, dyT, ts, wm, offs, out_0, out_1):
         dz0 = held("dz0", [P, PACK, N], F32)
         for t in range(PACK):
             dz[t, 0] = dz0[:, t, :]
-        dzt_bf[0, 0] = as_turned(held("dzt_bf00", [P, WIDE], BF16)[:])
+        three = held("dzt_bf0", [P, 3, P, PACK], BF16)
+        dzt_bf[0, 0] = three[:, :2]
+        room("stage0", PLANE)
         dzt_bf1 = held("dzt_bf1", [P, 2 * WIDE], BF16)[:]
-        for h in range(2):
-            dzt_bf[1, h] = as_turned(dzt_bf1[:, h * WIDE : (h + 1) * WIDE])
-        plain3 = held("plain3", [P, N], F32)
-        dzt_q[0] = planes("dzt_q0", DV)
+        plain23 = held("plain23", [P, 2, N], F32, over="plain2")
+        plain2, plain3 = plain23[:, 0, :], plain23[:, 1, :]
 
         for first in (0, HALF_N):
             gather_dz(0, 0, first, HALF_N)
         turn_dz(0, 0, 6)
         gather_dz(1, 0)
         turn_dz(1, 0, 7)
-        late = held("late", [P, PACK * N], F32, over="late")
-        dz1 = late[:].rearrange("p (t n) -> p t n", n=N)
-        dzn_bf0 = late[:, 2 * N :].bitcast(BF16)
-        for t in range(PACK):
-            dz[t, 1] = dz1[:, t, :]
-        nc.vector.tensor_tensor(dz[0, 1], plain01[:, 0, :], ts_g[1], MULT)
+        late = held("late", [P, 7 * N], BF16, over="late")
+        dz1 = late[:, : PACK * N].rearrange("p (t n) -> p t n", n=N)
+        dzn_bf0 = late[:, 3 * N :]
+        nc.vector.tensor_tensor(dz1[:, 0, :], plain01[:, 0, :], ts_g[1], MULT)
         scalar_copy(plain01[:, 1, :], dy_sb[1][:].indirect(entries(1)))
-        turn_dz(0, 1, 0)
         gather_dz(2, 0)
-        nc.vector.tensor_tensor(dz[1, 1], plain01[:, 1, :], ts_g[1], MULT)
+        scalar_copy(plain2, dy_sb[2][:].indirect(entries(1)))
+        nc.vector.tensor_tensor(dz1[:, 1, :], plain01[:, 1, :], ts_g[1], MULT)
         copy_out_dz(0, 0)
         copy_out_dz(1, 0)
         turn_dz(2, 0, 2)
-        turn_dz(1, 1, 1)
-        quantize_dzt(0, 0)
+        nc.vector.tensor_tensor(dz1[:, 2, :], plain2, ts_g[1], MULT)
         gather_dz(3, 0)
-        scalar_pair(as_words(dzn_bf0)[:, :, 0:2], dz0[:, 0:2, :])
-        scalar_copy(plain3[:], dy_sb[3][:].indirect(entries(1)))
-        copy_out_dz(0, 1)
-        copy_out_dz(1, 1)
+        scalar_copy(plain3, dy_sb[3][:].indirect(entries(1)))
+        turn_words(0, 0)
         turn_dz(3, 0, 4)
-        vector_pair(as_words(dzn_bf0)[:, :, 2:4], dz0[:, 2:4, :])
-        stage0 = held("stage0", [P, WIDE // 2], BF16)[:]
+        stage0 = held("stage0", [P, WIDE // 2], BF16, over="stage0")[:]
         vector_interleave(as_words(stage0), wm_sb[0, 0][:])
+        vector_interleave(as_words(dzn_bf0), dz0[:])
+        room("q_a", 2 * PLANE)
+        quantize_e4m3("q_a", stage0, [(0, 0)], over="q_a", skip=7 * PLANE // 8)
         quantize_dzn(0, dzn_bf0)
-        room("q_a", PLANE)
-        quantize_e4m3("q_a", stage0, [(0, 0)], over="q_a")
-        stage1 = held("stage1", [P, 3 * WIDE // 2], BF16, over="dzn1", skip=PLANE)[:]
+        scalar_copy(three[:, 2], turned[2, 0][:].rearrange("s k p -> s p k"))
+        stage1 = held("stage1", [P, 3 * WIDE // 2], BF16, over="wm02", skip=2 * PLANE)[:]
+        scalar_interleave(as_words(stage1[:, : WIDE // 2]), wm_sb[0, 1][:])
+        copy_out_words(0)
         scalar_interleave(as_words(stage1[:, WIDE // 2 :]), wm_sb[0, 2][:])
-        dzt_bf[0, 1] = as_turned(held("dzt_bf01", [P, WIDE], BF16, over="dzn1")[:])
-        copy_out_dz(2, 0)
-        copy_out_dz(3, 0)
+        fourth = held("dzt_bf03", [P, P, PACK], BF16, over="wm02", skip=3 * PLANE // 2)
+        scalar_copy(fourth[:], turned[3, 0][:].rearrange("s k p -> s p k"))
         multiply_dx(0, 0, 5)
-        vector_interleave(as_words(stage1[:, : WIDE // 2]), wm_sb[0, 1][:])
-        gather_dz(2, 1)
-        nc.vector.tensor_tensor(dz[3, 1], plain3[:], ts_g[1], MULT)
+        dzt_q[0] = planes("dzt_q0", DV, over="stage0")
+        quantize_dzt(0, 0)
+        quantize(dzt_q[0], three[:, 2].rearrange("s p k -> s (p k)"), E5M2, slice(2 * P, 3 * P))
+        nc.vector.tensor_tensor(dz1[:, 3, :], plain3, ts_g[1], MULT)
         quantize_e4m3("q_b", stage1, [(0, 1), (0, 2), (0, 3)])
-        quantize_dzt(0, 1)
-        copy_out_dx(0, 0, share("dx_sb00", over="wm10", skip=4 * T))
+        quantize(dzt_q[0], fourth[:].rearrange("s p k -> s (p k)"), E5M2, slice(3 * P, 4 * P))
+        copy_out_dx(0, 0, share("dx_sb00", over="wm02", skip=PLANE // 2))
         multiply_dx(0, 1, 6)
-        turn_dz(2, 1, 5)
+        turn_words(1, 5)
 
         scatter(0, 0)
-        dzn_bf1 = held("dzn_bf1", [P, 2 * WIDE], BF16, over="dzn1")[:]
+        dzn_bf1 = held("dzn_bf1", [P, 2 * WIDE], BF16, over="dzt_bf03")[:]
         gpsimd_interleave(as_words(dzn_bf1), dz1)
-        stage2 = held("stage2", [P, 2 * WIDE], BF16, over="dzn1", skip=2 * PLANE)
+        stage2 = held("stage2", [P, 2 * WIDE], BF16)
         gpsimd_interleave(as_words(stage2[:]), wm_sb[1, 0][:])
-        pick_into(0, held("x_g0", [P, B * N], BF16, over="q_a")[:])
+        pick_into(0, held("x_g0", [P, B * N], BF16, over="q_a", skip=PLANE)[:])
         gather_x(0, 0, B * N, scalar_copy)
         copy_out_dx(0, 1, share("dx_sb01"))
-        turn_dz(3, 1, 6)
         multiply_dx(0, 2, 3)
         turn_x(0, 7)
-        copy_out_dz(2, 1)
+        copy_out_words(1)
+        xt0 = held("xt0", [P, WIDE], BF16)
+        copy_out_x(0, xt0[:])
         scatter(0, 1)
         pick_into(1, held("x_g10", [P, N], BF16, over="x0", skip=7 * PLANE // 2)[:], (0,))
-        pick_into(1, held("x_g11", [P, N], BF16, over="dx_sb00", skip=PLANE // 2)[:], (1,))
+        pick_into(1, held("x_g11", [P, N], BF16, over="dx_sb00")[:], (1,))
         gather_x(1, 0, N, scalar_copy)
-        copy_out_dz(3, 1)
         gather_x(1, N, B * N, scalar_copy)
         turn_x(1, 0)
-        xt0 = held("xt0", [P, WIDE], BF16, over="x_g10", skip=-3 * PLANE // 4)
-        copy_out_x(0, xt0[:])
         copy_out_dx(0, 2, share("dx_sb02", over="wm10", skip=-PLANE // 4))
         xt1 = held("xt1", [P, WIDE], BF16)
         copy_out_x(1, xt1[:])
@@ -371,21 +382,22 @@ def tile_attend_gex_wx_kernel(tc, xT, dyT, ts, wm, offs, out_0, out_1):
         quantize_dzn(1, dzn_bf1, over="wm10", skip=3 * PLANE // 4)
         quantize_e4m3("q_x0", xt0[:], [], 0, over="wm10", skip=11 * PLANE // 4)
         quantize_e4m3("q_c", stage2[:], [(1, j) for j in range(BLOCKS)])
-        quantize_e4m3("q_x1", xt1[:], [], 1, over="wm10", skip=13 * PLANE // 4)
         dzt_q[1] = planes("dzt_q1", DV, over="wm10", skip=7 * PLANE // 4)
         quantize(dzt_q[1], dzt_bf1, E5M2)
         multiply_gw(0, 0, 3)
         multiply_dx(1, 0, 0)
-        multiply_gw(1, 0, 7)
+        multiply_gw(0, 1, 7)
         turn_x(2, 4)
 
         scatter(0, 2)
-        store_gw(0, 0, over="x_g20")
+        quantize_e4m3("q_x1", xt1[:], [], 1, over="wm10", skip=13 * PLANE // 4)
+        store_gw(0, 0, over="x_g20", skip=-PLANE // 2)
         copy_out_dx(1, 0, share("dx_sb10", over="x2", skip=PLANE))
         multiply_dx(1, 1, 3)
         multiply_dx(1, 2, 0)
-        store_gw(1, 0, over="x2", skip=2 * PLANE)
-        copy_out_dx(1, 1, share("dx_sb11"))
+        store_gw(0, 1, over="x2", skip=2 * PLANE)
+        room("fifth", 3 * PLANE)
+        copy_out_dx(1, 1, share("dx_sb11", over="fifth", skip=PLANE // 2))
         copy_out_dx(1, 2, share("dx_sb12"))
         scalar_scatter(1, 1, 0, dx_sb[1, 1, 0][:, :HALF_N])
         xt2 = held("xt2", [P, WIDE], BF16)
@@ -400,7 +412,7 @@ def tile_attend_gex_wx_kernel(tc, xT, dyT, ts, wm, offs, out_0, out_1):
         pick_into(3, held("x_g3", [P, B * N], BF16, over="dx_sb11")[:])
         gather_x(3, 0, N, scalar_copy)
         gather_x(3, N, B * N, scalar_copy)
-        multiply_gw(0, 1, 4)
+        multiply_gw(1, 0, 4)
         multiply_gw(1, 1, 3)
         turn_x(3, 2)
         multiply_dx(1, 3, 7)
@@ -408,11 +420,11 @@ def tile_attend_gex_wx_kernel(tc, xT, dyT, ts, wm, offs, out_0, out_1):
         store_window(2)
 
         scatter(0, 3)
-        store_gw(0, 1, over="dy1")
+        store_gw(1, 0, over="dy1")
         store_gw(1, 1, over="dy1", skip=PLANE)
         xt3 = held("xt3", [P, WIDE], BF16)
         copy_out_x(3, xt3[:])
-        copy_out_dx(1, 3, share("dx_sb13", over="x_g3"))
+        copy_out_dx(1, 3, share("dx_sb13", over="x_g3", skip=-PLANE // 2))
         multiply_gw(2, 0, 4)
         multiply_gw(2, 1, 3)
         quantize_e4m3("q_x3", xt3[:], [], 3)

@@ -357,7 +357,7 @@ def tile_attend_gex_wx_kernel(tc, xT, dyT, ts, wm, offs, out_0, out_1):
         dzn_bf1 = held("dzn_bf1", [P, 2 * WIDE], BF16, over="dzt_bf03")[:]
         gpsimd_interleave(as_words(dzn_bf1), dz1)
         stage2 = held("stage2", [P, 2 * WIDE], BF16)
-        gpsimd_interleave(as_words(stage2[:]), wm_sb[1, 0][:])
+        nc.gpsimd.tensor_copy(as_words(stage2[:]), wm_sb[1, 0][:].rearrange("p t c -> p c t"))
         pick_into(0, held("x_g0", [P, B * N], BF16, over="q_a", skip=PLANE)[:])
         gather_x(0, 0, B * N, scalar_copy)
         copy_out_dx(0, 1, share("dx_sb01"))

@@ -23,11 +23,13 @@ P = 128
 PACK = 4
 BLOCKS = D // P
 HALF_N = N // 2
-LIST_COLS = N // 16
+ROWS_OF_LIST = 16
 LINE = 4
 LAST = P - 1
-THIRD = 384
-WIDE = 2 * P * PACK
+ONE = P * PACK
+TWO = 2 * ONE
+KIB = 1024
+ALIGN = 64
 
 
 def tile_attend_gex_wx_kernel(tc, xT, dyT, ts, wm, offs, out_0, out_1):
@@ -36,46 +38,39 @@ def tile_attend_gex_wx_kernel(tc, xT, dyT, ts, wm, offs, out_0, out_1):
     with ExitStack() as ctx:
         keep = ctx.enter_context(tc.tile_pool(name="keep", bufs=1))
         psum = ctx.enter_context(tc.psum_pool(name="psum", bufs=1))
-
         shared = ctx.enter_context(tc.tile_pool(name="shared", bufs=1))
         start_of = {"end": 0}
         size_of = {F32: 4, U32: 4, BF16: 2}
-
-        def held(name, shape, dtype, over=None, skip=0, across=None):
-            size = size_of[dtype] * math.prod(shape[1:])
-            if over:
-                start_of[name] = start_of[over] + skip
-            elif across:
-                start_of[name] = start_of[across] - size // 2
-            else:
-                start_of[name] = start_of["end"]
-                start_of["end"] = start_of["end"] + -(-size // 64) * 64
-            return shared.tile(shape, dtype, name=name, offset=start_of[name], align_bytes=64)
 
         def room(name, size):
             start_of[name] = start_of["end"]
             start_of["end"] = start_of["end"] + size
 
+        def held(name, shape, dtype, over=None, skip=0):
+            if over:
+                start_of[name] = start_of[over] + skip
+            else:
+                size = size_of[dtype] * math.prod(shape[1:])
+                room(name, -(-size // ALIGN) * ALIGN)
+            return shared.tile(shape, dtype, name=name, offset=start_of[name], align_bytes=ALIGN)
+
         def bank(name, shape, number):
             return psum.tile(shape, F32, name=name, tag=f"bank{number}")
 
-        offsets = keep.tile([P, B * LIST_COLS], U16, name="offsets")
+        offsets = keep.tile([P, B * N // ROWS_OF_LIST], U16, name="offsets")
         ts_sb = held("ts_sb", [P, T], F32)
-        dy_sb, wm_sb, x_sb, picked, x_bank, x_q = {}, {}, {}, {}, {}, {}
-        ts_g, dz, turned, dzt_bf, dzt_q, dzn_q, wm_q, product, dx_sb, gw, windows = {}, {}, {}, {}, {}, {}, {}, {}, {}, {}, {}
+        dy_sb, wm_sb, x_sb, windows = {}, {}, {}, {}
+        turned, picked, x_bank, product, gw, shares = {}, {}, {}, {}, {}, {}
+        dzt_q, dzn_q, wm_q, x_q = {}, {}, {}, {}
 
-        def entries(b, first=0, width=N):
-            start = b * N + first
-            return offsets[:, start // 16 : (start + width) // 16]
+        def entries(first, count):
+            return offsets[:, first // ROWS_OF_LIST : (first + count) // ROWS_OF_LIST]
 
-        def vector_copy(out, in_):
-            nc.vector.tensor_copy(out, in_)
-
-        def scalar_copy(out, in_):
+        def scalar_move(out, in_):
             nc.scalar.activation(out, in_, COPY)
 
-        def load_dy(t, **place):
-            dy_sb[t] = held(f"dy{t}", [P, T], F32, **place)
+        def load_dy(t):
+            dy_sb[t] = held(f"dy{t}", [P, T], F32)
             nc.sync.dma_start(out=dy_sb[t][:], in_=dyT.rearrange("(p t) c -> t p c", t=PACK)[t])
 
         def load_wm(b, first, count, **place):
@@ -83,115 +78,127 @@ def tile_attend_gex_wx_kernel(tc, xT, dyT, ts, wm, offs, out_0, out_1):
             rows = wm[b].rearrange("(p t) d -> p t d", t=PACK)
             nc.sync.dma_start(out=wm_sb[b, first][:], in_=rows[:, :, first * P : (first + count) * P])
 
-        def load_x(j, **place):
-            x_sb[j] = held(f"x{j}", [P, T], F32, **place)
+        def load_x(j):
+            x_sb[j] = held(f"x{j}", [P, T], F32)
             nc.sync.dma_start(out=x_sb[j][:], in_=xT[j * P : (j + 1) * P, :])
 
-        def planes(name, width, **place):
-            codes = held(name + "_codes", [P, width], U32, **place)
-            scales = keep.tile([P, width], U8, name=name + "_scales", align_bytes=64)
+        def quantised(name, width, **place):
+            codes = held(name, [P, width], U32, **place)
+            scales = keep.tile([P, width], U8, name=name + "_scales", align_bytes=ALIGN)
             return codes, scales
 
         def quantize(dst, src, fmt, cols=slice(None)):
             nc.vector.quantize_mx(out=dst[0][:, cols].bitcast(fmt), scales=dst[1][:, cols], in_=src)
 
-        def vector_interleave(dst, src):
-            nc.vector.tensor_copy(
-                out=dst.rearrange("p (c i) t -> p c t i", i=LINE), in_=src.rearrange("p t (c i) -> p c t i", i=LINE)
+        def quantize_wm(name, src, b, blocks, **place):
+            dst = quantised(name, len(blocks) * P, **place)
+            quantize(dst, src, E4M3)
+            for k, j in enumerate(blocks):
+                wm_q[b, j] = dst, slice(k * P, (k + 1) * P)
+
+        def quantize_x(j, src, **place):
+            x_q[j] = quantised(f"x_q{j}", B * P, **place)
+            quantize(x_q[j], src, E4M3)
+
+        def quantize_dzn(b, src, **place):
+            dzn_q[b] = quantised(f"dzn_q{b}", N, **place)
+            quantize(dzn_q[b], src, E5M2)
+
+        def quantize_turned(src, first, count=1):
+            quantize(dzt_q[0], src, E5M2, slice(first * P, (first + count) * P))
+
+        def interleave(copy, dst, src):
+            words = dst.rearrange("p (c t) -> p c t", t=PACK)
+            copy(
+                out=words.rearrange("p (c i) t -> p c t i", i=LINE),
+                in_=src.rearrange("p t (c i) -> p c t i", i=LINE),
             )
-
-        def scalar_interleave(dst, src):
-            nc.scalar.copy(
-                out=dst.rearrange("p (c i) t -> p c t i", i=LINE), in_=src.rearrange("p t (c i) -> p c t i", i=LINE)
-            )
-
-        def vector_pair(dst, src):
-            nc.vector.tensor_copy(out=dst, in_=src.rearrange("p t i -> p i t"))
-
-        def scalar_pair(dst, src):
-            nc.scalar.copy(out=dst, in_=src.rearrange("p t i -> p i t"))
 
         def gpsimd_interleave(dst, src):
             nc.gpsimd.tensor_scalar(
-                out=dst, in0=src.rearrange("p t c -> p c t"), scalar1=1.0, scalar2=0.0, op0=MULT, op1=ADD
+                out=dst.rearrange("p (c t) -> p c t", t=PACK),
+                in0=src.rearrange("p t c -> p c t"),
+                scalar1=1.0,
+                scalar2=0.0,
+                op0=MULT,
+                op1=ADD,
             )
 
-        def ts_gather(b, first, width, copy):
-            row = held(f"ts_row{b}_{first}", [P, width], F32)
-            copy(row[:], ts_sb[:].indirect(entries(b, first, width)))
+        def gpsimd_words(dst, src):
+            nc.gpsimd.tensor_copy(dst.rearrange("p (c t) -> p c t", t=PACK), src.rearrange("p t c -> p c t"))
+
+        def ts_gather(k):
+            row = held(f"ts_row{k}", [P, HALF_N], F32)
+            nc.vector.tensor_copy(row[:], ts_sb[:].indirect(entries(k * HALF_N, HALF_N)))
             return row
 
-        def ts_down(row, k, number, copy):
-            count = row.shape[1] // P
-            down = bank(f"down{k}", [P, count, P], number)
-            for q in range(count):
-                nc.tensor.transpose(down[:, q, :], row[:, q * P : (q + 1) * P], ident[:])
-            copy(columns[k], down[:, :, LAST])
-            return columns[k]
+        def ts_down(k, number):
+            down = bank(f"down{k}", [P, 2, P], number)
+            for q in range(2):
+                nc.tensor.transpose(down[:, q, :], ts_rows[k][:, q * P : (q + 1) * P], ident[:])
+            nc.scalar.copy(ts_cols[k][:], down[:, :, LAST])
 
-        def ts_across(cols, b, first, number, copy):
-            count = cols.shape[1]
-            across = bank(f"across{b}_{first}", [P, count, P], number)
-            for q in range(count):
-                nc.tensor.transpose(across[:, q, :], cols[:, q : q + 1].to_broadcast([P, P]), ident[:])
-            copy(ts_g[b][:, first : first + count * P], across[:].rearrange("p q s -> p (q s)"))
+        def ts_across(k, number, copy):
+            b, half = divmod(k, 2)
+            across = bank(f"across{k}", [P, 2, P], number)
+            for q in range(2):
+                nc.tensor.transpose(across[:, q, :], ts_cols[k][:, q : q + 1].to_broadcast([P, P]), ident[:])
+            copy(ts_g[b][:, half * HALF_N : (half + 1) * HALF_N], across[:].rearrange("p q s -> p (q s)"))
 
-        def gather_dz(t, b, first=0, width=N):
-            slots = slice(first, first + width)
-            window = dy_sb[t][:].indirect(entries(b, first, width))
-            nc.vector.tensor_tensor(dz[t, b][:, slots], window, ts_g[b][:, slots], MULT)
+        def gather_dz0(t, first=0, count=N):
+            slots = slice(first, first + count)
+            window = dy_sb[t][:].indirect(entries(first, count))
+            nc.vector.tensor_tensor(dz0[:, t, slots], window, ts_g[0][:, slots], MULT)
 
-        def turn_dz(t, b, number):
-            turned[t, b] = bank(f"turned{t}{b}", [P, PACK, P], number)
+        def gather_dy1(t, dst):
+            scalar_move(dst, dy_sb[t][:].indirect(entries(N, N)))
+
+        def multiply_dz1(t, src):
+            nc.vector.tensor_tensor(dz1[:, t, :], src, ts_g[1][:], MULT)
+
+        def turn_dz0(t, number):
+            turned[t] = bank(f"turned{t}", [P, PACK, P], number)
             for r in range(PACK):
-                nc.tensor.transpose(turned[t, b][:, r, :], dz[t, b][:, r:N:PACK], ident[:])
+                nc.tensor.transpose(turned[t][:, r, :], dz0[:, t, r:N:PACK], ident[:])
 
-        def copy_out_dz(t, b, copy=scalar_copy):
-            copy(dzt_bf[b, t // 2][:, t % 2], turned[t, b][:].rearrange("s k p -> s p k"))
+        def copy_out_dz0(t, dst):
+            scalar_move(dst, turned[t][:].rearrange("s r p -> s p r"))
 
-        def turn_words(h, number):
-            turned[h] = bank(f"turned_words{h}", [P, 2, 2, P], number)
-            for e in range(2):
-                words = dz1[:, 2 * h + e, :].bitcast(F32)
+        def turn_words(name, pair, number):
+            dst = bank(name, [P, 2, 2, P], number)
+            for e, values in enumerate(pair):
+                words = values.bitcast(F32)
                 for u in range(2):
-                    nc.tensor.transpose(turned[h][:, e, u, :], words[:, u:HALF_N:2], ident[:])
+                    nc.tensor.transpose(dst[:, e, u, :], words[:, u:HALF_N:2], ident[:])
+            return dst
 
-        def copy_out_words(h):
+        def copy_out_words(dst, src):
             nc.scalar.copy(
-                out=dzt_bf1[:, h * WIDE : (h + 1) * WIDE].bitcast(F32).rearrange("s (e p u) -> s e p u", e=2, u=2),
-                in_=turned[h][:].rearrange("s e u p -> s e p u"),
+                out=dst.bitcast(F32).rearrange("s (e p u) -> s e p u", e=2, u=2),
+                in_=src[:].rearrange("s e u p -> s e p u"),
             )
 
-        def as_turned(part):
-            return part.rearrange("s (t p k) -> s t p k", t=2, k=PACK)
+        def gather_x(j, dst, first):
+            count = dst.shape[1]
+            for k in range(count // N):
+                picked[j, first // N + k] = dst[:, k * N : (k + 1) * N]
+            scalar_move(dst, x_sb[j][:].indirect(entries(first, count)))
 
-        def as_words(part):
-            return part.rearrange("p (c t) -> p c t", t=PACK)
+        def turn_x(j, number):
+            x_bank[j] = turn_words(f"x_bank{j}", [picked[j, b] for b in range(B)], number)
 
-        def quantize_e4m3(name, part, blocks, x_block=None, **place):
-            width = len(blocks) * P + (0 if x_block is None else B * P)
-            dst = planes(name, width, **place)
-            quantize(dst, part, E4M3)
-            for k, block in enumerate(blocks):
-                wm_q[block] = dst, slice(k * P, (k + 1) * P)
-            if x_block is not None:
-                x_q[x_block] = dst, len(blocks) * P
+        def copy_out_x(j):
+            dst = held(f"xt{j}", [P, TWO], BF16)[:]
+            copy_out_words(dst, x_bank[j])
+            return dst
 
-        def quantize_dzt(b, h):
-            cols = slice(h * DV // 2, (h + 1) * DV // 2)
-            quantize(dzt_q[b], dzt_bf[b, h].rearrange("s t p k -> s (t p k)"), E5M2, cols)
-
-        def quantize_dzn(b, src, **place):
-            dzn_q[b] = planes(f"dzn_q{b}", N, **place)
-            quantize(dzn_q[b], src, E5M2)
-
-        def multiply(out, stationary, cols, moving):
+        def multiply(out, stationary, cols, moving, slots=slice(None)):
             nc.tensor.matmul_mx(
                 out=out[:],
                 lhsT=stationary[0][:, cols].bitcast(E4M3),
                 lhsT_scale=stationary[1][:, cols],
-                rhs=moving[0][:].bitcast(E5M2),
-                rhs_scale=moving[1][:],
+                rhs=moving[0][:, slots].bitcast(E5M2),
+                rhs_scale=moving[1][:, slots],
                 start=True,
                 stop=True,
             )
@@ -200,53 +207,27 @@ def tile_attend_gex_wx_kernel(tc, xT, dyT, ts, wm, offs, out_0, out_1):
             product[b, j] = bank(f"dx{b}{j}", [P, N], number)
             multiply(product[b, j], *wm_q[b, j], dzn_q[b])
 
-        def copy_out_dx(b, j, dst, first=0):
-            dx_sb[b, j, first] = dst
-            nc.scalar.copy(out=dst, in_=product[b, j][:, first : first + dst.shape[1]])
+        def copy_out_share(b, j, **place):
+            shares[b, j] = held(f"share{b}{j}", [P, N], F32, **place)
+            nc.scalar.copy(out=shares[b, j][:], in_=product[b, j][:])
 
-        def scatter(b, j, first=0):
-            values = dx_sb[b, j, first]
-            nc.vector.tensor_copy(windows[j][:].indirect(entries(b, first, values.shape[1])), values)
+        def scatter(b, j):
+            nc.vector.tensor_copy(windows[j][:].indirect(entries(b * N, N)), shares[b, j][:])
 
-        def scalar_scatter(b, j, first, values):
-            scalar_copy(windows[j][:].indirect(entries(b, first, values.shape[1])), values)
-
-        def share(name, width=N, **place):
-            return held(name, [P, width], F32, **place)[:]
+        def scalar_scatter(b, j, half):
+            slots = slice(half * HALF_N, (half + 1) * HALF_N)
+            scalar_move(windows[j][:].indirect(entries(b * N + half * HALF_N, HALF_N)), shares[b, j][:, slots])
 
         def store_window(j, queue=nc.sync):
             queue.dma_start(out=out_1[j * P : (j + 1) * P, :], in_=windows[j][:])
 
-        def gather_x(j, first, last, copy):
-            dst, start = picked[j, first // N]
-            copy(dst[:, first - start : last - start], x_sb[j][:].indirect(entries(0, first, last - first)))
-
-        def pick_into(j, dst, experts=(0, 1)):
-            for b in experts:
-                picked[j, b] = dst, experts[0] * N
-
-        def turn_x(j, number):
-            x_bank[j] = bank(f"x_bank{j}", [P, B, 2, P], number)
-            for b in range(B):
-                dst, start = picked[j, b]
-                words = dst[:, b * N - start : (b + 1) * N - start].bitcast(F32)
-                for u in range(2):
-                    nc.tensor.transpose(x_bank[j][:, b, u, :], words[:, u:HALF_N:2], ident[:])
-
-        def copy_out_x(j, part):
-            nc.scalar.copy(
-                out=part.bitcast(F32).rearrange("s (b d u) -> s b d u", b=B, u=2),
-                in_=x_bank[j][:].rearrange("s b u d -> s b d u"),
-            )
-
         def multiply_gw(j, b, number):
             gw[j, b] = bank(f"gw{j}{b}", [P, DV], number)
-            codes, first = x_q[j]
-            multiply(gw[j, b], codes, slice(first + b * P, first + (b + 1) * P), dzt_q[b])
+            multiply(gw[j, b], x_q[j], slice(b * P, (b + 1) * P), dzt_q[b])
 
-        def store_gw(j, b, queue=nc.sync, copy=nc.scalar.copy, **place):
+        def store_gw(j, b, queue=nc.sync, **place):
             gw_sb = held(f"gw_sb{j}{b}", [P, P, PACK], F32, **place)
-            copy(out=gw_sb[:], in_=gw[j, b][:].rearrange("d (t p) -> d p t", t=PACK))
+            nc.scalar.copy(out=gw_sb[:], in_=gw[j, b][:].rearrange("d (t p) -> d p t", t=PACK))
             queue.dma_start(out=out_0[b, j * P : (j + 1) * P, :], in_=gw_sb[:].rearrange("d p t -> d (p t)"))
 
         ident = keep.tile([P, P], F32, name="ident")
@@ -261,176 +242,173 @@ def tile_attend_gex_wx_kernel(tc, xT, dyT, ts, wm, offs, out_0, out_1):
             windows[j] = keep.tile([P, T], F32, name=f"window{j}")
             nc.gpsimd.memset(windows[j][:].bitcast(I32), 0)
 
-        PLANE = 4 * N
-        room("late", 4 * T)
-        load_dy(0, over="late")
-        load_dy(1)
-        load_dy(2)
-        load_dy(3)
-        room("wm0", 5 * PLANE)
-        load_wm(0, 0, 1, over="wm0")
+        for t in range(PACK):
+            load_dy(t)
+        load_wm(0, 0, 1)
         load_wm(0, 1, 1)
-        room("wm02", 4 * PLANE)
-        load_wm(0, 2, 2, over="wm02")
-        room("x0_wm1", 2 * 4 * T)
-        load_x(0, over="x0_wm1")
-        load_wm(1, 0, BLOCKS, over="x0_wm1", skip=4 * T)
+        room("wm02", 8 * KIB)
+        load_wm(0, 2, 1, over="wm02", skip=2 * KIB)
+        load_x(0)
+        load_wm(1, 0, BLOCKS)
         load_x(1)
+        load_wm(0, 3, 1)
         load_x(2)
         load_x(3)
 
-        for b in range(B):
-            ts_g[b] = held(f"ts_g{b}", [P, N], F32)[:]
-        start_of["dzn1"] = start_of["wm0"] + PLANE
-        room("plain0", 2 * PLANE)
-        room("plain2", 2 * PLANE)
-        columns = [held(f"ts_cols{k}", [P, 2], F32, **place)[:] for k, place in enumerate(({}, {"over": "plain0"}, {}, {"over": "plain2"}))]
-        quarters = [(b, h * HALF_N) for b in range(B) for h in range(2)]
-        rows = [ts_gather(b, first, HALF_N, vector_copy) for b, first in quarters]
-        ts_down(rows[0], 0, 0, nc.scalar.copy)
-        ts_down(rows[1], 1, 1, nc.scalar.copy)
-        ts_across(columns[0], *quarters[0], 2, vector_copy)
-        ts_down(rows[2], 2, 0, nc.scalar.copy)
-        ts_across(columns[1], *quarters[1], 3, vector_copy)
-        plain01 = held("plain01", [P, 2, N], F32, over="plain0")
-        scalar_copy(plain01[:, 0, :], dy_sb[0][:].indirect(entries(1)))
-        ts_down(rows[3], 3, 1, nc.scalar.copy)
-        ts_across(columns[2], *quarters[2], 4, nc.scalar.copy)
-        ts_across(columns[3], *quarters[3], 5, nc.scalar.copy)
+        ts_g = [held(f"ts_g{b}", [P, N], F32) for b in range(B)]
+        room("plain01", 4 * KIB)
+        room("plain23", 4 * KIB)
+        under = {1: {"over": "plain01"}, 3: {"over": "plain23"}}
+        ts_cols = [held(f"ts_cols{k}", [P, 2], F32, **under.get(k, {})) for k in range(2 * B)]
+        ts_rows = [ts_gather(k) for k in range(2 * B)]
+        ts_down(0, 0)
+        ts_down(1, 1)
+        ts_across(0, 2, nc.vector.tensor_copy)
+        ts_down(2, 0)
+        ts_across(1, 3, nc.vector.tensor_copy)
+        plain01 = held("plain01", [P, 2, N], F32, over="plain01")
+        gather_dy1(0, plain01[:, 0, :])
+        ts_down(3, 1)
+        ts_across(2, 4, nc.scalar.copy)
+        ts_across(3, 5, nc.scalar.copy)
 
         dz0 = held("dz0", [P, PACK, N], F32)
-        for t in range(PACK):
-            dz[t, 0] = dz0[:, t, :]
-        three = held("dzt_bf0", [P, 3, P, PACK], BF16)
-        dzt_bf[0, 0] = three[:, :2]
-        room("stage0", PLANE)
-        dzt_bf1 = held("dzt_bf1", [P, 2 * WIDE], BF16)[:]
-        plain23 = held("plain23", [P, 2, N], F32, over="plain2")
-        plain2, plain3 = plain23[:, 0, :], plain23[:, 1, :]
+        dzt0_head = held("dzt0_head", [P, 3, P, PACK], BF16)
+        room("wm_words0", 2 * KIB)
+        dzt1 = held("dzt1", [P, PACK * ONE], BF16)
+        plain23 = held("plain23", [P, 2, N], F32, over="plain23")
 
         for first in (0, HALF_N):
-            gather_dz(0, 0, first, HALF_N)
-        turn_dz(0, 0, 6)
-        gather_dz(1, 0)
-        turn_dz(1, 0, 7)
-        late = held("late", [P, 7 * N], BF16, over="late")
-        dz1 = late[:, : PACK * N].rearrange("p (t n) -> p t n", n=N)
-        dzn_bf0 = late[:, 3 * N :]
-        nc.vector.tensor_tensor(dz1[:, 0, :], plain01[:, 0, :], ts_g[1], MULT)
-        scalar_copy(plain01[:, 1, :], dy_sb[1][:].indirect(entries(1)))
-        gather_dz(2, 0)
-        scalar_copy(plain2, dy_sb[2][:].indirect(entries(1)))
-        nc.vector.tensor_tensor(dz1[:, 1, :], plain01[:, 1, :], ts_g[1], MULT)
-        copy_out_dz(0, 0)
-        copy_out_dz(1, 0)
-        turn_dz(2, 0, 2)
-        nc.vector.tensor_tensor(dz1[:, 2, :], plain2, ts_g[1], MULT)
-        gather_dz(3, 0)
-        scalar_copy(plain3, dy_sb[3][:].indirect(entries(1)))
-        turn_words(0, 0)
-        turn_dz(3, 0, 4)
-        stage0 = held("stage0", [P, WIDE // 2], BF16, over="stage0")[:]
-        vector_interleave(as_words(stage0), wm_sb[0, 0][:])
-        vector_interleave(as_words(dzn_bf0), dz0[:])
-        room("q_a", 2 * PLANE)
-        quantize_e4m3("q_a", stage0, [(0, 0)], over="q_a", skip=7 * PLANE // 8)
-        quantize_dzn(0, dzn_bf0)
-        scalar_copy(three[:, 2], turned[2, 0][:].rearrange("s k p -> s p k"))
-        stage1 = held("stage1", [P, 3 * WIDE // 2], BF16, over="wm02", skip=2 * PLANE)[:]
-        scalar_interleave(as_words(stage1[:, : WIDE // 2]), wm_sb[0, 1][:])
-        copy_out_words(0)
-        scalar_interleave(as_words(stage1[:, WIDE // 2 :]), wm_sb[0, 2][:])
-        fourth = held("dzt_bf03", [P, P, PACK], BF16, over="wm02", skip=3 * PLANE // 2)
-        scalar_copy(fourth[:], turned[3, 0][:].rearrange("s k p -> s p k"))
-        multiply_dx(0, 0, 5)
-        dzt_q[0] = planes("dzt_q0", DV, over="stage0")
-        quantize_dzt(0, 0)
-        quantize(dzt_q[0], three[:, 2].rearrange("s p k -> s (p k)"), E5M2, slice(2 * P, 3 * P))
-        nc.vector.tensor_tensor(dz1[:, 3, :], plain3, ts_g[1], MULT)
-        quantize_e4m3("q_b", stage1, [(0, 1), (0, 2), (0, 3)])
-        quantize(dzt_q[0], fourth[:].rearrange("s p k -> s (p k)"), E5M2, slice(3 * P, 4 * P))
-        copy_out_dx(0, 0, share("dx_sb00", over="wm02", skip=PLANE // 2))
+            gather_dz0(0, first, HALF_N)
+        turn_dz0(0, 6)
+        gather_dz0(1)
+        turn_dz0(1, 7)
+        both = held("both", [P, 7 * N], BF16, over="dy0")
+        dz1 = both[:, : PACK * N].rearrange("p (t n) -> p t n", n=N)
+        dzn0 = both[:, 3 * N :]
+        multiply_dz1(0, plain01[:, 0, :])
+        gather_dy1(1, plain01[:, 1, :])
+        gather_dz0(2)
+        gather_dy1(2, plain23[:, 0, :])
+        multiply_dz1(1, plain01[:, 1, :])
+        for t in range(2):
+            copy_out_dz0(t, dzt0_head[:, t])
+        turn_dz0(2, 2)
+        multiply_dz1(2, plain23[:, 0, :])
+        gather_dz0(3)
+        gather_dy1(3, plain23[:, 1, :])
+        dz1_bank = turn_words("dz1_bank0", [dz1[:, 0, :], dz1[:, 1, :]], 0)
+        turn_dz0(3, 4)
+
+        wm_words0 = held("wm_words0", [P, ONE], BF16, over="wm_words0")[:]
+        interleave(nc.vector.tensor_copy, wm_words0, wm_sb[0, 0][:])
+        interleave(nc.vector.tensor_copy, dzn0[:, :TWO], dz0[:, :, :HALF_N])
+        room("x_g0", 4 * KIB)
+        quantize_wm("wm_q00", wm_words0, 0, [0], over="x_g0", skip=7 * KIB // 4)
+        interleave(nc.vector.tensor_copy, dzn0[:, TWO:], dz0[:, :, HALF_N:])
+        dzn_q[0] = quantised("dzn_q0", N)
+        for half in range(2):
+            quantize(dzn_q[0], dzn0[:, half * TWO : (half + 1) * TWO], E5M2, slice(half * HALF_N, (half + 1) * HALF_N))
+        copy_out_dz0(2, dzt0_head[:, 2])
+        wm_words1 = held("wm_words1", [P, TWO], BF16, over="wm02", skip=2 * KIB)[:]
+        interleave(nc.scalar.copy, wm_words1[:, :ONE], wm_sb[0, 1][:])
+        copy_out_words(dzt1[:, :TWO], dz1_bank)
+        interleave(nc.scalar.copy, wm_words1[:, ONE:], wm_sb[0, 2][:])
+        dzt0_last = held("dzt0_last", [P, P, PACK], BF16, over="wm02", skip=KIB)[:]
+        copy_out_dz0(3, dzt0_last)
+        halves = [bank(f"dx00{half}", [P, HALF_N], 5 + 2 * half) for half in range(2)]
+        for half in range(2):
+            multiply(halves[half], *wm_q[0, 0], dzn_q[0], slice(half * HALF_N, (half + 1) * HALF_N))
+
+        dzt_q[0] = quantised("dzt_q0", DV, over="wm_words0")
+        quantize_turned(dzt0_head[:, :2].rearrange("s t p r -> s (t p r)"), 0, 2)
+        quantize_turned(dzt0_head[:, 2].rearrange("s p r -> s (p r)"), 2)
+        multiply_dz1(3, plain23[:, 1, :])
+        quantize_wm("wm_q01", wm_words1, 0, [1, 2])
+        quantize_turned(dzt0_last.rearrange("s p r -> s (p r)"), 3)
+        shares[0, 0] = held("share00", [P, N], F32, over="wm02", skip=-KIB)
+        for half in range(2):
+            nc.scalar.copy(out=shares[0, 0][:, half * HALF_N : (half + 1) * HALF_N], in_=halves[half][:])
         multiply_dx(0, 1, 6)
-        turn_words(1, 5)
+        dz1_bank = turn_words("dz1_bank1", [dz1[:, 2, :], dz1[:, 3, :]], 5)
 
         scatter(0, 0)
-        dzn_bf1 = held("dzn_bf1", [P, 2 * WIDE], BF16, over="dzt_bf03")[:]
-        gpsimd_interleave(as_words(dzn_bf1), dz1)
-        stage2 = held("stage2", [P, 2 * WIDE], BF16)
-        nc.gpsimd.tensor_copy(as_words(stage2[:]), wm_sb[1, 0][:].rearrange("p t c -> p c t"))
-        pick_into(0, held("x_g0", [P, B * N], BF16, over="q_a", skip=PLANE)[:])
-        gather_x(0, 0, B * N, scalar_copy)
-        copy_out_dx(0, 1, share("dx_sb01"))
+        dzn1 = held("dzn1", [P, PACK * N], BF16, over="dzt0_last")[:]
+        gpsimd_interleave(dzn1, dz1)
+        wm_words2 = held("wm_words2", [P, BLOCKS * ONE], BF16)[:]
+        gpsimd_words(wm_words2, wm_sb[1, 0][:])
+        gather_x(0, held("x_g0", [P, B * N], BF16, over="x_g0", skip=2 * KIB)[:], 0)
+        copy_out_share(0, 1)
         multiply_dx(0, 2, 3)
         turn_x(0, 7)
-        copy_out_words(1)
-        xt0 = held("xt0", [P, WIDE], BF16)
-        copy_out_x(0, xt0[:])
+        copy_out_words(dzt1[:, TWO:], dz1_bank)
+        xt0 = copy_out_x(0)
         scatter(0, 1)
-        pick_into(1, held("x_g10", [P, N], BF16, over="x0", skip=7 * PLANE // 2)[:], (0,))
-        pick_into(1, held("x_g11", [P, N], BF16, over="dx_sb00")[:], (1,))
-        gather_x(1, 0, N, scalar_copy)
-        gather_x(1, N, B * N, scalar_copy)
+        x_g10 = held("x_g10", [P, N], BF16, over="x0", skip=7 * KIB)[:]
+        x_g11 = held("x_g11", [P, N], BF16, over="share00")[:]
+        gather_x(1, x_g10, 0)
+        gather_x(1, x_g11, N)
         turn_x(1, 0)
-        copy_out_dx(0, 2, share("dx_sb02", over="wm10", skip=-PLANE // 4))
-        xt1 = held("xt1", [P, WIDE], BF16)
-        copy_out_x(1, xt1[:])
-        pick_into(2, held("x_g20", [P, N], BF16, over="x_g11")[:], (0,))
-        pick_into(2, held("x_g21", [P, N], BF16)[:], (1,))
-        gather_x(2, 0, N, scalar_copy)
-        gather_x(2, N, B * N, scalar_copy)
-        quantize_dzn(1, dzn_bf1, over="wm10", skip=3 * PLANE // 4)
-        quantize_e4m3("q_x0", xt0[:], [], 0, over="wm10", skip=11 * PLANE // 4)
-        quantize_e4m3("q_c", stage2[:], [(1, j) for j in range(BLOCKS)])
-        dzt_q[1] = planes("dzt_q1", DV, over="wm10", skip=7 * PLANE // 4)
-        quantize(dzt_q[1], dzt_bf1, E5M2)
+        copy_out_share(0, 2, over="wm10", skip=-KIB // 2)
+        xt1 = copy_out_x(1)
+        x_g20 = held("x_g20", [P, N], BF16, over="x_g11")[:]
+        x_g21 = held("x_g21", [P, N], BF16)[:]
+        gather_x(2, x_g20, 0)
+        gather_x(2, x_g21, N)
+
+        quantize_dzn(1, dzn1, over="wm10", skip=3 * KIB // 2)
+        quantize_x(0, xt0, over="wm10", skip=11 * KIB // 2)
+        quantize_wm("wm_q1", wm_words2, 1, range(BLOCKS))
+        dzt_q[1] = quantised("dzt_q1", DV, over="wm10", skip=7 * KIB // 2)
+        quantize(dzt_q[1], dzt1[:], E5M2)
         multiply_gw(0, 0, 3)
         multiply_dx(1, 0, 0)
         multiply_gw(0, 1, 7)
         turn_x(2, 4)
 
         scatter(0, 2)
-        quantize_e4m3("q_x1", xt1[:], [], 1, over="wm10", skip=13 * PLANE // 4)
-        store_gw(0, 0, over="x_g20", skip=-PLANE // 2)
-        copy_out_dx(1, 0, share("dx_sb10", over="x2", skip=PLANE))
+        wm_words3 = held("wm_words3", [P, ONE], BF16, over="dzt1")[:]
+        gpsimd_words(wm_words3, wm_sb[0, 3][:])
+        quantize_x(1, xt1, over="wm10", skip=13 * KIB // 2)
+        quantize_wm("wm_q03", wm_words3, 0, [3])
+        store_gw(0, 0, over="x_g20", skip=-KIB)
+        copy_out_share(1, 0, over="x2", skip=2 * KIB)
         multiply_dx(1, 1, 3)
         multiply_dx(1, 2, 0)
-        store_gw(0, 1, over="x2", skip=2 * PLANE)
-        room("fifth", 3 * PLANE)
-        copy_out_dx(1, 1, share("dx_sb11", over="fifth", skip=PLANE // 2))
-        copy_out_dx(1, 2, share("dx_sb12"))
-        scalar_scatter(1, 1, 0, dx_sb[1, 1, 0][:, :HALF_N])
-        xt2 = held("xt2", [P, WIDE], BF16)
-        copy_out_x(2, xt2[:])
-        scalar_scatter(1, 1, HALF_N, dx_sb[1, 1, 0][:, HALF_N:])
+        store_gw(0, 1, over="x2", skip=4 * KIB)
+        room("share13", 6 * KIB)
+        copy_out_share(1, 1, over="share13", skip=KIB)
+        copy_out_share(1, 2)
+        scalar_scatter(1, 1, 0)
+        xt2 = copy_out_x(2)
+        scalar_scatter(1, 1, 1)
         scatter(1, 0)
         store_window(0)
         scatter(1, 2)
         multiply_dx(0, 3, 3)
-        copy_out_dx(0, 3, share("dx_sb03"))
+        copy_out_share(0, 3)
         store_window(1, nc.scalar)
-        pick_into(3, held("x_g3", [P, B * N], BF16, over="dx_sb11")[:])
-        gather_x(3, 0, N, scalar_copy)
-        gather_x(3, N, B * N, scalar_copy)
+        x_g3 = held("x_g3", [P, B * N], BF16, over="share11")[:]
+        for b in range(B):
+            gather_x(3, x_g3[:, b * N : (b + 1) * N], b * N)
         multiply_gw(1, 0, 4)
         multiply_gw(1, 1, 3)
         turn_x(3, 2)
         multiply_dx(1, 3, 7)
-        quantize_e4m3("q_x2", xt2[:], [], 2)
+        quantize_x(2, xt2)
         store_window(2)
 
         scatter(0, 3)
-        store_gw(1, 0, over="dy1")
-        store_gw(1, 1, over="dy1", skip=PLANE)
-        xt3 = held("xt3", [P, WIDE], BF16)
-        copy_out_x(3, xt3[:])
-        copy_out_dx(1, 3, share("dx_sb13", over="x_g3", skip=-PLANE // 2))
+        for b in range(B):
+            store_gw(1, b, over="dy1", skip=2 * b * KIB)
+        xt3 = copy_out_x(3)
+        copy_out_share(1, 3, over="share13")
         multiply_gw(2, 0, 4)
         multiply_gw(2, 1, 3)
-        quantize_e4m3("q_x3", xt3[:], [], 3)
+        quantize_x(3, xt3)
         multiply_gw(3, 0, 5)
         multiply_gw(3, 1, 1)
         scatter(1, 3)
         for k, (j, b) in enumerate(((2, 0), (2, 1), (3, 0), (3, 1))):
-            store_gw(j, b, nc.scalar, over="dy2", skip=k * PLANE)
+            store_gw(j, b, nc.scalar, over="dy2", skip=2 * k * KIB)
         store_window(3)

@@ -350,7 +350,9 @@ def tile_attend_gex_wx_kernel(tc, xT, dyT, ts, wm, offs, out_0, out_1):
         gather_x(1, x_g11, N)
         turn_x(1, 0)
         copy_out_share(0, 2, over="wm10", skip=-KIB // 2)
-        xt1 = copy_out_x(1)
+        mixed = held("mixed", [P, ONE + TWO], BF16)[:]
+        interleave(nc.scalar.copy, mixed[:, :ONE], wm_sb[0, 3][:])
+        copy_out_words(mixed[:, ONE:], x_bank[1])
         x_g20 = held("x_g20", [P, N], BF16, over="x_g11")[:]
         x_g21 = held("x_g21", [P, N], BF16)[:]
         gather_x(2, x_g20, 0)
@@ -367,10 +369,10 @@ def tile_attend_gex_wx_kernel(tc, xT, dyT, ts, wm, offs, out_0, out_1):
         turn_x(2, 4)
 
         scatter(0, 2)
-        wm_words3 = held("wm_words3", [P, ONE], BF16, over="dzt1")[:]
-        gpsimd_words(wm_words3, wm_sb[0, 3][:])
-        quantize_x(1, xt1, over="wm10", skip=13 * KIB // 2)
-        quantize_wm("wm_q03", wm_words3, 0, [3])
+        mixed_q = quantised("mixed_q", (1 + B) * P, over="wm10", skip=13 * KIB // 2)
+        quantize(mixed_q, mixed, E4M3)
+        wm_q[0, 3] = mixed_q, slice(0, P)
+        x_q[1] = mixed_q[0][:, P:], mixed_q[1][:, P:]
         store_gw(0, 0, over="x_g20", skip=-KIB)
         copy_out_share(1, 0, over="x2", skip=2 * KIB)
         multiply_dx(1, 1, 3)

@@ -60,8 +60,8 @@ def tile_attend_gex_wx_kernel(tc, xT, dyT, ts, wm, offs, out_0, out_1):
         offsets = keep.tile([P, B * N // ROWS_OF_LIST], U16, name="offsets")
         ts_sb = held("ts_sb", [P, T], F32)
         dy_sb, wm_sb, x_sb, windows = {}, {}, {}, {}
-        turned, picked, x_bank, product, gw, shares = {}, {}, {}, {}, {}, {}
-        dzt_q, dzn_q, wm_q, x_q = {}, {}, {}, {}
+        xt, turned, picked, x_bank, product, gw, shares = {}, {}, {}, {}, {}, {}, {}
+        dzt_q, dzn_q, wm_q, x_q, ts_rows, gw_sb = {}, {}, {}, {}, {}, {}
 
         def entries(first, count):
             return offsets[:, first // ROWS_OF_LIST : (first + count) // ROWS_OF_LIST]
@@ -90,15 +90,15 @@ def tile_attend_gex_wx_kernel(tc, xT, dyT, ts, wm, offs, out_0, out_1):
         def quantize(dst, src, fmt, cols=slice(None)):
             nc.vector.quantize_mx(out=dst[0][:, cols].bitcast(fmt), scales=dst[1][:, cols], in_=src)
 
-        def quantize_wm(name, src, b, blocks, **place):
+        def quantize_wm(name, src, blocks, **place):
             dst = quantised(name, len(blocks) * P, **place)
             quantize(dst, src, E4M3)
-            for k, j in enumerate(blocks):
-                wm_q[b, j] = dst, slice(k * P, (k + 1) * P)
+            for k, block in enumerate(blocks):
+                wm_q[block] = dst, slice(k * P, (k + 1) * P)
 
-        def quantize_x(j, src, **place):
+        def quantize_x(j, **place):
             x_q[j] = quantised(f"x_q{j}", B * P, **place)
-            quantize(x_q[j], src, E4M3)
+            quantize(x_q[j], xt[j], E4M3)
 
         def quantize_dzn(b, src, **place):
             dzn_q[b] = quantised(f"dzn_q{b}", N, **place)
@@ -127,16 +127,15 @@ def tile_attend_gex_wx_kernel(tc, xT, dyT, ts, wm, offs, out_0, out_1):
         def gpsimd_words(dst, src):
             nc.gpsimd.tensor_copy(dst.rearrange("p (c t) -> p c t", t=PACK), src.rearrange("p t c -> p c t"))
 
-        def ts_gather(k):
-            row = held(f"ts_row{k}", [P, HALF_N], F32)
-            nc.vector.tensor_copy(row[:], ts_sb[:].indirect(entries(k * HALF_N, HALF_N)))
-            return row
+        def ts_gather(k, move):
+            ts_rows[k] = held(f"ts_row{k}", [P, HALF_N], F32)
+            move(ts_rows[k][:], ts_sb[:].indirect(entries(k * HALF_N, HALF_N)))
 
-        def ts_down(k, number):
+        def ts_down(k, number, copy):
             down = bank(f"down{k}", [P, 2, P], number)
             for q in range(2):
                 nc.tensor.transpose(down[:, q, :], ts_rows[k][:, q * P : (q + 1) * P], ident[:])
-            nc.scalar.copy(ts_cols[k][:], down[:, :, LAST])
+            copy(ts_cols[k][:], down[:, :, LAST])
 
         def ts_across(k, number, copy):
             b, half = divmod(k, 2)
@@ -172,25 +171,22 @@ def tile_attend_gex_wx_kernel(tc, xT, dyT, ts, wm, offs, out_0, out_1):
                     nc.tensor.transpose(dst[:, e, u, :], words[:, u:HALF_N:2], ident[:])
             return dst
 
-        def copy_out_words(dst, src):
-            nc.scalar.copy(
+        def copy_out_words(dst, src, copy=nc.scalar.copy):
+            copy(
                 out=dst.bitcast(F32).rearrange("s (e p u) -> s e p u", e=2, u=2),
                 in_=src[:].rearrange("s e u p -> s e p u"),
             )
 
-        def gather_x(j, dst, first):
-            count = dst.shape[1]
-            for k in range(count // N):
-                picked[j, first // N + k] = dst[:, k * N : (k + 1) * N]
-            scalar_move(dst, x_sb[j][:].indirect(entries(first, count)))
+        def gather_x(j, b, move, **place):
+            picked[j, b] = held(f"x_g{j}{b}", [P, N], BF16, **place)[:]
+            move(picked[j, b], x_sb[j][:].indirect(entries(b * N, N)))
 
         def turn_x(j, number):
             x_bank[j] = turn_words(f"x_bank{j}", [picked[j, b] for b in range(B)], number)
 
-        def copy_out_x(j):
-            dst = held(f"xt{j}", [P, TWO], BF16)[:]
-            copy_out_words(dst, x_bank[j])
-            return dst
+        def copy_out_x(j, copy=nc.scalar.copy, **place):
+            xt[j] = held(f"xt{j}", [P, TWO], BF16, **place)[:]
+            copy_out_words(xt[j], x_bank[j], copy)
 
         def multiply(out, stationary, cols, moving, slots=slice(None)):
             nc.tensor.matmul_mx(
@@ -207,16 +203,16 @@ def tile_attend_gex_wx_kernel(tc, xT, dyT, ts, wm, offs, out_0, out_1):
             product[b, j] = bank(f"dx{b}{j}", [P, N], number)
             multiply(product[b, j], *wm_q[b, j], dzn_q[b])
 
-        def copy_out_share(b, j, **place):
+        def copy_out_share(b, j, copy=nc.scalar.copy, **place):
             shares[b, j] = held(f"share{b}{j}", [P, N], F32, **place)
-            nc.scalar.copy(out=shares[b, j][:], in_=product[b, j][:])
+            copy(out=shares[b, j][:], in_=product[b, j][:])
 
         def scatter(b, j):
             nc.vector.tensor_copy(windows[j][:].indirect(entries(b * N, N)), shares[b, j][:])
 
-        def scalar_scatter(b, j, half):
-            slots = slice(half * HALF_N, (half + 1) * HALF_N)
-            scalar_move(windows[j][:].indirect(entries(b * N + half * HALF_N, HALF_N)), shares[b, j][:, slots])
+        def scalar_scatter(b, j):
+            window = windows[j][:].indirect(entries(b * N, N))
+            nc.scalar.activation(window, shares[b, j][:], COPY, scale=ones[:])
 
         def store_window(j, queue=nc.sync):
             queue.dma_start(out=out_1[j * P : (j + 1) * P, :], in_=windows[j][:])
@@ -225,13 +221,22 @@ def tile_attend_gex_wx_kernel(tc, xT, dyT, ts, wm, offs, out_0, out_1):
             gw[j, b] = bank(f"gw{j}{b}", [P, DV], number)
             multiply(gw[j, b], x_q[j], slice(b * P, (b + 1) * P), dzt_q[b])
 
-        def store_gw(j, b, queue=nc.sync, **place):
-            gw_sb = held(f"gw_sb{j}{b}", [P, P, PACK], F32, **place)
-            nc.scalar.copy(out=gw_sb[:], in_=gw[j, b][:].rearrange("d (t p) -> d p t", t=PACK))
-            queue.dma_start(out=out_0[b, j * P : (j + 1) * P, :], in_=gw_sb[:].rearrange("d p t -> d (p t)"))
+        def copy_out_gw(j, b, copy=nc.scalar.copy, **place):
+            place = place or {"over": f"dy{j // 2 * 2}", "skip": (j % 2 * B + b) * 2 * KIB}
+            gw_sb[j, b] = held(f"gw_sb{j}{b}", [P, P, PACK], F32, **place)
+            copy(out=gw_sb[j, b][:], in_=gw[j, b][:].rearrange("d (t p) -> d p t", t=PACK))
 
+        def store_gw(j, b, queue=nc.sync):
+            rows = out_0[b, j * P : (j + 1) * P, :]
+            queue.dma_start(out=rows, in_=gw_sb[j, b][:].rearrange("d p t -> d (p t)"))
+
+        vector_move = nc.vector.tensor_copy
         ident = keep.tile([P, P], F32, name="ident")
         make_identity(nc, ident[:])
+        one = keep.tile([P, 1], F32, name="one")
+        ones = keep.tile([P, 1], F32, name="ones")
+        nc.vector.memset(one[:], 1.0)
+        nc.scalar.copy(ones[:], one[:])
 
         nc.sync.dma_start(out=ts_sb[LAST:, :], in_=ts[LAST:, :])
         nc.gpsimd.memset(ts_sb[:LAST, : T // 4], 0.0)
@@ -246,171 +251,164 @@ def tile_attend_gex_wx_kernel(tc, xT, dyT, ts, wm, offs, out_0, out_1):
             load_dy(t)
         load_wm(0, 0, 1)
         load_wm(0, 1, 1)
-        room("wm02", 8 * KIB)
-        load_wm(0, 2, 1, over="wm02", skip=2 * KIB)
         load_x(0)
-        load_wm(1, 0, BLOCKS)
         load_x(1)
-        load_wm(0, 3, 1)
+        load_wm(1, 0, 2)
         load_x(2)
+        load_wm(0, 2, 2)
         load_x(3)
+        load_wm(1, 2, 2)
 
         ts_g = [held(f"ts_g{b}", [P, N], F32) for b in range(B)]
-        room("plain01", 4 * KIB)
-        room("plain23", 4 * KIB)
-        under = {1: {"over": "plain01"}, 3: {"over": "plain23"}}
-        ts_cols = [held(f"ts_cols{k}", [P, 2], F32, **under.get(k, {})) for k in range(2 * B)]
-        ts_rows = [ts_gather(k) for k in range(2 * B)]
-        ts_down(0, 0)
-        ts_down(1, 1)
-        ts_across(0, 2, nc.vector.tensor_copy)
-        ts_down(2, 0)
-        ts_across(1, 3, nc.vector.tensor_copy)
-        plain01 = held("plain01", [P, 2, N], F32, over="plain01")
-        gather_dy1(0, plain01[:, 0, :])
-        ts_down(3, 1)
-        ts_across(2, 4, nc.scalar.copy)
-        ts_across(3, 5, nc.scalar.copy)
-
         dz0 = held("dz0", [P, PACK, N], F32)
-        dzt0_head = held("dzt0_head", [P, 3, P, PACK], BF16)
-        room("wm_words0", 2 * KIB)
-        dzt1 = held("dzt1", [P, PACK * ONE], BF16)
-        plain23 = held("plain23", [P, 2, N], F32, over="plain23")
+        ts_cols = [held("ts_cols0", [P, 2], F32), dz0[:, 2, :2], dz0[:, 3, :2], dz0[:, 3, 8:10]]
+        ts_gather(0, vector_move)
+        ts_gather(1, scalar_move)
+        ts_gather(2, vector_move)
+        ts_gather(3, scalar_move)
+        ts_down(0, 0, vector_move)
+        ts_down(1, 1, nc.scalar.copy)
+        ts_down(2, 4, vector_move)
+        ts_across(0, 2, vector_move)
+        ts_across(1, 3, vector_move)
+        ts_down(3, 5, vector_move)
+        plain = [dz0[:, 2, :], dz0[:, 3, :]] + [held(f"plain{t}", [P, N], F32, over="dy1", skip=5 * KIB)[:] for t in (2, 3)]
+        dz1 = held("dz1", [P, PACK, N], BF16)
 
+        gather_dy1(0, plain[0])
         for first in (0, HALF_N):
             gather_dz0(0, first, HALF_N)
-        turn_dz0(0, 6)
+        ts_across(2, 6, nc.scalar.copy)
+        ts_across(3, 7, nc.scalar.copy)
+        turn_dz0(0, 0)
+        gather_dy1(1, plain[1])
         gather_dz0(1)
-        turn_dz0(1, 7)
-        both = held("both", [P, 7 * N], BF16, over="dy0")
-        dz1 = both[:, : PACK * N].rearrange("p (t n) -> p t n", n=N)
-        dzn0 = both[:, 3 * N :]
-        multiply_dz1(0, plain01[:, 0, :])
-        gather_dy1(1, plain01[:, 1, :])
+        turn_dz0(1, 1)
+        dzt00 = held("dzt00", [P, P, PACK], BF16, over="dy1")
+        copy_out_dz0(0, dzt00[:])
+        multiply_dz1(0, plain[0])
+        multiply_dz1(1, plain[1])
+        words01 = turn_words("dz1_bank0", [dz1[:, 0, :], dz1[:, 1, :]], 2)
         gather_dz0(2)
-        gather_dy1(2, plain23[:, 0, :])
-        multiply_dz1(1, plain01[:, 1, :])
-        for t in range(2):
-            copy_out_dz0(t, dzt0_head[:, t])
-        turn_dz0(2, 2)
-        multiply_dz1(2, plain23[:, 0, :])
-        gather_dz0(3)
-        gather_dy1(3, plain23[:, 1, :])
-        dz1_bank = turn_words("dz1_bank0", [dz1[:, 0, :], dz1[:, 1, :]], 0)
+        gather_dy1(2, plain[2])
+        turn_dz0(2, 3)
+        dzt1 = held("dzt1", [P, 2 * TWO], BF16, over="dy2")
+        dzt01 = held("dzt01", [P, P, PACK], BF16, over="dy2", skip=4 * KIB)
+        copy_out_dz0(1, dzt01[:])
+        multiply_dz1(2, plain[2])
+        for first in (0, HALF_N):
+            gather_dz0(3, first, HALF_N)
+        gather_dy1(3, plain[3])
+        copy_out_words(dzt1[:, :TWO], words01)
         turn_dz0(3, 4)
 
-        wm_words0 = held("wm_words0", [P, ONE], BF16, over="wm_words0")[:]
-        interleave(nc.vector.tensor_copy, wm_words0, wm_sb[0, 0][:])
-        interleave(nc.vector.tensor_copy, dzn0[:, :TWO], dz0[:, :, :HALF_N])
-        room("x_g0", 4 * KIB)
-        quantize_wm("wm_q00", wm_words0, 0, [0], over="x_g0", skip=7 * KIB // 4)
-        interleave(nc.vector.tensor_copy, dzn0[:, TWO:], dz0[:, :, HALF_N:])
+        wm_words0 = held("wm_words0", [P, ONE], BF16, over="ts_g0")[:]
+        wm_words1 = held("wm_words1", [P, ONE], BF16, over="dy3", skip=7 * KIB)[:]
+        dzn0 = held("dzn0", [P, PACK * N], BF16)
+        dzt02 = held("dzt02", [P, 2, P, PACK], BF16, over="dy3", skip=3 * KIB)
+        interleave(vector_move, dzn0[:, :TWO], dz0[:, :, :HALF_N])
+        interleave(vector_move, wm_words0, wm_sb[0, 0][:])
+        interleave(vector_move, dzn0[:, TWO:], dz0[:, :, HALF_N:])
+        copy_out_dz0(2, dzt02[:, 0])
+        interleave(nc.scalar.copy, wm_words1, wm_sb[0, 1][:])
         dzn_q[0] = quantised("dzn_q0", N)
-        for half in range(2):
-            quantize(dzn_q[0], dzn0[:, half * TWO : (half + 1) * TWO], E5M2, slice(half * HALF_N, (half + 1) * HALF_N))
-        copy_out_dz0(2, dzt0_head[:, 2])
-        wm_words1 = held("wm_words1", [P, TWO], BF16, over="wm02", skip=2 * KIB)[:]
-        interleave(nc.scalar.copy, wm_words1[:, :ONE], wm_sb[0, 1][:])
-        copy_out_words(dzt1[:, :TWO], dz1_bank)
-        interleave(nc.scalar.copy, wm_words1[:, ONE:], wm_sb[0, 2][:])
-        dzt0_last = held("dzt0_last", [P, P, PACK], BF16, over="wm02", skip=KIB)[:]
-        copy_out_dz0(3, dzt0_last)
-        halves = [bank(f"dx00{half}", [P, HALF_N], 5 + 2 * half) for half in range(2)]
-        for half in range(2):
-            multiply(halves[half], *wm_q[0, 0], dzn_q[0], slice(half * HALF_N, (half + 1) * HALF_N))
-
-        dzt_q[0] = quantised("dzt_q0", DV, over="wm_words0")
-        quantize_turned(dzt0_head[:, :2].rearrange("s t p r -> s (t p r)"), 0, 2)
-        quantize_turned(dzt0_head[:, 2].rearrange("s p r -> s (p r)"), 2)
-        multiply_dz1(3, plain23[:, 1, :])
-        quantize_wm("wm_q01", wm_words1, 0, [1, 2])
-        quantize_turned(dzt0_last.rearrange("s p r -> s (p r)"), 3)
-        shares[0, 0] = held("share00", [P, N], F32, over="wm02", skip=-KIB)
-        for half in range(2):
-            nc.scalar.copy(out=shares[0, 0][:, half * HALF_N : (half + 1) * HALF_N], in_=halves[half][:])
+        quantize(dzn_q[0], dzn0[:, :TWO], E5M2, slice(0, HALF_N))
+        quantize_wm("wm_q00", wm_words0, [(0, 0)])
+        quantize(dzn_q[0], dzn0[:, TWO:], E5M2, slice(HALF_N, N))
+        quantize_wm("wm_q01", wm_words1, [(0, 1)])
+        copy_out_dz0(3, dzt02[:, 1])
+        multiply_dx(0, 0, 5)
         multiply_dx(0, 1, 6)
-        dz1_bank = turn_words("dz1_bank1", [dz1[:, 2, :], dz1[:, 3, :]], 5)
-
-        scatter(0, 0)
-        dzn1 = held("dzn1", [P, PACK * N], BF16, over="dzt0_last")[:]
-        gpsimd_interleave(dzn1, dz1)
-        wm_words2 = held("wm_words2", [P, BLOCKS * ONE], BF16)[:]
-        gpsimd_words(wm_words2, wm_sb[1, 0][:])
-        gather_x(0, held("x_g0", [P, B * N], BF16, over="x_g0", skip=2 * KIB)[:], 0)
+        multiply_dz1(3, plain[3])
+        words23 = turn_words("dz1_bank1", [dz1[:, 2, :], dz1[:, 3, :]], 7)
+        gather_x(0, 0, scalar_move, over="dz0")
+        copy_out_share(0, 0)
         copy_out_share(0, 1)
-        multiply_dx(0, 2, 3)
-        turn_x(0, 7)
-        copy_out_words(dzt1[:, TWO:], dz1_bank)
-        xt0 = copy_out_x(0)
-        scatter(0, 1)
-        x_g10 = held("x_g10", [P, N], BF16, over="x0", skip=7 * KIB)[:]
-        x_g11 = held("x_g11", [P, N], BF16, over="share00")[:]
-        gather_x(1, x_g10, 0)
-        gather_x(1, x_g11, N)
-        turn_x(1, 0)
-        copy_out_share(0, 2, over="wm10", skip=-KIB // 2)
-        mixed = held("mixed", [P, ONE + TWO], BF16)[:]
-        interleave(nc.scalar.copy, mixed[:, :ONE], wm_sb[0, 3][:])
-        copy_out_words(mixed[:, ONE:], x_bank[1])
-        x_g20 = held("x_g20", [P, N], BF16, over="x_g11")[:]
-        x_g21 = held("x_g21", [P, N], BF16)[:]
-        gather_x(2, x_g20, 0)
-        gather_x(2, x_g21, N)
+        gather_x(0, 1, vector_move, over="wm_words1")
+        copy_out_words(dzt1[:, TWO:], words23)
 
-        quantize_dzn(1, dzn1, over="wm10", skip=3 * KIB // 2)
-        quantize_x(0, xt0, over="wm10", skip=11 * KIB // 2)
-        quantize_wm("wm_q1", wm_words2, 1, range(BLOCKS))
-        dzt_q[1] = quantised("dzt_q1", DV, over="wm10", skip=7 * KIB // 2)
+        dzn1 = held("dzn1", [P, PACK * N], BF16, over="plain3", skip=-3 * KIB)[:]
+        gpsimd_interleave(dzn1, dz1[:])
+        wm_words2 = held("wm_words2", [P, TWO], BF16, over="plain3", skip=KIB)[:]
+        gpsimd_words(wm_words2, wm_sb[1, 0][:])
+        scatter(0, 0)
+        turn_x(0, 5)
+        room("xt0", 6 * KIB)
+        copy_out_x(0, over="xt0", skip=KIB)
+        scalar_scatter(0, 1)
+
+        quantize_dzn(1, dzn1, over="wm10")
+        quantize_wm("wm_q10", wm_words2, [(1, 0), (1, 1)])
+        dzt_q[0] = quantised("dzt_q0", DV, over="dzn1")
+        quantize_turned(dzt00[:].rearrange("s p r -> s (p r)"), 0)
+        quantize_turned(dzt01[:].rearrange("s p r -> s (p r)"), 1)
+        quantize_turned(dzt02[:].rearrange("s t p r -> s (t p r)"), 2, 2)
+        dzt_q[1] = quantised("dzt_q1", DV, over="dzn1", skip=2 * KIB)
         quantize(dzt_q[1], dzt1[:], E5M2)
-        multiply_gw(0, 0, 3)
-        multiply_dx(1, 0, 0)
-        multiply_gw(0, 1, 7)
-        turn_x(2, 4)
-
-        scatter(0, 2)
-        mixed_q = quantised("mixed_q", (1 + B) * P, over="wm10", skip=13 * KIB // 2)
-        quantize(mixed_q, mixed, E4M3)
-        wm_q[0, 3] = mixed_q, slice(0, P)
-        x_q[1] = mixed_q[0][:, P:], mixed_q[1][:, P:]
-        store_gw(0, 0, over="x_g20", skip=-KIB)
-        copy_out_share(1, 0, over="x2", skip=2 * KIB)
+        quantize_x(0, over="dzt02")
+        multiply_dx(1, 0, 2)
         multiply_dx(1, 1, 3)
-        multiply_dx(1, 2, 0)
-        store_gw(0, 1, over="x2", skip=4 * KIB)
-        room("share13", 6 * KIB)
-        copy_out_share(1, 1, over="share13", skip=KIB)
-        copy_out_share(1, 2)
-        scalar_scatter(1, 1, 0)
-        xt2 = copy_out_x(2)
-        scalar_scatter(1, 1, 1)
+        wm_words3 = held("wm_words3", [P, 2 * TWO], BF16, over="xt0")[:]
+        gpsimd_words(wm_words3[:, :TWO], wm_sb[0, 2][:])
+        gpsimd_words(wm_words3[:, TWO:], wm_sb[1, 2][:])
+        gather_x(1, 0, scalar_move, over="x_g00")
+        gather_x(1, 1, vector_move, over="dzt1", skip=3 * KIB)
+        copy_out_share(1, 0)
+        gather_x(2, 0, scalar_move, over="dzt1")
+        multiply_gw(0, 0, 4)
+        multiply_gw(0, 1, 5)
+        turn_x(1, 2)
+        copy_out_gw(0, 0)
+        store_gw(0, 0)
+        copy_out_x(1)
+        copy_out_share(1, 1, over="x_g11", skip=-3 * KIB // 2)
+        copy_out_gw(0, 1, over="x_g11", skip=KIB // 2)
+        store_gw(0, 1)
         scatter(1, 0)
         store_window(0)
-        scatter(1, 2)
-        multiply_dx(0, 3, 3)
-        copy_out_share(0, 3)
-        store_window(1, nc.scalar)
-        x_g3 = held("x_g3", [P, B * N], BF16, over="share11")[:]
-        for b in range(B):
-            gather_x(3, x_g3[:, b * N : (b + 1) * N], b * N)
-        multiply_gw(1, 0, 4)
-        multiply_gw(1, 1, 3)
-        turn_x(3, 2)
-        multiply_dx(1, 3, 7)
-        quantize_x(2, xt2)
-        store_window(2)
+        scalar_scatter(1, 1)
+        store_window(1)
 
-        scatter(0, 3)
-        for b in range(B):
-            store_gw(1, b, over="dy1", skip=2 * b * KIB)
-        xt3 = copy_out_x(3)
-        copy_out_share(1, 3, over="share13")
-        multiply_gw(2, 0, 4)
-        multiply_gw(2, 1, 3)
-        quantize_x(3, xt3)
-        multiply_gw(3, 0, 5)
-        multiply_gw(3, 1, 1)
+        quantize_wm("wm_q2", wm_words3, [(0, 2), (0, 3), (1, 2), (1, 3)], over="wm02")
+        multiply_dx(0, 2, 7)
+        multiply_dx(0, 3, 1)
+        gather_x(2, 1, vector_move, over="wm12", skip=KIB)
+        copy_out_share(0, 2, vector_move)
+        quantize_x(1, over="dzn_q0")
+        turn_x(2, 7)
+        multiply_gw(1, 0, 0)
+        multiply_gw(1, 1, 4)
+        scatter(0, 2)
+        copy_out_x(2)
+        multiply_dx(1, 2, 7)
+        gather_x(3, 0, scalar_move, over="x_g21", skip=-KIB // 2)
+        gather_x(3, 1, scalar_move, over="x_g21", skip=KIB // 2)
+        quantize_x(2)
+        copy_out_share(1, 2, vector_move)
+        turn_x(3, 7)
+        copy_out_gw(1, 0)
+        multiply_dx(1, 3, 0)
+        copy_out_share(0, 3, over="x3", skip=KIB)
+        store_gw(1, 0, nc.scalar)
+        copy_out_gw(1, 1, over="x3", skip=5 * KIB)
+        multiply_gw(2, 0, 1)
+        multiply_gw(2, 1, 6)
+        scatter(1, 2)
+        store_window(2)
+        scalar_scatter(0, 3)
+        store_gw(1, 1, nc.scalar)
+        copy_out_x(3, vector_move)
+        copy_out_share(1, 3, vector_move, over="x_g31")
+        quantize_x(3)
+        multiply_gw(3, 0, 3)
+        multiply_gw(3, 1, 5)
         scatter(1, 3)
-        for k, (j, b) in enumerate(((2, 0), (2, 1), (3, 0), (3, 1))):
-            store_gw(j, b, nc.scalar, over="dy2", skip=2 * k * KIB)
+        copy_out_gw(2, 0, over="share03", skip=-KIB)
+        copy_out_gw(2, 1, over="share03", skip=KIB)
+        store_gw(2, 0, nc.scalar)
+        copy_out_gw(3, 0)
+        store_gw(2, 1, nc.scalar)
+        copy_out_gw(3, 1)
+        store_gw(3, 0, nc.scalar)
+        store_gw(3, 1, nc.scalar)
         store_window(3)

@@ -249,15 +249,14 @@ def tile_attend_gex_wx_kernel(tc, xT, dyT, ts, wm, offs, out_0, out_1):
 
         for t in range(PACK):
             load_dy(t)
-        load_wm(0, 0, 1)
-        load_wm(0, 1, 1)
+        load_wm(0, 0, 2)
         load_x(0)
         load_x(1)
         load_wm(1, 0, 2)
         load_x(2)
         load_wm(0, 2, 2)
-        load_x(3)
         load_wm(1, 2, 2)
+        load_x(3)
 
         ts_g = [held(f"ts_g{b}", [P, N], F32) for b in range(B)]
         dz0 = held("dz0", [P, PACK, N], F32)
@@ -292,8 +291,8 @@ def tile_attend_gex_wx_kernel(tc, xT, dyT, ts, wm, offs, out_0, out_1):
         gather_dz0(2)
         gather_dy1(2, plain[2])
         turn_dz0(2, 3)
-        dzt1 = held("dzt1", [P, 2 * TWO], BF16, over="dy2")
-        dzt01 = held("dzt01", [P, P, PACK], BF16, over="dy2", skip=4 * KIB)
+        dzt1 = held("dzt1", [P, 2 * TWO + HALF_N], BF16, over="dy2")
+        dzt01 = held("dzt01", [P, P, PACK], BF16, over="dy2", skip=5 * KIB)
         copy_out_dz0(1, dzt01[:])
         multiply_dz1(2, plain[2])
         for first in (0, HALF_N):
@@ -307,10 +306,10 @@ def tile_attend_gex_wx_kernel(tc, xT, dyT, ts, wm, offs, out_0, out_1):
         dzn0 = held("dzn0", [P, PACK * N], BF16)
         dzt02 = held("dzt02", [P, 2, P, PACK], BF16, over="dy3", skip=3 * KIB)
         interleave(vector_move, dzn0[:, :TWO], dz0[:, :, :HALF_N])
-        interleave(vector_move, wm_words0, wm_sb[0, 0][:])
+        interleave(vector_move, wm_words0, wm_sb[0, 0][:, :, :P])
         interleave(vector_move, dzn0[:, TWO:], dz0[:, :, HALF_N:])
         copy_out_dz0(2, dzt02[:, 0])
-        interleave(nc.scalar.copy, wm_words1, wm_sb[0, 1][:])
+        interleave(nc.scalar.copy, wm_words1, wm_sb[0, 0][:, :, P:])
         dzn_q[0] = quantised("dzn_q0", N)
         quantize(dzn_q[0], dzn0[:, :TWO], E5M2, slice(0, HALF_N))
         quantize_wm("wm_q00", wm_words0, [(0, 0)])
@@ -325,7 +324,7 @@ def tile_attend_gex_wx_kernel(tc, xT, dyT, ts, wm, offs, out_0, out_1):
         copy_out_share(0, 0)
         copy_out_share(0, 1)
         gather_x(0, 1, vector_move, over="wm_words1")
-        copy_out_words(dzt1[:, TWO:], words23)
+        copy_out_words(dzt1[:, TWO : 2 * TWO], words23)
 
         dzn1 = held("dzn1", [P, PACK * N], BF16, over="plain3", skip=-3 * KIB)[:]
         gpsimd_interleave(dzn1, dz1[:])
@@ -337,6 +336,8 @@ def tile_attend_gex_wx_kernel(tc, xT, dyT, ts, wm, offs, out_0, out_1):
         copy_out_x(0, over="xt0", skip=KIB)
         scalar_scatter(0, 1)
 
+        picked[1, 1] = dzt1[:, 2 * TWO - HALF_N :]
+        vector_move(picked[1, 1][:, HALF_N:], x_sb[1][:].indirect(entries(N + HALF_N, HALF_N)))
         quantize_dzn(1, dzn1, over="wm10")
         quantize_wm("wm_q10", wm_words2, [(1, 0), (1, 1)])
         dzt_q[0] = quantised("dzt_q0", DV, over="dzn1")
@@ -344,26 +345,26 @@ def tile_attend_gex_wx_kernel(tc, xT, dyT, ts, wm, offs, out_0, out_1):
         quantize_turned(dzt01[:].rearrange("s p r -> s (p r)"), 1)
         quantize_turned(dzt02[:].rearrange("s t p r -> s (t p r)"), 2, 2)
         dzt_q[1] = quantised("dzt_q1", DV, over="dzn1", skip=2 * KIB)
-        quantize(dzt_q[1], dzt1[:], E5M2)
+        quantize(dzt_q[1], dzt1[:, : 2 * TWO], E5M2)
         quantize_x(0, over="dzt02")
         multiply_dx(1, 0, 2)
         multiply_dx(1, 1, 3)
-        wm_words3 = held("wm_words3", [P, 2 * TWO], BF16, over="xt0")[:]
+        wm_words3 = held("wm_words3", [P, 2 * TWO], BF16, over="xt0", skip=KIB // 2)[:]
         gpsimd_words(wm_words3[:, :TWO], wm_sb[0, 2][:])
         gpsimd_words(wm_words3[:, TWO:], wm_sb[1, 2][:])
         gather_x(1, 0, scalar_move, over="x_g00")
-        gather_x(1, 1, vector_move, over="dzt1", skip=3 * KIB)
+        vector_move(picked[1, 1][:, :HALF_N], x_sb[1][:].indirect(entries(N, HALF_N)))
         copy_out_share(1, 0)
-        gather_x(2, 0, scalar_move, over="dzt1")
+        gather_x(2, 0, scalar_move, over="xt0", skip=-KIB // 2)
         multiply_gw(0, 0, 4)
         multiply_gw(0, 1, 5)
         turn_x(1, 2)
         copy_out_gw(0, 0)
         store_gw(0, 0)
-        copy_out_x(1)
-        copy_out_share(1, 1, over="x_g11", skip=-3 * KIB // 2)
-        copy_out_gw(0, 1, over="x_g11", skip=KIB // 2)
+        copy_out_gw(0, 1)
         store_gw(0, 1)
+        copy_out_share(1, 1, over="dzt1")
+        copy_out_x(1)
         scatter(1, 0)
         store_window(0)
         scalar_scatter(1, 1)
@@ -375,24 +376,24 @@ def tile_attend_gex_wx_kernel(tc, xT, dyT, ts, wm, offs, out_0, out_1):
         gather_x(2, 1, vector_move, over="wm12", skip=KIB)
         copy_out_share(0, 2, vector_move)
         quantize_x(1, over="dzn_q0")
-        turn_x(2, 7)
+        turn_x(2, 4)
         multiply_gw(1, 0, 0)
-        multiply_gw(1, 1, 4)
+        multiply_gw(1, 1, 6)
+        multiply_dx(1, 3, 2)
         scatter(0, 2)
         copy_out_x(2)
-        multiply_dx(1, 2, 7)
+        multiply_dx(1, 2, 4)
         gather_x(3, 0, scalar_move, over="x_g21", skip=-KIB // 2)
         gather_x(3, 1, scalar_move, over="x_g21", skip=KIB // 2)
-        quantize_x(2)
         copy_out_share(1, 2, vector_move)
-        turn_x(3, 7)
+        quantize_x(2, over="dzn_q1")
+        turn_x(3, 4)
         copy_out_gw(1, 0)
-        multiply_dx(1, 3, 0)
         copy_out_share(0, 3, over="x3", skip=KIB)
         store_gw(1, 0, nc.scalar)
         copy_out_gw(1, 1, over="x3", skip=5 * KIB)
         multiply_gw(2, 0, 1)
-        multiply_gw(2, 1, 6)
+        multiply_gw(2, 1, 7)
         scatter(1, 2)
         store_window(2)
         scalar_scatter(0, 3)

@@ -30,6 +30,7 @@ ONE = P * PACK
 TWO = 2 * ONE
 KIB = 1024
 ALIGN = 64
+ROW_ALIGN = 256
 
 
 def tile_attend_gex_wx_kernel(tc, xT, dyT, ts, wm, offs, out_0, out_1):
@@ -52,7 +53,8 @@ def tile_attend_gex_wx_kernel(tc, xT, dyT, ts, wm, offs, out_0, out_1):
             else:
                 size = size_of[dtype] * math.prod(shape[1:])
                 room(name, -(-size // ALIGN) * ALIGN)
-            return shared.tile(shape, dtype, name=name, offset=start_of[name], align_bytes=ALIGN)
+            align = ROW_ALIGN if start_of[name] % ROW_ALIGN == 0 else ALIGN
+            return shared.tile(shape, dtype, name=name, offset=start_of[name], align_bytes=align)
 
         def bank(name, shape, number):
             return psum.tile(shape, F32, name=name, tag=f"bank{number}")
@@ -244,7 +246,7 @@ def tile_attend_gex_wx_kernel(tc, xT, dyT, ts, wm, offs, out_0, out_1):
         nc.sync.dma_start(offsets[:], offs)
 
         for j in range(BLOCKS):
-            windows[j] = keep.tile([P, T], F32, name=f"window{j}")
+            windows[j] = keep.tile([P, T], F32, name=f"window{j}", align_bytes=ROW_ALIGN)
             nc.gpsimd.memset(windows[j][:].bitcast(I32), 0)
 
         for t in range(PACK):

import math
from contextlib import ExitStack

import concourse.mybir as mybir
from concourse.masks import make_identity

B, N, T, D, DV = 2, 512, 2048, 512, 512
FLOPS = 2 * 2 * B * N * D * DV

F32 = mybir.dt.float32
BF16 = mybir.dt.bfloat16
U32 = mybir.dt.uint32
I32 = mybir.dt.int32
U16 = mybir.dt.uint16
U8 = mybir.dt.uint8
E4M3 = mybir.dt.float8_e4m3fn_x4
E5M2 = mybir.dt.float8_e5m2_x4
COPY = mybir.ActivationFunctionType.Copy
MULT = mybir.AluOpType.mult
ADD = mybir.AluOpType.add

P = 128
PACK = 4
BLOCKS = D // P
HALF_N = N // 2
ROWS_OF_LIST = 16
LINE = 4
LAST = P - 1
ONE = P * PACK
TWO = 2 * ONE
KIB = 1024
ALIGN = 64
ROW_ALIGN = 256


def tile_attend_gex_wx_kernel(tc, xT, dyT, ts, wm, offs, out_0, out_1):
    nc = tc.nc

    with ExitStack() as ctx:
        keep = ctx.enter_context(tc.tile_pool(name="keep", bufs=1))
        psum = ctx.enter_context(tc.psum_pool(name="psum", bufs=1))
        shared = ctx.enter_context(tc.tile_pool(name="shared", bufs=1))
        start_of = {"end": 0}
        size_of = {F32: 4, U32: 4, BF16: 2}

        def room(name, size):
            start_of[name] = start_of["end"]
            start_of["end"] = start_of["end"] + size

        def held(name, shape, dtype, over=None, skip=0):
            if over:
                start_of[name] = start_of[over] + skip
            else:
                size = size_of[dtype] * math.prod(shape[1:])
                room(name, -(-size // ALIGN) * ALIGN)
            align = ROW_ALIGN if start_of[name] % ROW_ALIGN == 0 else ALIGN
            return shared.tile(shape, dtype, name=name, offset=start_of[name], align_bytes=align)

        def bank(name, shape, number):
            return psum.tile(shape, F32, name=name, tag=f"bank{number}")

        offsets = keep.tile([P, B * N // ROWS_OF_LIST], U16, name="offsets")
        ts_sb = held("ts_sb", [P, T], F32)
        dy_sb, wm_sb, x_sb, windows = {}, {}, {}, {}
        xt, turned, picked, x_bank, product, gw, shares = {}, {}, {}, {}, {}, {}, {}
        dzt_q, dzn_q, wm_q, x_q, ts_rows, gw_sb = {}, {}, {}, {}, {}, {}

        def entries(first, count):
            return offsets[:, first // ROWS_OF_LIST : (first + count) // ROWS_OF_LIST]

        def scalar_move(out, in_):
            nc.scalar.activation(out, in_, COPY)

        def load_dy(t):
            dy_sb[t] = held(f"dy{t}", [P, T], F32)
            nc.sync.dma_start(out=dy_sb[t][:], in_=dyT.rearrange("(p t) c -> t p c", t=PACK)[t])

        def load_wm(b, first, count, **place):
            wm_sb[b, first] = held(f"wm{b}{first}", [P, PACK, count * P], F32, **place)
            rows = wm[b].rearrange("(p t) d -> p t d", t=PACK)
            nc.sync.dma_start(out=wm_sb[b, first][:], in_=rows[:, :, first * P : (first + count) * P])

        def load_x(j):
            x_sb[j] = held(f"x{j}", [P, T], F32)
            nc.sync.dma_start(out=x_sb[j][:], in_=xT[j * P : (j + 1) * P, :])

        def quantised(name, width, **place):
            codes = held(name, [P, width], U32, **place)
            scales = keep.tile([P, width], U8, name=name + "_scales", align_bytes=ALIGN)
            return codes, scales

        def quantize(dst, src, fmt, cols=slice(None)):
            nc.vector.quantize_mx(out=dst[0][:, cols].bitcast(fmt), scales=dst[1][:, cols], in_=src)

        def quantize_wm(name, src, blocks, **place):
            dst = quantised(name, len(blocks) * P, **place)
            quantize(dst, src, E4M3)
            for k, block in enumerate(blocks):
                wm_q[block] = dst, slice(k * P, (k + 1) * P)

        def quantize_x(j, **place):
            x_q[j] = quantised(f"x_q{j}", B * P, **place)
            quantize(x_q[j], xt[j], E4M3)

        def quantize_dzn(b, src, **place):
            dzn_q[b] = quantised(f"dzn_q{b}", N, **place)
            quantize(dzn_q[b], src, E5M2)

        def quantize_turned(src, first, count=1):
            quantize(dzt_q[0], src, E5M2, slice(first * P, (first + count) * P))

        def interleave(copy, dst, src):
            words = dst.rearrange("p (c t) -> p c t", t=PACK)
            copy(
                out=words.rearrange("p (c i) t -> p c t i", i=LINE),
                in_=src.rearrange("p t (c i) -> p c t i", i=LINE),
            )

        def gpsimd_interleave(dst, src):
            nc.gpsimd.tensor_scalar(
                out=dst.rearrange("p (c t) -> p c t", t=PACK),
                in0=src.rearrange("p t c -> p c t"),
                scalar1=1.0,
                scalar2=0.0,
                op0=MULT,
                op1=ADD,
            )

        def gpsimd_words(dst, src):
            nc.gpsimd.tensor_copy(dst.rearrange("p (c t) -> p c t", t=PACK), src.rearrange("p t c -> p c t"))

        def ts_gather(k, move):
            ts_rows[k] = held(f"ts_row{k}", [P, HALF_N], F32)
            move(ts_rows[k][:], ts_sb[:].indirect(entries(k * HALF_N, HALF_N)))

        def ts_down(k, number, copy):
            down = bank(f"down{k}", [P, 2, P], number)
            for q in range(2):
                nc.tensor.transpose(down[:, q, :], ts_rows[k][:, q * P : (q + 1) * P], ident[:])
            copy(ts_cols[k][:], down[:, :, LAST])

        def ts_across(k, number, copy):
            b, half = divmod(k, 2)
            across = bank(f"across{k}", [P, 2, P], number)
            for q in range(2):
                nc.tensor.transpose(across[:, q, :], ts_cols[k][:, q : q + 1].to_broadcast([P, P]), ident[:])
            copy(ts_g[b][:, half * HALF_N : (half + 1) * HALF_N], across[:].rearrange("p q s -> p (q s)"))

        def gather_dz0(t, first=0, count=N):
            slots = slice(first, first + count)
            window = dy_sb[t][:].indirect(entries(first, count))
            nc.vector.tensor_tensor(dz0[:, t, slots], window, ts_g[0][:, slots], MULT)

        def gather_dy1(t, dst):
            scalar_move(dst, dy_sb[t][:].indirect(entries(N, N)))

        def multiply_dz1(t, src):
            nc.vector.tensor_tensor(dz1[:, t, :], src, ts_g[1][:], MULT)

        def turn_dz0(t, number):
            turned[t] = bank(f"turned{t}", [P, PACK, P], number)
            for r in range(PACK):
                nc.tensor.transpose(turned[t][:, r, :], dz0[:, t, r:N:PACK], ident[:])

        def copy_out_dz0(t, dst):
            scalar_move(dst, turned[t][:].rearrange("s r p -> s p r"))

        def turn_words(name, pair, number):
            dst = bank(name, [P, 2, 2, P], number)
            for e, values in enumerate(pair):
                words = values.bitcast(F32)
                for u in range(2):
                    nc.tensor.transpose(dst[:, e, u, :], words[:, u:HALF_N:2], ident[:])
            return dst

        def copy_out_words(dst, src, copy=nc.scalar.copy):
            copy(
                out=dst.bitcast(F32).rearrange("s (e p u) -> s e p u", e=2, u=2),
                in_=src[:].rearrange("s e u p -> s e p u"),
            )

        def gather_x(j, b, move, **place):
            picked[j, b] = held(f"x_g{j}{b}", [P, N], BF16, **place)[:]
            move(picked[j, b], x_sb[j][:].indirect(entries(b * N, N)))

        def turn_x(j, number):
            x_bank[j] = turn_words(f"x_bank{j}", [picked[j, b] for b in range(B)], number)

        def copy_out_x(j, copy=nc.scalar.copy, **place):
            xt[j] = held(f"xt{j}", [P, TWO], BF16, **place)[:]
            copy_out_words(xt[j], x_bank[j], copy)

        def multiply(out, stationary, cols, moving, slots=slice(None)):
            nc.tensor.matmul_mx(
                out=out[:],
                lhsT=stationary[0][:, cols].bitcast(E4M3),
                lhsT_scale=stationary[1][:, cols],
                rhs=moving[0][:, slots].bitcast(E5M2),
                rhs_scale=moving[1][:, slots],
                start=True,
                stop=True,
            )

        def multiply_dx(b, j, number):
            product[b, j] = bank(f"dx{b}{j}", [P, N], number)
            multiply(product[b, j], *wm_q[b, j], dzn_q[b])

        def copy_out_share(b, j, copy=nc.scalar.copy, **place):
            shares[b, j] = held(f"share{b}{j}", [P, N], F32, **place)
            copy(out=shares[b, j][:], in_=product[b, j][:])

        def scatter(b, j):
            nc.vector.tensor_copy(windows[j][:].indirect(entries(b * N, N)), shares[b, j][:])

        def scalar_scatter(b, j):
            window = windows[j][:].indirect(entries(b * N, N))
            nc.scalar.activation(window, shares[b, j][:], COPY, scale=ones[:])

        def store_window(j, queue=nc.sync):
            queue.dma_start(out=out_1[j * P : (j + 1) * P, :], in_=windows[j][:])

        def multiply_gw(j, b, number):
            gw[j, b] = bank(f"gw{j}{b}", [P, DV], number)
            multiply(gw[j, b], x_q[j], slice(b * P, (b + 1) * P), dzt_q[b])

        def copy_out_gw(j, b, copy=nc.scalar.copy, **place):
            place = place or {"over": f"dy{j // 2 * 2}", "skip": (j % 2 * B + b) * 2 * KIB}
            gw_sb[j, b] = held(f"gw_sb{j}{b}", [P, P, PACK], F32, **place)
            copy(out=gw_sb[j, b][:], in_=gw[j, b][:].rearrange("d (t p) -> d p t", t=PACK))

        def store_gw(j, b, queue=nc.sync):
            rows = out_0[b, j * P : (j + 1) * P, :]
            queue.dma_start(out=rows, in_=gw_sb[j, b][:].rearrange("d p t -> d (p t)"))

        vector_move = nc.vector.tensor_copy
        ident = keep.tile([P, P], F32, name="ident")
        make_identity(nc, ident[:])
        one = keep.tile([P, 1], F32, name="one")
        ones = keep.tile([P, 1], F32, name="ones")
        nc.vector.memset(one[:], 1.0)
        nc.scalar.copy(ones[:], one[:])

        nc.sync.dma_start(out=ts_sb[LAST:, :], in_=ts[LAST:, :])
        nc.gpsimd.memset(ts_sb[:LAST, : T // 4], 0.0)
        nc.vector.memset(ts_sb[:LAST, T // 4 :], 0.0)
        nc.sync.dma_start(offsets[:], offs)

        for j in range(BLOCKS):
            windows[j] = keep.tile([P, T], F32, name=f"window{j}", align_bytes=ROW_ALIGN)
            nc.gpsimd.memset(windows[j][:].bitcast(I32), 0)

        for t in range(PACK):
            load_dy(t)
        load_wm(0, 0, 2)
        load_x(0)
        load_x(1)
        load_wm(1, 0, 2)
        load_x(2)
        load_wm(0, 2, 2)
        load_wm(1, 2, 2)
        load_x(3)

        ts_g = [held(f"ts_g{b}", [P, N], F32) for b in range(B)]
        dz0 = held("dz0", [P, PACK, N], F32)
        ts_cols = [held("ts_cols0", [P, 2], F32), dz0[:, 2, :2], dz0[:, 3, :2], dz0[:, 3, 8:10]]
        ts_gather(0, vector_move)
        ts_gather(1, scalar_move)
        ts_gather(2, vector_move)
        ts_gather(3, scalar_move)
        ts_down(0, 0, vector_move)
        ts_down(1, 1, nc.scalar.copy)
        ts_down(2, 4, vector_move)
        ts_across(0, 2, vector_move)
        ts_across(1, 3, vector_move)
        ts_down(3, 5, vector_move)
        plain = [dz0[:, 2, :], dz0[:, 3, :]] + [held(f"plain{t}", [P, N], F32, over="dy1", skip=5 * KIB)[:] for t in (2, 3)]
        dz1 = held("dz1", [P, PACK, N], BF16)

        gather_dy1(0, plain[0])
        for first in (0, HALF_N):
            gather_dz0(0, first, HALF_N)
        ts_across(2, 6, nc.scalar.copy)
        ts_across(3, 7, nc.scalar.copy)
        turn_dz0(0, 0)
        gather_dy1(1, plain[1])
        gather_dz0(1)
        turn_dz0(1, 1)
        dzt00 = held("dzt00", [P, P, PACK], BF16, over="dy1")
        copy_out_dz0(0, dzt00[:])
        multiply_dz1(0, plain[0])
        multiply_dz1(1, plain[1])
        words01 = turn_words("dz1_bank0", [dz1[:, 0, :], dz1[:, 1, :]], 2)
        gather_dz0(2)
        gather_dy1(2, plain[2])
        turn_dz0(2, 3)
        dzt1 = held("dzt1", [P, 2 * TWO + HALF_N], BF16, over="dy2")
        dzt01 = held("dzt01", [P, P, PACK], BF16, over="dy2", skip=5 * KIB)
        copy_out_dz0(1, dzt01[:])
        multiply_dz1(2, plain[2])
        for first in (0, HALF_N):
            gather_dz0(3, first, HALF_N)
        gather_dy1(3, plain[3])
        copy_out_words(dzt1[:, :TWO], words01)
        turn_dz0(3, 4)

        wm_words0 = held("wm_words0", [P, ONE], BF16, over="ts_g0")[:]
        wm_words1 = held("wm_words1", [P, ONE], BF16, over="dy3", skip=7 * KIB)[:]
        dzn0 = held("dzn0", [P, PACK * N], BF16)
        dzt02 = held("dzt02", [P, 2, P, PACK], BF16, over="dy3", skip=3 * KIB)
        interleave(vector_move, dzn0[:, :TWO], dz0[:, :, :HALF_N])
        interleave(vector_move, wm_words0, wm_sb[0, 0][:, :, :P])
        interleave(vector_move, dzn0[:, TWO:], dz0[:, :, HALF_N:])
        copy_out_dz0(2, dzt02[:, 0])
        interleave(nc.scalar.copy, wm_words1, wm_sb[0, 0][:, :, P:])
        dzn_q[0] = quantised("dzn_q0", N)
        quantize(dzn_q[0], dzn0[:, :TWO], E5M2, slice(0, HALF_N))
        quantize_wm("wm_q00", wm_words0, [(0, 0)])
        quantize(dzn_q[0], dzn0[:, TWO:], E5M2, slice(HALF_N, N))
        quantize_wm("wm_q01", wm_words1, [(0, 1)])
        copy_out_dz0(3, dzt02[:, 1])
        multiply_dx(0, 0, 5)
        multiply_dx(0, 1, 6)
        multiply_dz1(3, plain[3])
        words23 = turn_words("dz1_bank1", [dz1[:, 2, :], dz1[:, 3, :]], 7)
        gather_x(0, 0, scalar_move, over="dz0")
        copy_out_share(0, 0)
        copy_out_share(0, 1)
        gather_x(0, 1, vector_move, over="wm_words1")
        copy_out_words(dzt1[:, TWO : 2 * TWO], words23)

        dzn1 = held("dzn1", [P, PACK * N], BF16, over="plain3", skip=-3 * KIB)[:]
        gpsimd_interleave(dzn1, dz1[:])
        wm_words2 = held("wm_words2", [P, TWO], BF16, over="plain3", skip=KIB)[:]
        gpsimd_words(wm_words2, wm_sb[1, 0][:])
        scatter(0, 0)
        turn_x(0, 5)
        room("xt0", 6 * KIB)
        copy_out_x(0, over="xt0", skip=KIB)
        scalar_scatter(0, 1)

        picked[1, 1] = dzt1[:, 2 * TWO - HALF_N :]
        vector_move(picked[1, 1][:, HALF_N:], x_sb[1][:].indirect(entries(N + HALF_N, HALF_N)))
        quantize_dzn(1, dzn1, over="wm10")
        quantize_wm("wm_q10", wm_words2, [(1, 0), (1, 1)])
        dzt_q[0] = quantised("dzt_q0", DV, over="dzn1")
        quantize_turned(dzt00[:].rearrange("s p r -> s (p r)"), 0)
        quantize_turned(dzt01[:].rearrange("s p r -> s (p r)"), 1)
        quantize_turned(dzt02[:].rearrange("s t p r -> s (t p r)"), 2, 2)
        dzt_q[1] = quantised("dzt_q1", DV, over="dzn1", skip=2 * KIB)
        quantize(dzt_q[1], dzt1[:, : 2 * TWO], E5M2)
        quantize_x(0, over="dzt02")
        multiply_dx(1, 0, 2)
        multiply_dx(1, 1, 3)
        wm_words3 = held("wm_words3", [P, 2 * TWO], BF16, over="xt0", skip=KIB // 2)[:]
        gpsimd_words(wm_words3[:, :TWO], wm_sb[0, 2][:])
        gpsimd_words(wm_words3[:, TWO:], wm_sb[1, 2][:])
        gather_x(1, 0, scalar_move, over="x_g00")
        vector_move(picked[1, 1][:, :HALF_N], x_sb[1][:].indirect(entries(N, HALF_N)))
        copy_out_share(1, 0)
        gather_x(2, 0, scalar_move, over="xt0", skip=-KIB // 2)
        multiply_gw(0, 0, 4)
        multiply_gw(0, 1, 5)
        turn_x(1, 2)
        copy_out_gw(0, 0)
        store_gw(0, 0)
        copy_out_gw(0, 1)
        store_gw(0, 1)
        copy_out_share(1, 1, over="dzt1")
        copy_out_x(1)
        scatter(1, 0)
        store_window(0)
        scalar_scatter(1, 1)
        store_window(1)

        quantize_wm("wm_q2", wm_words3, [(0, 2), (0, 3), (1, 2), (1, 3)], over="wm02")
        multiply_dx(0, 2, 7)
        multiply_dx(0, 3, 1)
        gather_x(2, 1, vector_move, over="wm12", skip=KIB)
        copy_out_share(0, 2, vector_move)
        quantize_x(1, over="dzn_q0")
        turn_x(2, 4)
        multiply_gw(1, 0, 0)
        multiply_gw(1, 1, 6)
        multiply_dx(1, 3, 2)
        scatter(0, 2)
        copy_out_x(2)
        multiply_dx(1, 2, 4)
        gather_x(3, 0, scalar_move, over="x_g21", skip=-KIB // 2)
        gather_x(3, 1, scalar_move, over="x_g21", skip=KIB // 2)
        copy_out_share(1, 2, vector_move)
        quantize_x(2, over="dzn_q1")
        turn_x(3, 4)
        copy_out_gw(1, 0)
        copy_out_share(0, 3, over="x3", skip=KIB)
        store_gw(1, 0, nc.scalar)
        copy_out_gw(1, 1, over="x3", skip=5 * KIB)
        multiply_gw(2, 0, 1)
        multiply_gw(2, 1, 7)
        scatter(1, 2)
        store_window(2)
        scalar_scatter(0, 3)
        store_gw(1, 1, nc.scalar)
        copy_out_x(3, vector_move)
        copy_out_share(1, 3, vector_move, over="x_g31")
        quantize_x(3)
        multiply_gw(3, 0, 3)
        multiply_gw(3, 1, 5)
        scatter(1, 3)
        copy_out_gw(2, 0, over="share03", skip=-KIB)
        copy_out_gw(2, 1, over="share03", skip=KIB)
        store_gw(2, 0, nc.scalar)
        copy_out_gw(3, 0)
        store_gw(2, 1, nc.scalar)
        copy_out_gw(3, 1)
        store_gw(3, 0, nc.scalar)
        store_gw(3, 1, nc.scalar)
        store_window(3)
